import numpy as np
import ml_dtypes


def mxq(x, axis, fmt="e4m3"):
    dtype, down = {"e4m3": (ml_dtypes.float8_e4m3fn, 7), "e5m2": (ml_dtypes.float8_e5m2, 14)}[fmt]
    v = np.moveaxis(np.asarray(x, np.float32).astype(ml_dtypes.bfloat16).astype(np.float64), axis, -1)
    blocks = v.reshape(v.shape[:-1] + (-1, 32))
    amax = np.abs(blocks).max(-1, keepdims=True)
    byte = np.maximum(np.where(amax > 0, np.frexp(amax)[1] - 1 + 127, 0) - down, 1)
    scale = np.exp2(byte - 127.0)
    codes = (blocks / scale).astype(np.float32).astype(dtype).astype(np.float64)
    return np.moveaxis((codes * scale).reshape(v.shape), -1, axis)


WIDE = False


def mx_kscale(k):
    if not WIDE:
        return np.ones(k)
    levels = np.array([10, -10, 5, -5, 0])
    if k % 512:
        return np.exp2(np.random.permutation(np.resize(levels, k // 32))).repeat(32)
    a = np.empty((k // 512, 16))
    for p in range(k // 512):
        a[p, :8] = np.random.permutation(np.resize(levels, 8))
        for g in range(8):
            far = levels[np.abs(levels - a[p, g]) >= 10]
            a[p, g + 8] = far[np.random.randint(len(far))]
    return np.exp2(a.ravel()).repeat(32)


def f64(x):
    return np.asarray(x).astype(np.float64)


def striped(idx):
    return np.tile(idx.reshape(-1, 16).T, (8, 1)).astype(np.uint16)


def unstriped(offs):
    return offs[:16].T.reshape(-1).astype(np.int64)


E2M1 = np.array([0.0, 0.5, 1.0, 1.5, 2.0, 3.0, 4.0, 6.0, -0.0, -0.5, -1.0, -1.5, -2.0, -3.0, -4.0, -6.0])


def pack_weight(w, fmt):
    k, n = w.shape
    w = f64(np.asarray(w, np.float32).astype(ml_dtypes.bfloat16)).reshape(k // 32, 32, n)
    amax = np.abs(w).max(1)
    if fmt == "e4m3":
        byte = np.frexp(amax)[1] - 1 + 127 - 7
    else:
        mant, ex = np.frexp(amax / 6.0)
        byte = np.where(mant > 0.5, ex, ex - 1) + 127
    byte = np.clip(np.where(amax > 0, byte, 1), 1, 254)
    scaled = (w * np.exp2(127.0 - byte)[:, None, :]).reshape(k, n).astype(np.float32)
    by_word = np.ascontiguousarray(scaled.reshape(k // 512, 128, 4, n).transpose(0, 1, 3, 2))
    if fmt == "e4m3":
        words = by_word.astype(ml_dtypes.float8_e4m3fn).view(np.uint8)
    else:
        c = by_word.astype(ml_dtypes.float4_e2m1fn).view(np.uint8) & 0xF
        words = (c[..., 0::2] | (c[..., 1::2] << 4)).reshape(k // 512, 128, 2 * n)
    return np.ascontiguousarray(words), np.ascontiguousarray(byte.astype(np.uint8).reshape(k // 512, 16, n))


def unpack_weight(words, scales, fmt):
    g, _, n = scales.shape
    words = np.ascontiguousarray(words).reshape(g, 128, n, -1)
    if fmt == "e4m3":
        vals = words.view(ml_dtypes.float8_e4m3fn).astype(np.float64)
    else:
        nib = np.empty((g, 128, n, 4), np.uint8)
        nib[..., 0::2] = words & 0xF
        nib[..., 1::2] = words >> 4
        vals = E2M1[nib]
    vals = vals * np.repeat(np.exp2(scales.astype(np.float64) - 127.0), 8, axis=1)[..., None]
    return vals.transpose(0, 1, 3, 2).reshape(g * 512, n)


def gelu(v):
    return 0.5 * v * (1.0 + np.tanh(np.sqrt(2.0 / np.pi) * (v + 0.044715 * v**3)))


K, H, N, T, S, T2 = 1024, 1024, 512, 2048, 1024, 2048

def setup_inputs():
    n = np.random.standard_normal
    s = mx_kscale(K)[:, None]
    u = mx_kscale(H)[:, None]
    tab_words, tab_scales = pack_weight(n((K, T)) * s, "e4m3")
    wr = n((K, H)) / np.sqrt(K) / s
    rate = np.exp(0.3 * n(H)) * u[:, 0]
    wt4_words, wt4_scales = pack_weight(1.5 * n((H, N)) / np.sqrt(H) / u, "e2m1")
    wd = -np.exp(0.2 * n((K, 1))) * n((K, N)) / np.sqrt(K) / s
    return {
        "tab_words": tab_words, "tab_scales": tab_scales,
        "offs": striped(np.random.permutation(T)[:S]),
        "wr": wr.astype(np.float32), "rate": rate.astype(np.float32),
        "wt4_words": wt4_words, "wt4_scales": wt4_scales,
        "wd": wd.astype(np.float32),
        "wgo": np.exp(0.3 * n((128, S))).astype(np.float32),
        "offs2": striped(np.random.permutation(T2)[:S]),
    }

def reference(tab_words, tab_scales, offs, wr, rate, wt4_words, wt4_scales, wd, wgo, offs2):
    v = unpack_weight(tab_words, tab_scales, "e4m3")[:, unstriped(offs)]
    wt = unpack_weight(wt4_words, wt4_scales, "e2m1")
    a = mxq(f64(wr), 0, "e4m3").T @ v
    sq = a * a
    h = f64(rate)[:, None] * (sq / (1.0 + sq))
    hq = mxq(h, 0, "e4m3")
    y = wt.T @ hq + mxq(f64(wd), 0, "e4m3").T @ v
    out = np.zeros((N, T2))
    out[:, unstriped(offs2)] = np.tile(f64(wgo), (N // 128, 1)) * y
    return out

@@ -1,0 +1,262 @@
+from contextlib import ExitStack
+
+import concourse.mybir as mybir
+
+F32 = mybir.dt.float32
+BF16 = mybir.dt.bfloat16
+I32 = mybir.dt.int32
+U32 = mybir.dt.uint32
+U16 = mybir.dt.uint16
+U8 = mybir.dt.uint8
+FP8X4 = mybir.dt.float8_e4m3fn_x4
+FP4X4 = mybir.dt.float4_e2m1fn_x4
+MULT = mybir.AluOpType.mult
+ADD = mybir.AluOpType.add
+ACT = mybir.ActivationFunctionType
+
+K, H, N, T, S, T2 = 1024, 1024, 512, 2048, 1024, 2048
+FLOPS = 2 * K * H * S + 2 * H * N * S + 2 * K * N * S
+P = 128
+BANK = 512
+CHUNKS = [256,256,256,256]
+RATE_ON = [["B","S","S","S"],["S","B","S","S"]]
+WR_CAST = [["VV","GS"],["VG","V"]]
+WD_CAST = ["VV","VV"]
+ORDER = [("cr", 0, 0,), ("cr", 0, 1,), ("gw", 3, 0,), ("gw", 0, 0,), ("qr", 0, 1,), ("gw", 2, 0,), ("gs", 0,), ("qr", 0, 0,), ("gw", 0, 1,), ("gs", 1,), ("gw", 1, 1,), ("gw", 3, 1,), ("gw", 1, 0,), ("gw", 2, 1,), ("cr", 1, 0,), ("cr", 1, 1,), ("qr", 1, 0,), ("u", 0, 0,), ("u", 0, 1,), ("qr", 1, 1,), ("gs", 2,), ("cd", 1,), ("u", 1, 0,), ("cd", 0,), ("u", 1, 1,), ("qd", 0,), ("y", 1, 1,), ("y", 1, 0,), ("u", 1, 2,), ("y", 0, 0,), ("gs", 3,), ("s", 1, 0,), ("qd", 1,), ("s", 1, 1,), ("u", 0, 2,), ("y", 3, 2,), ("y", 2, 1,), ("u", 0, 3,), ("s", 0, 0,), ("y", 3, 0,), ("y", 3, 1,), ("y", 1, 2,), ("y", 0, 2,), ("y", 2, 0,), ("s", 1, 2,), ("s", 3, 1,), ("y", 2, 2,), ("y", 0, 1,), ("s", 0, 1,), ("s", 2, 1,), ("u", 1, 3,), ("s", 2, 0,), ("s", 0, 2,), ("y", 1, 3,), ("s", 2, 2,), ("s", 1, 3,), ("y", 0, 3,), ("y", 2, 3,), ("s", 3, 0,), ("s", 0, 3,), ("y", 3, 3,), ("s", 2, 3,), ("s", 3, 2,), ("s", 3, 3,)]
+FIN = [["V","V","V","V"],["V","V","V","V"]]
+YMUL = ["V","V","V","V"]
+MEMSET = ["V","G","V","G"]
+LOADS = [["idx",1],["tsc",1],["wr00",1],["wr01",1],["wtsc",1],["tab0",1],["tab1",1],["wr10",1],["wr11b",1],["wr11a",2],["wgo3",1],["wt",1],["wd00",1],["wgo0",1],["wgo1",1],["wd10",2],["wd01",2],["wgo2",1],["idx2",1],["wd11",1]]
+
+
+def tile_list_gene_regulation_derivatives_kernel(
+    tc, tab_words, tab_scales, offs, wr, rate, wt4_words, wt4_scales, wd, wgo, offs2, out
+):
+    nc = tc.nc
+    starts = [sum(CHUNKS[:c]) for c in range(len(CHUNKS))]
+
+    with ExitStack() as ctx:
+        keep = ctx.enter_context(tc.tile_pool(name="keep", bufs=1))
+        hill = ctx.enter_context(tc.tile_pool(name="hill", bufs=4))
+        ypool = ctx.enter_context(tc.tile_pool(name="ypool", bufs=8))
+        apsum = ctx.enter_context(tc.psum_pool(name="apsum", bufs=4))
+        ypsum = ctx.enter_context(tc.psum_pool(name="ypsum", bufs=4))
+
+        idx = keep.tile([P, S // 16], U16, name="idx")
+        idx2 = keep.tile([P, S // 16], U16, name="idx2")
+        tab_w = [keep.tile([P, T], I32, name="tab_w%d" % a, align_bytes=64) for a in range(2)]
+        tab_s = keep.tile([P, T // 4], I32, name="tab_s", align_bytes=64)
+        wr_raw = [[keep.tile([P, 4, 512], F32, name="wr_raw%d%d" % (b, a), align_bytes=64) for a in range(2)] for b in range(2)]
+        wr_bf = [[keep.tile([P, 2048], BF16, name="wr_bf%d%d" % (b, a), align_bytes=64) for a in range(2)] for b in range(2)]
+        wr_q = [[keep.tile([P, 512], U32, name="wr_q%d%d" % (b, a), align_bytes=64) for a in range(2)] for b in range(2)]
+        wr_s = [[keep.tile([P, 512], U8, name="wr_s%d%d" % (b, a), align_bytes=64) for a in range(2)] for b in range(2)]
+        wd_raw = [[keep.tile([P, 4, 256], F32, name="wd_raw%d%d" % (g, a), align_bytes=64) for a in range(2)] for g in range(2)]
+        wd_bf = [keep.tile([P, 2, 1024], BF16, name="wd_bf%d" % g, align_bytes=64) for g in range(2)]
+        wd_q = [keep.tile([P, 2, 256], U32, name="wd_q%d" % g, align_bytes=64) for g in range(2)]
+        wd_s = [keep.tile([P, 2, 256], U8, name="wd_s%d" % g, align_bytes=64) for g in range(2)]
+        wt_w = keep.tile([P, 2, 1024], U8, name="wt_w", align_bytes=64)
+        wt_s = keep.tile([P, 2, 512], U8, name="wt_s", align_bytes=64)
+        rate_t = keep.tile([P, 2, 4], F32, name="rate_t")
+        wgo_t = [keep.tile([P, w], F32, name="wgo%d" % c, align_bytes=64) for c, w in enumerate(CHUNKS)]
+        cache = [keep.tile([P, T2], F32, name="cache%d" % n, align_bytes=64) for n in range(4)]
+        v_w = [[keep.tile([P, w], U32, name="v_w%d%d" % (c, a), align_bytes=64) for a in range(2)] for c, w in enumerate(CHUNKS)]
+        v_s = [keep.tile([P, w], U8, name="v_s%d" % c, align_bytes=64) for c, w in enumerate(CHUNKS)]
+        h_q = [[keep.tile([P, w], U32, name="h_q%d%d" % (c, b), align_bytes=64) for b in range(2)] for c, w in enumerate(CHUNKS)]
+        h_s = [[keep.tile([P, w], U8, name="h_s%d%d" % (c, b), align_bytes=64) for b in range(2)] for c, w in enumerate(CHUNKS)]
+
+        warm = keep.tile([P, 1], F32, name="warm")
+        nc.gpsimd.memset(warm[:], 1.0)
+        nc.scalar.activation(out=warm[:], in_=warm[:], func=ACT.Abs_reciprocal_sqrt)
+        nc.gpsimd.memset(tab_s[:], 0)
+        nc.gpsimd.memset(wt_s[:].rearrange("p a n -> p (a n)").bitcast(I32), 0)
+        for n in range(4):
+            (nc.vector if MEMSET[n] == "V" else nc.gpsimd).memset(cache[n][:], 0.0)
+
+        def load_wr(b, a, lo, hi, pieces):
+            src = wr[512 * a : 512 * (a + 1), 512 * b + lo : 512 * b + hi].rearrange("(p j) c -> p j c", j=4)
+            for j in range(0, 4, 4 // pieces):
+                nc.sync.dma_start(out=wr_raw[b][a][:, j : j + 4 // pieces, lo:hi], in_=src[:, j : j + 4 // pieces, :])
+
+        def load_wd(g, a, pieces):
+            src = wd[512 * a : 512 * (a + 1), 256 * g : 256 * (g + 1)].rearrange("(p j) c -> p j c", j=4)
+            for j in range(0, 4, 4 // pieces):
+                nc.sync.dma_start(out=wd_raw[g][a][:, j : j + 4 // pieces, :], in_=src[:, j : j + 4 // pieces, :])
+
+        def load_tab(a, pieces):
+            src = tab_words[a].rearrange("p t i -> p (t i)").bitcast(I32)
+            for t in range(0, T, T // pieces):
+                nc.sync.dma_start(out=tab_w[a][:, t : t + T // pieces], in_=src[:, t : t + T // pieces])
+
+        nc.scalar.dma_start(out=rate_t[:], in_=rate.rearrange("(b p t) -> p b t", b=2, t=4))
+        for name, pieces in LOADS:
+            if name == "idx":
+                nc.sync.dma_start(idx[:], offs)
+            elif name == "idx2":
+                nc.sync.dma_start(idx2[:], offs2)
+            elif name == "tsc":
+                for q in range(4):
+                    nc.sync.dma_start(out=tab_s[32 * q : 32 * q + 8, :], in_=tab_scales[:, 4 * q : 4 * q + 4, :].bitcast(I32))
+            elif name == "wtsc":
+                for q in range(4):
+                    nc.sync.dma_start(
+                        out=wt_s[32 * q : 32 * q + 4, :, :].bitcast(I32),
+                        in_=wt4_scales[:, 4 * q : 4 * q + 4, :].rearrange("a r n -> r a n").bitcast(I32),
+                    )
+            elif name == "wt":
+                nc.sync.dma_start(out=wt_w[:].bitcast(I32), in_=wt4_words.rearrange("a p c -> p a c").bitcast(I32))
+            elif name.startswith("tab"):
+                load_tab(int(name[3]), pieces)
+            elif name.startswith("wr"):
+                lo, hi = {"": (0, 512), "a": (0, 256), "b": (256, 512)}[name[4:]]
+                load_wr(int(name[2]), int(name[3]), lo, hi, pieces)
+            elif name.startswith("wd"):
+                load_wd(int(name[2]), int(name[3]), pieces)
+            else:
+                c = int(name[3])
+                nc.sync.dma_start(out=wgo_t[c][:], in_=wgo[:, starts[c] : starts[c] + CHUNKS[c]])
+
+        def cast(engine, dst, src):
+            if engine == "V":
+                nc.vector.tensor_copy(out=dst, in_=src)
+            elif engine == "S":
+                nc.scalar.activation(out=dst, in_=src, func=ACT.Copy)
+            else:
+                nc.gpsimd.tensor_scalar(dst, src, 1.0, 0.0, MULT, ADD)
+
+        def cast_wr(b, a):
+            engines = WR_CAST[b][a]
+            step = 128 // len(engines)
+            for i, engine in enumerate(engines):
+                walk = "p m t j" if engine == "G" else "p m j t"
+                dst = wr_bf[b][a][:].rearrange("p (t m j) -> " + walk, t=4, j=4)
+                src = wr_raw[b][a][:].rearrange("p j (m t) -> " + walk, t=4)
+                cast(engine, dst[:, i * step : (i + 1) * step], src[:, i * step : (i + 1) * step])
+
+        def quant_wr(b, a):
+            nc.vector.quantize_mx(out=wr_q[b][a][:].bitcast(FP8X4), scales=wr_s[b][a][:], in_=wr_bf[b][a][:])
+
+        def cast_wd(g):
+            for a in range(2):
+                walk = "p c i j" if WD_CAST[g][a] == "G" else "p c j i"
+                dst = wd_bf[g][:, a, :].rearrange("p (c i j) -> " + walk, i=4, j=4)
+                src = wd_raw[g][a][:].rearrange("p j (c i) -> " + walk, i=4)
+                cast(WD_CAST[g][a], dst, src)
+
+        def quant_wd(g):
+            nc.vector.quantize_mx(
+                out=wd_q[g][:].rearrange("p a n -> p (a n)").bitcast(FP8X4),
+                scales=wd_s[g][:].rearrange("p a n -> p (a n)"),
+                in_=wd_bf[g][:].rearrange("p a n -> p (a n)"),
+            )
+
+        def entries(tile, c):
+            return tile[:, starts[c] // 16 : (starts[c] + CHUNKS[c]) // 16]
+
+        def gather_words(c, a):
+            nc.vector.tensor_copy(v_w[c][a][:], tab_w[a][:].bitcast(U32).indirect(entries(idx, c)))
+
+        def gather_scales(c):
+            nc.vector.tensor_copy(v_s[c][:], tab_s[:].bitcast(U8).indirect(entries(idx, c)))
+
+        def unit(b, c):
+            w = CHUNKS[c]
+            per_bank = BANK // w
+            sq = hill.tile([P, 4, w], F32, name="sq", align_bytes=64)
+            inv = hill.tile([P, 4, w], F32, name="inv", align_bytes=64)
+            h_bf = hill.tile([P, 4 * w], BF16, name="h_bf", align_bytes=64)
+            for t0 in range(0, 4, per_bank):
+                acc = apsum.tile([P, per_bank, w], F32, name="acc")
+                for t in range(t0, t0 + per_bank):
+                    for a in range(2):
+                        nc.tensor.matmul_mx(
+                            out=acc[:, t - t0, :],
+                            lhsT=wr_q[b][a][:, P * t : P * (t + 1)].bitcast(FP8X4),
+                            lhsT_scale=wr_s[b][a][:, P * t : P * (t + 1)],
+                            rhs=v_w[c][a][:].bitcast(FP8X4),
+                            rhs_scale=v_s[c][4 * a : P, :],
+                            start=(a == 0),
+                            stop=(a == 1),
+                        )
+                nc.scalar.activation(out=sq[:, t0 : t0 + per_bank, :], in_=acc[:], func=ACT.Square)
+            mode = RATE_ON[b][c]
+            sq_r = sq
+            halves = [(0, 2), (2, 4)] if mode == "B" else [(0, 4)]
+            for lo, hi in halves:
+                nc.scalar.activation(out=inv[:, lo:hi, :], in_=sq[:, lo:hi, :], func=ACT.Abs_reciprocal_sqrt, bias=1.0)
+            if mode != "B":
+                nc.scalar.activation(out=inv[:], in_=inv[:], func=ACT.Square)
+            for t in range(4):
+                r_col = rate_t[:, b, t : t + 1]
+                if mode == "B":
+                    nc.vector.scalar_tensor_tensor(inv[:, t, :], inv[:, t, :], r_col, inv[:, t, :], MULT, MULT)
+                elif mode == "S":
+                    nc.scalar.activation(out=inv[:, t, :], in_=inv[:, t, :], func=ACT.Copy, scale=r_col)
+                elif mode == "V":
+                    nc.vector.tensor_scalar(sq_r[:, t, :], sq[:, t, :], r_col, None, MULT)
+                else:
+                    nc.gpsimd.tensor_scalar(sq_r[:, t, :], sq[:, t, :], r_col, 0.0, MULT, ADD)
+            fin = nc.gpsimd if FIN[b][c] == "G" else nc.vector
+            walk = "p c i t" if FIN[b][c] == "G" else "p c t i"
+            fin.tensor_tensor(
+                h_bf[:].rearrange("p (c i t) -> " + walk, i=4, t=4),
+                sq_r[:].rearrange("p t (c i) -> " + walk, i=4),
+                inv[:].rearrange("p t (c i) -> " + walk, i=4),
+                MULT,
+            )
+            nc.vector.quantize_mx(out=h_q[c][b][:].bitcast(FP8X4), scales=h_s[c][b][:], in_=h_bf[:])
+
+        y_sb = {}
+        done = []
+
+        def product(n, c):
+            w = CHUNKS[c]
+            width = 512 if w == 512 else 128
+            g, n0 = n // 2, P * (n % 2)
+            acc = ypsum.tile([P, w], F32, name="yacc")
+            for j0 in range(0, w, width):
+                cols = slice(j0, j0 + width)
+                for b in range(2):
+                    nc.tensor.matmul_mx(
+                        out=acc[:, cols],
+                        lhsT=wt_w[:, b, 2 * P * n : 2 * P * (n + 1)].bitcast(FP4X4),
+                        lhsT_scale=wt_s[:, b, P * n : P * (n + 1)],
+                        rhs=h_q[c][b][:, cols].bitcast(FP8X4),
+                        rhs_scale=h_s[c][b][:, cols],
+                        start=(b == 0),
+                        stop=False,
+                    )
+                for a in range(2):
+                    nc.tensor.matmul_mx(
+                        out=acc[:, cols],
+                        lhsT=wd_q[g][:, a, n0 : n0 + P].bitcast(FP8X4),
+                        lhsT_scale=wd_s[g][:, a, n0 : n0 + P],
+                        rhs=v_w[c][a][:, cols].bitcast(FP8X4),
+                        rhs_scale=v_s[c][4 * a : P, cols],
+                        start=False,
+                        stop=(a == 1),
+                    )
+            y = ypool.tile([P, w], F32, name="y", align_bytes=64)
+            if YMUL[c] == "V":
+                nc.vector.tensor_tensor(y[:], acc[:], wgo_t[c][:], MULT)
+            else:
+                nc.scalar.activation(out=y[:], in_=acc[:], func=ACT.Copy)
+            if YMUL[c] == "G":
+                nc.gpsimd.tensor_tensor(y[:], y[:], wgo_t[c][:], MULT)
+            y_sb[(n, c)] = y
+
+        def scatter(n, c):
+            window = cache[n][:].indirect(entries(idx2, c))
+            if YMUL[c] == "F":
+                nc.vector.tensor_tensor(window, y_sb[(n, c)][:], wgo_t[c][:], MULT)
+            else:
+                nc.vector.tensor_copy(window, y_sb[(n, c)][:])
+            done.append(n)
+            if len([m for m in done if m == n]) == len(CHUNKS):
+                nc.sync.dma_start(out=out[P * n : P * (n + 1), :], in_=cache[n][:])
+
+        steps = {
+            "gw": gather_words, "gs": gather_scales, "cr": cast_wr, "qr": quant_wr, "cd": cast_wd, "qd": quant_wd,
+            "u": unit, "y": product, "s": scatter,
+        }
+        for step in ORDER:
+            steps[step[0]](*step[1:])

@@ -19,14 +19,16 @@ FLOPS = 2 * K * H * S + 2 * H * N * S + 2 * K * N * S
 P = 128
 BANK = 512
 CHUNKS = [256,256,256,256]
-RATE_ON = [["B","S","S","S"],["S","B","S","S"]]
-WR_CAST = [["VV","GS"],["VG","V"]]
-WD_CAST = ["VV","VV"]
-ORDER = [("cr", 0, 0,), ("cr", 0, 1,), ("gw", 3, 0,), ("gw", 0, 0,), ("qr", 0, 1,), ("gw", 2, 0,), ("gs", 0,), ("qr", 0, 0,), ("gw", 0, 1,), ("gs", 1,), ("gw", 1, 1,), ("gw", 3, 1,), ("gw", 1, 0,), ("gw", 2, 1,), ("cr", 1, 0,), ("cr", 1, 1,), ("qr", 1, 0,), ("u", 0, 0,), ("u", 0, 1,), ("qr", 1, 1,), ("gs", 2,), ("cd", 1,), ("u", 1, 0,), ("cd", 0,), ("u", 1, 1,), ("qd", 0,), ("y", 1, 1,), ("y", 1, 0,), ("u", 1, 2,), ("y", 0, 0,), ("gs", 3,), ("s", 1, 0,), ("qd", 1,), ("s", 1, 1,), ("u", 0, 2,), ("y", 3, 2,), ("y", 2, 1,), ("u", 0, 3,), ("s", 0, 0,), ("y", 3, 0,), ("y", 3, 1,), ("y", 1, 2,), ("y", 0, 2,), ("y", 2, 0,), ("s", 1, 2,), ("s", 3, 1,), ("y", 2, 2,), ("y", 0, 1,), ("s", 0, 1,), ("s", 2, 1,), ("u", 1, 3,), ("s", 2, 0,), ("s", 0, 2,), ("y", 1, 3,), ("s", 2, 2,), ("s", 1, 3,), ("y", 0, 3,), ("y", 2, 3,), ("s", 3, 0,), ("s", 0, 3,), ("y", 3, 3,), ("s", 2, 3,), ("s", 3, 2,), ("s", 3, 3,)]
+RATE_ON = [["V","B","S","S"],["B","B","S","S"]]
+WR_CAST = [["SV","VS"],["VS","VV"]]
+WD_CAST = ["VV","SV"]
+ORDER = [("cr", 1, 1,), ("cr", 0, 1,), ("ga", 1,), ("cr", 0, 0,), ("qr", 0, 1,), ("cr", 1, 0,), ("qr", 0, 0,), ("qr", 1, 0,), ("qr", 1, 1,), ("gb", 0,), ("cd", 0,), ("ga", 0,), ("u", 0, 1,), ("u", 0, 0,), ("u", 1, 1,), ("qd", 0,), ("u", 1, 0,), ("u", 0, 2,), ("y", 0, 1,), ("u", 0, 3,), ("y", 1, 0,), ("cd", 1,), ("qd", 1,), ("s", 0, 1,), ("y", 0, 0,), ("y", 3, 1,), ("y", 2, 1,), ("y", 1, 1,), ("s", 0, 0,), ("u", 1, 2,), ("u", 1, 3,), ("y", 3, 0,), ("y", 2, 0,), ("s", 1, 0,), ("y", 2, 2,), ("y", 2, 3,), ("s", 2, 1,), ("y", 0, 2,), ("y", 3, 3,), ("s", 3, 1,), ("y", 1, 2,), ("s", 2, 0,), ("s", 1, 1,), ("s", 2, 2,), ("s", 1, 2,), ("y", 1, 3,), ("s", 0, 2,), ("y", 0, 3,), ("y", 3, 2,), ("s", 3, 0,), ("s", 1, 3,), ("s", 0, 3,), ("s", 3, 2,), ("s", 2, 3,), ("s", 3, 3,)]
 FIN = [["V","V","V","V"],["V","V","V","V"]]
-YMUL = ["V","V","V","V"]
-MEMSET = ["V","G","V","G"]
-LOADS = [["idx",1],["tsc",1],["wr00",1],["wr01",1],["wtsc",1],["tab0",1],["tab1",1],["wr10",1],["wr11b",1],["wr11a",2],["wgo3",1],["wt",1],["wd00",1],["wgo0",1],["wgo1",1],["wd10",2],["wd01",2],["wgo2",1],["idx2",1],["wd11",1]]
+YMUL = ["F","F","F","F"]
+MEMSET = ["G","G","G","G"]
+GATE = {"wd1":"qr01","cd0":"cr00","y00":"u02","wgo":"cr10","y22":"u13","cd1":"qr00","y20":"u11","y23":"u11","y32":"u03","y03":"u00","y02":"u12","y12":"u13","y11":"u11","y31":"u02","y21":"u10","y10":"u00","y33":"u10","y30":"u01"}
+GSPLIT = 1
+LOADS = [["idx",1],["tab1",1],["tab0",1],["tsc",1],["wr00",1],["wr01",1],["wgo1",1],["wr10",1],["wr11a",2],["wd01",2],["wr11b",2],["wd11",1],["wtsc",1],["wd10",2],["wgo3",1],["idx2",1],["wd00",1],["wgo0",1],["wgo2",1],["wt",1]]
 
 
 def tile_list_gene_regulation_derivatives_kernel(
@@ -36,51 +38,90 @@ def tile_list_gene_regulation_derivatives_kernel(
     starts = [sum(CHUNKS[:c]) for c in range(len(CHUNKS))]
 
     with ExitStack() as ctx:
+        lists = ctx.enter_context(tc.tile_pool(name="lists", bufs=1))
         keep = ctx.enter_context(tc.tile_pool(name="keep", bufs=1))
-        hill = ctx.enter_context(tc.tile_pool(name="hill", bufs=4))
-        ypool = ctx.enter_context(tc.tile_pool(name="ypool", bufs=8))
-        apsum = ctx.enter_context(tc.psum_pool(name="apsum", bufs=4))
-        ypsum = ctx.enter_context(tc.psum_pool(name="ypsum", bufs=4))
+        psum = ctx.enter_context(tc.psum_pool(name="psum", bufs=1))
+        a_banks = [psum.tile([P, BANK], F32, name="a_bank%d" % i) for i in range(2)]
+        y_banks = [psum.tile([P, BANK], F32, name="y_bank%d" % i) for i in range(6)]
+        sq_ring = [keep.tile([P, 4 * 256], F32, name="sq%d" % i, align_bytes=64) for i in range(3)]
+        inv_ring = [keep.tile([P, 4 * 256], F32, name="inv%d" % i, align_bytes=64) for i in range(3)]
+        h_ring = [keep.tile([P, 4 * 256], BF16, name="h_bf%d" % i, align_bytes=64) for i in range(3)]
+        y_ring = [keep.tile([P, 256], F32, name="y%d" % i, align_bytes=64) for i in range(16)]
+        turns = {"a": 0, "y": 0, "unit": 0}
 
-        idx = keep.tile([P, S // 16], U16, name="idx")
-        idx2 = keep.tile([P, S // 16], U16, name="idx2")
-        tab_w = [keep.tile([P, T], I32, name="tab_w%d" % a, align_bytes=64) for a in range(2)]
-        tab_s = keep.tile([P, T // 4], I32, name="tab_s", align_bytes=64)
-        wr_raw = [[keep.tile([P, 4, 512], F32, name="wr_raw%d%d" % (b, a), align_bytes=64) for a in range(2)] for b in range(2)]
-        wr_bf = [[keep.tile([P, 2048], BF16, name="wr_bf%d%d" % (b, a), align_bytes=64) for a in range(2)] for b in range(2)]
+        def turn(kind):
+            turns[kind] += 1
+            return turns[kind] - 1
+
+        def slot(key):
+            source = GATE.get(key)
+            if source is None:
+                return "slot_" + key
+            kind, rest = source[:2], source[2:]
+            if kind in ("cr", "cd"):
+                return slot("w" + kind[1] + rest)
+            if kind in ("qr", "qd"):
+                return slot("c" + kind[1] + rest)
+            return "slot_" + source
+
+        words = {"wr": 2048, "wd": 2048, "wg": 1024, "cr": 1024, "cd": 1024}
+        keys = ["wr00", "wr01", "wr10", "wr11", "wd0", "wd1", "wgo", "cr00", "cr01", "cr10", "cr11", "cd0", "cd1"]
+        rooms = {}
+
+        def room(key, size, dtype):
+            root = slot(key)
+            if root not in rooms:
+                most = max([words[k[:2]] for k in keys if slot(k) == root] + [size])
+                rooms[root] = keep.tile([P, most], F32, name="room_" + key, tag=root, align_bytes=64)
+            return rooms[root][:, 0:size].bitcast(dtype) if dtype != F32 else rooms[root][:, 0:size]
+
+        idx = lists.tile([P, S // 16], U16, name="idx")
+        idx2 = lists.tile([P, S // 16], U16, name="idx2")
+        tab_w = [keep.tile([P, T], I32, name="tab_w%d" % a, tag="slot_ga%d" % a, align_bytes=64) for a in range(2)]
+        tab_s = keep.tile([P, T // 4], I32, name="tab_s", tag="slot_gb0", align_bytes=64)
+        wr_raw = {}
+        wr_bf = {}
         wr_q = [[keep.tile([P, 512], U32, name="wr_q%d%d" % (b, a), align_bytes=64) for a in range(2)] for b in range(2)]
         wr_s = [[keep.tile([P, 512], U8, name="wr_s%d%d" % (b, a), align_bytes=64) for a in range(2)] for b in range(2)]
-        wd_raw = [[keep.tile([P, 4, 256], F32, name="wd_raw%d%d" % (g, a), align_bytes=64) for a in range(2)] for g in range(2)]
-        wd_bf = [keep.tile([P, 2, 1024], BF16, name="wd_bf%d" % g, align_bytes=64) for g in range(2)]
+        wd_raw = {}
+        wd_bf = {}
         wd_q = [keep.tile([P, 2, 256], U32, name="wd_q%d" % g, align_bytes=64) for g in range(2)]
         wd_s = [keep.tile([P, 2, 256], U8, name="wd_s%d" % g, align_bytes=64) for g in range(2)]
         wt_w = keep.tile([P, 2, 1024], U8, name="wt_w", align_bytes=64)
         wt_s = keep.tile([P, 2, 512], U8, name="wt_s", align_bytes=64)
         rate_t = keep.tile([P, 2, 4], F32, name="rate_t")
-        wgo_t = [keep.tile([P, w], F32, name="wgo%d" % c, align_bytes=64) for c, w in enumerate(CHUNKS)]
+        wgo_all = {}
         cache = [keep.tile([P, T2], F32, name="cache%d" % n, align_bytes=64) for n in range(4)]
-        v_w = [[keep.tile([P, w], U32, name="v_w%d%d" % (c, a), align_bytes=64) for a in range(2)] for c, w in enumerate(CHUNKS)]
-        v_s = [keep.tile([P, w], U8, name="v_s%d" % c, align_bytes=64) for c, w in enumerate(CHUNKS)]
+        v_all = [keep.tile([P, S], U32, name="v_w%d" % a, align_bytes=64) for a in range(2)]
+        vs_all = keep.tile([P, S], U8, name="v_s", align_bytes=64)
+        v_w = [[v_all[a][:, starts[c] : starts[c] + w] for a in range(2)] for c, w in enumerate(CHUNKS)]
+        v_s = [vs_all[:, starts[c] : starts[c] + w] for c, w in enumerate(CHUNKS)]
         h_q = [[keep.tile([P, w], U32, name="h_q%d%d" % (c, b), align_bytes=64) for b in range(2)] for c, w in enumerate(CHUNKS)]
         h_s = [[keep.tile([P, w], U8, name="h_s%d%d" % (c, b), align_bytes=64) for b in range(2)] for c, w in enumerate(CHUNKS)]
 
         warm = keep.tile([P, 1], F32, name="warm")
-        nc.gpsimd.memset(warm[:], 1.0)
+        nc.vector.memset(warm[:], 1.0)
         nc.scalar.activation(out=warm[:], in_=warm[:], func=ACT.Abs_reciprocal_sqrt)
-        nc.gpsimd.memset(tab_s[:], 0)
-        nc.gpsimd.memset(wt_s[:].rearrange("p a n -> p (a n)").bitcast(I32), 0)
+        nc.vector.memset(tab_s[:], 0)
+        nc.vector.memset(wt_s[:].rearrange("p a n -> p (a n)").bitcast(I32), 0)
         for n in range(4):
             (nc.vector if MEMSET[n] == "V" else nc.gpsimd).memset(cache[n][:], 0.0)
 
         def load_wr(b, a, lo, hi, pieces):
+            if (b, a) not in wr_raw:
+                group = "wr%d%d" % (b, a)
+                wr_raw[(b, a)] = room(group, 2048, F32).rearrange("p (j c) -> p j c", j=4)
             src = wr[512 * a : 512 * (a + 1), 512 * b + lo : 512 * b + hi].rearrange("(p j) c -> p j c", j=4)
             for j in range(0, 4, 4 // pieces):
-                nc.sync.dma_start(out=wr_raw[b][a][:, j : j + 4 // pieces, lo:hi], in_=src[:, j : j + 4 // pieces, :])
+                nc.sync.dma_start(out=wr_raw[(b, a)][:, j : j + 4 // pieces, lo:hi], in_=src[:, j : j + 4 // pieces, :])
 
         def load_wd(g, a, pieces):
+            if g not in wd_raw:
+                group = "wd%d" % g
+                wd_raw[g] = room(group, 2048, F32).rearrange("p (a j c) -> p a j c", a=2, j=4)
             src = wd[512 * a : 512 * (a + 1), 256 * g : 256 * (g + 1)].rearrange("(p j) c -> p j c", j=4)
             for j in range(0, 4, 4 // pieces):
-                nc.sync.dma_start(out=wd_raw[g][a][:, j : j + 4 // pieces, :], in_=src[:, j : j + 4 // pieces, :])
+                nc.sync.dma_start(out=wd_raw[g][:, a, j : j + 4 // pieces, :], in_=src[:, j : j + 4 // pieces, :])
 
         def load_tab(a, pieces):
             src = tab_words[a].rearrange("p t i -> p (t i)").bitcast(I32)
@@ -88,7 +129,13 @@ def tile_list_gene_regulation_derivatives_kernel(
                 nc.sync.dma_start(out=tab_w[a][:, t : t + T // pieces], in_=src[:, t : t + T // pieces])
 
         nc.scalar.dma_start(out=rate_t[:], in_=rate.rearrange("(b p t) -> p b t", b=2, t=4))
-        for name, pieces in LOADS:
+        def wgo_cols(c):
+            return wgo_all[0][:, starts[c] : starts[c] + CHUNKS[c]]
+
+        def group_of(name):
+            return "wgo" if name.startswith("wgo") else name[:3] if name.startswith("wd") else name[:4]
+
+        def load(name, pieces):
             if name == "idx":
                 nc.sync.dma_start(idx[:], offs)
             elif name == "idx2":
@@ -113,7 +160,13 @@ def tile_list_gene_regulation_derivatives_kernel(
                 load_wd(int(name[2]), int(name[3]), pieces)
             else:
                 c = int(name[3])
-                nc.sync.dma_start(out=wgo_t[c][:], in_=wgo[:, starts[c] : starts[c] + CHUNKS[c]])
+                if not wgo_all:
+                    wgo_all[0] = room("wgo", 1024, F32)
+                nc.sync.dma_start(out=wgo_cols(c), in_=wgo[:, starts[c] : starts[c] + CHUNKS[c]])
+
+        for name, pieces in LOADS:
+            if group_of(name) not in GATE:
+                load(name, pieces)
 
         def cast(engine, dst, src):
             if engine == "V":
@@ -124,22 +177,24 @@ def tile_list_gene_regulation_derivatives_kernel(
                 nc.gpsimd.tensor_scalar(dst, src, 1.0, 0.0, MULT, ADD)
 
         def cast_wr(b, a):
+            wr_bf[(b, a)] = room("cr%d%d" % (b, a), 1024, BF16)
             engines = WR_CAST[b][a]
             step = 128 // len(engines)
             for i, engine in enumerate(engines):
                 walk = "p m t j" if engine == "G" else "p m j t"
-                dst = wr_bf[b][a][:].rearrange("p (t m j) -> " + walk, t=4, j=4)
-                src = wr_raw[b][a][:].rearrange("p j (m t) -> " + walk, t=4)
+                dst = wr_bf[(b, a)][:].rearrange("p (t m j) -> " + walk, t=4, j=4)
+                src = wr_raw[(b, a)][:].rearrange("p j (m t) -> " + walk, t=4)
                 cast(engine, dst[:, i * step : (i + 1) * step], src[:, i * step : (i + 1) * step])
 
         def quant_wr(b, a):
-            nc.vector.quantize_mx(out=wr_q[b][a][:].bitcast(FP8X4), scales=wr_s[b][a][:], in_=wr_bf[b][a][:])
+            nc.vector.quantize_mx(out=wr_q[b][a][:].bitcast(FP8X4), scales=wr_s[b][a][:], in_=wr_bf[(b, a)][:])
 
         def cast_wd(g):
+            wd_bf[g] = room("cd%d" % g, 1024, BF16).rearrange("p (a n) -> p a n", a=2)
             for a in range(2):
                 walk = "p c i j" if WD_CAST[g][a] == "G" else "p c j i"
                 dst = wd_bf[g][:, a, :].rearrange("p (c i j) -> " + walk, i=4, j=4)
-                src = wd_raw[g][a][:].rearrange("p j (c i) -> " + walk, i=4)
+                src = wd_raw[g][:, a].rearrange("p j (c i) -> " + walk, i=4)
                 cast(WD_CAST[g][a], dst, src)
 
         def quant_wd(g):
@@ -153,27 +208,37 @@ def tile_list_gene_regulation_derivatives_kernel(
             return tile[:, starts[c] // 16 : (starts[c] + CHUNKS[c]) // 16]
 
         def gather_words(c, a):
-            nc.vector.tensor_copy(v_w[c][a][:], tab_w[a][:].bitcast(U32).indirect(entries(idx, c)))
+            nc.vector.tensor_copy(v_w[c][a], tab_w[a][:].bitcast(U32).indirect(entries(idx, c)))
 
         def gather_scales(c):
-            nc.vector.tensor_copy(v_s[c][:], tab_s[:].bitcast(U8).indirect(entries(idx, c)))
+            nc.vector.tensor_copy(v_s[c], tab_s[:].bitcast(U8).indirect(entries(idx, c)))
+
+        def gather_all_words(a):
+            nc.vector.tensor_copy(v_all[a][:], tab_w[a][:].bitcast(U32).indirect(idx[:]))
+
+        def gather_all_scales(unused):
+            nc.vector.tensor_copy(vs_all[:], tab_s[:].bitcast(U8).indirect(idx[:]))
 
         def unit(b, c):
             w = CHUNKS[c]
             per_bank = BANK // w
-            sq = hill.tile([P, 4, w], F32, name="sq", align_bytes=64)
-            inv = hill.tile([P, 4, w], F32, name="inv", align_bytes=64)
-            h_bf = hill.tile([P, 4 * w], BF16, name="h_bf", align_bytes=64)
+            mine = turn("unit") % len(sq_ring)
+            if "u%d%d" % (b, c) in [GATE[k] for k in GATE]:
+                sq = room("u%d%d" % (b, c), 4 * w, F32).rearrange("p (t c) -> p t c", t=4)
+            else:
+                sq = sq_ring[mine][:, 0 : 4 * w].rearrange("p (t c) -> p t c", t=4)
+            inv = inv_ring[mine][:, 0 : 4 * w].rearrange("p (t c) -> p t c", t=4)
+            h_bf = h_ring[mine][:, 0 : 4 * w]
             for t0 in range(0, 4, per_bank):
-                acc = apsum.tile([P, per_bank, w], F32, name="acc")
+                acc = a_banks[turn("a") % len(a_banks)][:].rearrange("p (t c) -> p t c", c=w)
                 for t in range(t0, t0 + per_bank):
                     for a in range(2):
                         nc.tensor.matmul_mx(
                             out=acc[:, t - t0, :],
                             lhsT=wr_q[b][a][:, P * t : P * (t + 1)].bitcast(FP8X4),
                             lhsT_scale=wr_s[b][a][:, P * t : P * (t + 1)],
-                            rhs=v_w[c][a][:].bitcast(FP8X4),
-                            rhs_scale=v_s[c][4 * a : P, :],
+                            rhs=v_w[c][a].bitcast(FP8X4),
+                            rhs_scale=vs_all[4 * a : P, starts[c] : starts[c] + w],
                             start=(a == 0),
                             stop=(a == 1),
                         )
@@ -197,12 +262,15 @@ def tile_list_gene_regulation_derivatives_kernel(
                     nc.gpsimd.tensor_scalar(sq_r[:, t, :], sq[:, t, :], r_col, 0.0, MULT, ADD)
             fin = nc.gpsimd if FIN[b][c] == "G" else nc.vector
             walk = "p c i t" if FIN[b][c] == "G" else "p c t i"
-            fin.tensor_tensor(
-                h_bf[:].rearrange("p (c i t) -> " + walk, i=4, t=4),
-                sq_r[:].rearrange("p t (c i) -> " + walk, i=4),
-                inv[:].rearrange("p t (c i) -> " + walk, i=4),
-                MULT,
-            )
+            parts = GSPLIT if FIN[b][c] == "G" else 1
+            for i in range(parts):
+                part = slice(i * w // 4 // parts, (i + 1) * w // 4 // parts)
+                fin.tensor_tensor(
+                    h_bf[:].rearrange("p (c i t) -> " + walk, i=4, t=4)[:, part],
+                    sq_r[:].rearrange("p t (c i) -> " + walk, i=4)[:, part],
+                    inv[:].rearrange("p t (c i) -> " + walk, i=4)[:, part],
+                    MULT,
+                )
             nc.vector.quantize_mx(out=h_q[c][b][:].bitcast(FP8X4), scales=h_s[c][b][:], in_=h_bf[:])
 
         y_sb = {}
@@ -212,7 +280,8 @@ def tile_list_gene_regulation_derivatives_kernel(
             w = CHUNKS[c]
             width = 512 if w == 512 else 128
             g, n0 = n // 2, P * (n % 2)
-            acc = ypsum.tile([P, w], F32, name="yacc")
+            mine = turn("y")
+            acc = y_banks[mine % len(y_banks)][:, 0:w]
             for j0 in range(0, w, width):
                 cols = slice(j0, j0 + width)
                 for b in range(2):
@@ -230,24 +299,29 @@ def tile_list_gene_regulation_derivatives_kernel(
                         out=acc[:, cols],
                         lhsT=wd_q[g][:, a, n0 : n0 + P].bitcast(FP8X4),
                         lhsT_scale=wd_s[g][:, a, n0 : n0 + P],
-                        rhs=v_w[c][a][:, cols].bitcast(FP8X4),
-                        rhs_scale=v_s[c][4 * a : P, cols],
+                        rhs=v_all[a][:, starts[c] + j0 : starts[c] + j0 + width].bitcast(FP8X4),
+                        rhs_scale=vs_all[4 * a : P, starts[c] + j0 : starts[c] + j0 + width],
                         start=False,
                         stop=(a == 1),
                     )
-            y = ypool.tile([P, w], F32, name="y", align_bytes=64)
+            y = y_ring[mine % len(y_ring)][:, 0:w]
+            source = GATE.get("y%d%d" % (n, c))
+            if source is not None:
+                place = turns.get(source, 0)
+                turns[source] = place + 1
+                y = rooms["slot_" + source][:, place * w : (place + 1) * w]
             if YMUL[c] == "V":
-                nc.vector.tensor_tensor(y[:], acc[:], wgo_t[c][:], MULT)
+                nc.vector.tensor_tensor(y[:], acc[:], wgo_cols(c), MULT)
             else:
                 nc.scalar.activation(out=y[:], in_=acc[:], func=ACT.Copy)
             if YMUL[c] == "G":
-                nc.gpsimd.tensor_tensor(y[:], y[:], wgo_t[c][:], MULT)
+                nc.gpsimd.tensor_tensor(y[:], y[:], wgo_cols(c), MULT)
             y_sb[(n, c)] = y
 
         def scatter(n, c):
             window = cache[n][:].indirect(entries(idx2, c))
             if YMUL[c] == "F":
-                nc.vector.tensor_tensor(window, y_sb[(n, c)][:], wgo_t[c][:], MULT)
+                nc.vector.tensor_tensor(window, y_sb[(n, c)][:], wgo_cols(c), MULT)
             else:
                 nc.vector.tensor_copy(window, y_sb[(n, c)][:])
             done.append(n)
@@ -255,8 +329,12 @@ def tile_list_gene_regulation_derivatives_kernel(
                 nc.sync.dma_start(out=out[P * n : P * (n + 1), :], in_=cache[n][:])
 
         steps = {
-            "gw": gather_words, "gs": gather_scales, "cr": cast_wr, "qr": quant_wr, "cd": cast_wd, "qd": quant_wd,
+            "ga": gather_all_words, "gb": gather_all_scales, "gw": gather_words, "gs": gather_scales, "cr": cast_wr, "qr": quant_wr, "cd": cast_wd, "qd": quant_wd,
             "u": unit, "y": product, "s": scatter,
         }
         for step in ORDER:
             steps[step[0]](*step[1:])
+            key = step[0] + "".join([str(i) for i in step[1:]])
+            for name, pieces in LOADS:
+                if GATE.get(group_of(name)) == key:
+                    load(name, pieces)

@@ -11,330 +11,263 @@ U8 = mybir.dt.uint8
 FP8X4 = mybir.dt.float8_e4m3fn_x4
 FP4X4 = mybir.dt.float4_e2m1fn_x4
 MULT = mybir.AluOpType.mult
-ADD = mybir.AluOpType.add
 ACT = mybir.ActivationFunctionType
 
 K, H, N, T, S, T2 = 1024, 1024, 512, 2048, 1024, 2048
 FLOPS = 2 * K * H * S + 2 * H * N * S + 2 * K * N * S
+
 P = 128
+PACK = 4
+PASS = P * PACK
+PASSES = K // PASS
+ROW_TILES = N // P
+CHUNK = 256
+CHUNKS = S // CHUNK
+LIST_COLS = CHUNK // 16
 BANK = 512
-CHUNKS = [256,256,256,256]
-RATE_ON = [["V","B","S","S"],["B","B","S","S"]]
-WR_CAST = [["SV","VS"],["VS","VV"]]
-WD_CAST = ["VV","SV"]
-ORDER = [("cr", 1, 1,), ("cr", 0, 1,), ("ga", 1,), ("cr", 0, 0,), ("qr", 0, 1,), ("cr", 1, 0,), ("qr", 0, 0,), ("qr", 1, 0,), ("qr", 1, 1,), ("gb", 0,), ("cd", 0,), ("ga", 0,), ("u", 0, 1,), ("u", 0, 0,), ("u", 1, 1,), ("qd", 0,), ("u", 1, 0,), ("u", 0, 2,), ("y", 0, 1,), ("u", 0, 3,), ("y", 1, 0,), ("cd", 1,), ("qd", 1,), ("s", 0, 1,), ("y", 0, 0,), ("y", 3, 1,), ("y", 2, 1,), ("y", 1, 1,), ("s", 0, 0,), ("u", 1, 2,), ("u", 1, 3,), ("y", 3, 0,), ("y", 2, 0,), ("s", 1, 0,), ("y", 2, 2,), ("y", 2, 3,), ("s", 2, 1,), ("y", 0, 2,), ("y", 3, 3,), ("s", 3, 1,), ("y", 1, 2,), ("s", 2, 0,), ("s", 1, 1,), ("s", 2, 2,), ("s", 1, 2,), ("y", 1, 3,), ("s", 0, 2,), ("y", 0, 3,), ("y", 3, 2,), ("s", 3, 0,), ("s", 1, 3,), ("s", 0, 3,), ("s", 3, 2,), ("s", 2, 3,), ("s", 3, 3,)]
-FIN = [["V","V","V","V"],["V","V","V","V"]]
-YMUL = ["F","F","F","F"]
-MEMSET = ["G","G","G","G"]
-GATE = {"wd1":"qr01","cd0":"cr00","y00":"u02","wgo":"cr10","y22":"u13","cd1":"qr00","y20":"u11","y23":"u11","y32":"u03","y03":"u00","y02":"u12","y12":"u13","y11":"u11","y31":"u02","y21":"u10","y10":"u00","y33":"u10","y30":"u01"}
-GSPLIT = 1
-LOADS = [["idx",1],["tab1",1],["tab0",1],["tsc",1],["wr00",1],["wr01",1],["wgo1",1],["wr10",1],["wr11a",2],["wd01",2],["wr11b",2],["wd11",1],["wtsc",1],["wd10",2],["wgo3",1],["idx2",1],["wd00",1],["wgo0",1],["wgo2",1],["wt",1]]
+Y_WIDTH = 128
+HALF = N // 2
+RUN = 4
+A_BANKS = 4
+Y_BANKS = 4
+HILL_SLOTS = 3
+
+RATE_BY = [
+    ["vector_both", "vector_rate", "scalar", "scalar"],
+    ["vector_both", "vector_both", "scalar", "scalar"],
+]
+WR_CAST_BY = [
+    [["scalar"], ["scalar", "vector"]],
+    [["scalar", "vector"], ["vector", "vector"]],
+]
+WD_CAST_BY = [["vector", "vector"], ["scalar", "vector"]]
 
 
 def tile_list_gene_regulation_derivatives_kernel(
     tc, tab_words, tab_scales, offs, wr, rate, wt4_words, wt4_scales, wd, wgo, offs2, out
 ):
     nc = tc.nc
-    starts = [sum(CHUNKS[:c]) for c in range(len(CHUNKS))]
+    both = range(PASSES)
 
     with ExitStack() as ctx:
         lists = ctx.enter_context(tc.tile_pool(name="lists", bufs=1))
         keep = ctx.enter_context(tc.tile_pool(name="keep", bufs=1))
         psum = ctx.enter_context(tc.psum_pool(name="psum", bufs=1))
-        a_banks = [psum.tile([P, BANK], F32, name="a_bank%d" % i) for i in range(2)]
-        y_banks = [psum.tile([P, BANK], F32, name="y_bank%d" % i) for i in range(6)]
-        sq_ring = [keep.tile([P, 4 * 256], F32, name="sq%d" % i, align_bytes=64) for i in range(3)]
-        inv_ring = [keep.tile([P, 4 * 256], F32, name="inv%d" % i, align_bytes=64) for i in range(3)]
-        h_ring = [keep.tile([P, 4 * 256], BF16, name="h_bf%d" % i, align_bytes=64) for i in range(3)]
-        y_ring = [keep.tile([P, 256], F32, name="y%d" % i, align_bytes=64) for i in range(16)]
-        turns = {"a": 0, "y": 0, "unit": 0}
 
-        def turn(kind):
-            turns[kind] += 1
-            return turns[kind] - 1
-
-        def slot(key):
-            source = GATE.get(key)
-            if source is None:
-                return "slot_" + key
-            kind, rest = source[:2], source[2:]
-            if kind in ("cr", "cd"):
-                return slot("w" + kind[1] + rest)
-            if kind in ("qr", "qd"):
-                return slot("c" + kind[1] + rest)
-            return "slot_" + source
-
-        words = {"wr": 2048, "wd": 2048, "wg": 1024, "cr": 1024, "cd": 1024}
-        keys = ["wr00", "wr01", "wr10", "wr11", "wd0", "wd1", "wgo", "cr00", "cr01", "cr10", "cr11", "cd0", "cd1"]
-        rooms = {}
-
-        def room(key, size, dtype):
-            root = slot(key)
-            if root not in rooms:
-                most = max([words[k[:2]] for k in keys if slot(k) == root] + [size])
-                rooms[root] = keep.tile([P, most], F32, name="room_" + key, tag=root, align_bytes=64)
-            return rooms[root][:, 0:size].bitcast(dtype) if dtype != F32 else rooms[root][:, 0:size]
+        def held(name, shape, dtype):
+            return keep.tile(shape, dtype, name=name, align_bytes=64)
 
         idx = lists.tile([P, S // 16], U16, name="idx")
         idx2 = lists.tile([P, S // 16], U16, name="idx2")
-        tab_w = [keep.tile([P, T], I32, name="tab_w%d" % a, tag="slot_ga%d" % a, align_bytes=64) for a in range(2)]
-        tab_s = keep.tile([P, T // 4], I32, name="tab_s", tag="slot_gb0", align_bytes=64)
-        wr_raw = {}
-        wr_bf = {}
-        wr_q = [[keep.tile([P, 512], U32, name="wr_q%d%d" % (b, a), align_bytes=64) for a in range(2)] for b in range(2)]
-        wr_s = [[keep.tile([P, 512], U8, name="wr_s%d%d" % (b, a), align_bytes=64) for a in range(2)] for b in range(2)]
-        wd_raw = {}
-        wd_bf = {}
-        wd_q = [keep.tile([P, 2, 256], U32, name="wd_q%d" % g, align_bytes=64) for g in range(2)]
-        wd_s = [keep.tile([P, 2, 256], U8, name="wd_s%d" % g, align_bytes=64) for g in range(2)]
-        wt_w = keep.tile([P, 2, 1024], U8, name="wt_w", align_bytes=64)
-        wt_s = keep.tile([P, 2, 512], U8, name="wt_s", align_bytes=64)
-        rate_t = keep.tile([P, 2, 4], F32, name="rate_t")
-        wgo_all = {}
-        cache = [keep.tile([P, T2], F32, name="cache%d" % n, align_bytes=64) for n in range(4)]
-        v_all = [keep.tile([P, S], U32, name="v_w%d" % a, align_bytes=64) for a in range(2)]
-        vs_all = keep.tile([P, S], U8, name="v_s", align_bytes=64)
-        v_w = [[v_all[a][:, starts[c] : starts[c] + w] for a in range(2)] for c, w in enumerate(CHUNKS)]
-        v_s = [vs_all[:, starts[c] : starts[c] + w] for c, w in enumerate(CHUNKS)]
-        h_q = [[keep.tile([P, w], U32, name="h_q%d%d" % (c, b), align_bytes=64) for b in range(2)] for c, w in enumerate(CHUNKS)]
-        h_s = [[keep.tile([P, w], U8, name="h_s%d%d" % (c, b), align_bytes=64) for b in range(2)] for c, w in enumerate(CHUNKS)]
+        a_banks = [psum.tile([P, BANK // CHUNK, CHUNK], F32, name="a_bank%d" % i) for i in range(A_BANKS)]
+        y_banks = [psum.tile([P, CHUNK], F32, name="y_bank%d" % i) for i in range(Y_BANKS)]
 
-        warm = keep.tile([P, 1], F32, name="warm")
-        nc.vector.memset(warm[:], 1.0)
-        nc.scalar.activation(out=warm[:], in_=warm[:], func=ACT.Abs_reciprocal_sqrt)
+        tab_w = [held("tab_w%d" % g, [P, T], I32) for g in both]
+        tab_s = held("tab_s", [P, T // 4], I32)
+        v_w = [held("v_w%d" % g, [P, S], U32) for g in both]
+        v_s = held("v_s", [P, S], U8)
+        wr_raw = [[held("wr_raw%d%d" % (b, g), [P, PACK, PASS], F32) for g in both] for b in both]
+        wr_bf = [[held("wr_bf%d%d" % (b, g), [P, PACK * PASS], BF16) for g in both] for b in both]
+        wr_q = [[held("wr_q%d%d" % (b, g), [P, PASS], U32) for g in both] for b in both]
+        wr_s = [[held("wr_s%d%d" % (b, g), [P, PASS], U8) for g in both] for b in both]
+        wd_raw = [held("wd_raw%d" % g, [P, PACK, N], F32) for g in both]
+        wd_bf = [held("wd_bf%d" % half, [P, PASSES, PACK * HALF], BF16) for half in range(2)]
+        wd_q = [held("wd_q%d" % half, [P, PASSES, HALF], U32) for half in range(2)]
+        wd_s = [held("wd_s%d" % half, [P, PASSES, HALF], U8) for half in range(2)]
+        wt_w = held("wt_w", [P, PASSES, 2 * N], U8)
+        wt_s = held("wt_s", [P, PASSES, N], U8)
+        rate_t = held("rate_t", [P, PASSES, PACK], F32)
+        wgo_t = held("wgo_t", [P, S], F32)
+        one = held("one", [P, 1], F32)
+        squares = [held("square%d" % i, [P, PACK, CHUNK], F32) for i in range(HILL_SLOTS)]
+        factors = [held("factor%d" % i, [P, PACK, CHUNK], F32) for i in range(HILL_SLOTS)]
+        h_bfs = [held("h_bf%d" % i, [P, PACK * CHUNK], BF16) for i in range(HILL_SLOTS)]
+        h_q = [[held("h_q%d%d" % (b, c), [P, CHUNK], U32) for c in range(CHUNKS)] for b in both]
+        h_s = [[held("h_s%d%d" % (b, c), [P, CHUNK], U8) for c in range(CHUNKS)] for b in both]
+        y_sb = [[held("y%d%d" % (n, c), [P, CHUNK], F32) for c in range(CHUNKS)] for n in range(ROW_TILES)]
+        cache = [held("cache%d" % n, [P, T2], F32) for n in range(ROW_TILES)]
+
+        nc.vector.memset(one[:], 1.0)
+        nc.scalar.activation(out=one[:], in_=one[:], func=ACT.Abs_reciprocal_sqrt)
+        nc.scalar.activation(out=one[:], in_=one[:], func=ACT.Sign)
         nc.vector.memset(tab_s[:], 0)
-        nc.vector.memset(wt_s[:].rearrange("p a n -> p (a n)").bitcast(I32), 0)
-        for n in range(4):
-            (nc.vector if MEMSET[n] == "V" else nc.gpsimd).memset(cache[n][:], 0.0)
+        nc.vector.memset(wt_s[:].rearrange("p g n -> p (g n)").bitcast(I32), 0)
+        for n in range(ROW_TILES):
+            nc.vector.memset(cache[n][:], 0.0)
 
-        def load_wr(b, a, lo, hi, pieces):
-            if (b, a) not in wr_raw:
-                group = "wr%d%d" % (b, a)
-                wr_raw[(b, a)] = room(group, 2048, F32).rearrange("p (j c) -> p j c", j=4)
-            src = wr[512 * a : 512 * (a + 1), 512 * b + lo : 512 * b + hi].rearrange("(p j) c -> p j c", j=4)
-            for j in range(0, 4, 4 // pieces):
-                nc.sync.dma_start(out=wr_raw[(b, a)][:, j : j + 4 // pieces, lo:hi], in_=src[:, j : j + 4 // pieces, :])
+        def rows_of_pass(weight, g):
+            return weight[PASS * g : PASS * (g + 1), :].rearrange("(p j) c -> p j c", j=PACK)
 
-        def load_wd(g, a, pieces):
-            if g not in wd_raw:
-                group = "wd%d" % g
-                wd_raw[g] = room(group, 2048, F32).rearrange("p (a j c) -> p a j c", a=2, j=4)
-            src = wd[512 * a : 512 * (a + 1), 256 * g : 256 * (g + 1)].rearrange("(p j) c -> p j c", j=4)
-            for j in range(0, 4, 4 // pieces):
-                nc.sync.dma_start(out=wd_raw[g][:, a, j : j + 4 // pieces, :], in_=src[:, j : j + 4 // pieces, :])
-
-        def load_tab(a, pieces):
-            src = tab_words[a].rearrange("p t i -> p (t i)").bitcast(I32)
-            for t in range(0, T, T // pieces):
-                nc.sync.dma_start(out=tab_w[a][:, t : t + T // pieces], in_=src[:, t : t + T // pieces])
-
-        nc.scalar.dma_start(out=rate_t[:], in_=rate.rearrange("(b p t) -> p b t", b=2, t=4))
-        def wgo_cols(c):
-            return wgo_all[0][:, starts[c] : starts[c] + CHUNKS[c]]
-
-        def group_of(name):
-            return "wgo" if name.startswith("wgo") else name[:3] if name.startswith("wd") else name[:4]
-
-        def load(name, pieces):
-            if name == "idx":
-                nc.sync.dma_start(idx[:], offs)
-            elif name == "idx2":
-                nc.sync.dma_start(idx2[:], offs2)
-            elif name == "tsc":
-                for q in range(4):
-                    nc.sync.dma_start(out=tab_s[32 * q : 32 * q + 8, :], in_=tab_scales[:, 4 * q : 4 * q + 4, :].bitcast(I32))
-            elif name == "wtsc":
-                for q in range(4):
+        nc.scalar.dma_start(out=rate_t[:], in_=rate.rearrange("(b p t) -> p b t", b=PASSES, t=PACK))
+        nc.sync.dma_start(idx[:], offs)
+        for g in both:
+            nc.sync.dma_start(out=tab_w[g][:], in_=tab_words[g].rearrange("p t i -> p (t i)").bitcast(I32))
+        for q in range(4):
+            nc.sync.dma_start(out=tab_s[32 * q : 32 * q + 8, :], in_=tab_scales[:, 4 * q : 4 * q + 4, :].bitcast(I32))
+        for b in both:
+            for g in both:
+                width = PASS // 2 if (b, g) == (PASSES - 1, PASSES - 1) else PASS
+                for c0 in range(0, PASS, width):
                     nc.sync.dma_start(
-                        out=wt_s[32 * q : 32 * q + 4, :, :].bitcast(I32),
-                        in_=wt4_scales[:, 4 * q : 4 * q + 4, :].rearrange("a r n -> r a n").bitcast(I32),
+                        out=wr_raw[b][g][:, :, c0 : c0 + width],
+                        in_=rows_of_pass(wr, g)[:, :, PASS * b + c0 : PASS * b + c0 + width],
                     )
-            elif name == "wt":
-                nc.sync.dma_start(out=wt_w[:].bitcast(I32), in_=wt4_words.rearrange("a p c -> p a c").bitcast(I32))
-            elif name.startswith("tab"):
-                load_tab(int(name[3]), pieces)
-            elif name.startswith("wr"):
-                lo, hi = {"": (0, 512), "a": (0, 256), "b": (256, 512)}[name[4:]]
-                load_wr(int(name[2]), int(name[3]), lo, hi, pieces)
-            elif name.startswith("wd"):
-                load_wd(int(name[2]), int(name[3]), pieces)
-            else:
-                c = int(name[3])
-                if not wgo_all:
-                    wgo_all[0] = room("wgo", 1024, F32)
-                nc.sync.dma_start(out=wgo_cols(c), in_=wgo[:, starts[c] : starts[c] + CHUNKS[c]])
-
-        for name, pieces in LOADS:
-            if group_of(name) not in GATE:
-                load(name, pieces)
+        for g in both:
+            nc.sync.dma_start(out=wd_raw[g][:], in_=rows_of_pass(wd, g))
+        for q in range(4):
+            nc.sync.dma_start(
+                out=wt_s[32 * q : 32 * q + 4, :, :].bitcast(I32),
+                in_=wt4_scales[:, 4 * q : 4 * q + 4, :].rearrange("g r n -> r g n").bitcast(I32),
+            )
+        nc.sync.dma_start(out=wt_w[:].bitcast(I32), in_=wt4_words.rearrange("g p c -> p g c").bitcast(I32))
+        nc.sync.dma_start(idx2[:], offs2)
+        nc.sync.dma_start(out=wgo_t[:], in_=wgo)
 
         def cast(engine, dst, src):
-            if engine == "V":
+            if engine == "vector":
                 nc.vector.tensor_copy(out=dst, in_=src)
-            elif engine == "S":
-                nc.scalar.activation(out=dst, in_=src, func=ACT.Copy)
             else:
-                nc.gpsimd.tensor_scalar(dst, src, 1.0, 0.0, MULT, ADD)
+                nc.scalar.copy(out=dst, in_=src)
 
-        def cast_wr(b, a):
-            wr_bf[(b, a)] = room("cr%d%d" % (b, a), 1024, BF16)
-            engines = WR_CAST[b][a]
-            step = 128 // len(engines)
-            for i, engine in enumerate(engines):
-                walk = "p m t j" if engine == "G" else "p m j t"
-                dst = wr_bf[(b, a)][:].rearrange("p (t m j) -> " + walk, t=4, j=4)
-                src = wr_raw[(b, a)][:].rearrange("p j (m t) -> " + walk, t=4)
-                cast(engine, dst[:, i * step : (i + 1) * step], src[:, i * step : (i + 1) * step])
+        def cast_wr(b, g):
+            dst = wr_bf[b][g][:].rearrange("p (t m j) -> p m j t", t=PACK, j=PACK)
+            src = wr_raw[b][g][:].rearrange("p j (m t) -> p m j t", t=PACK)
+            share = P // len(WR_CAST_BY[b][g])
+            for i, engine in enumerate(WR_CAST_BY[b][g]):
+                cast(engine, dst[:, i * share : (i + 1) * share], src[:, i * share : (i + 1) * share])
 
-        def quant_wr(b, a):
-            nc.vector.quantize_mx(out=wr_q[b][a][:].bitcast(FP8X4), scales=wr_s[b][a][:], in_=wr_bf[(b, a)][:])
+        def quantise_wr(b, g):
+            nc.vector.quantize_mx(out=wr_q[b][g][:].bitcast(FP8X4), scales=wr_s[b][g][:], in_=wr_bf[b][g][:])
 
-        def cast_wd(g):
-            wd_bf[g] = room("cd%d" % g, 1024, BF16).rearrange("p (a n) -> p a n", a=2)
-            for a in range(2):
-                walk = "p c i j" if WD_CAST[g][a] == "G" else "p c j i"
-                dst = wd_bf[g][:, a, :].rearrange("p (c i j) -> " + walk, i=4, j=4)
-                src = wd_raw[g][:, a].rearrange("p j (c i) -> " + walk, i=4)
-                cast(WD_CAST[g][a], dst, src)
+        def cast_wd(half):
+            for g in both:
+                dst = wd_bf[half][:, g, :].rearrange("p (c i j) -> p c j i", i=RUN, j=PACK)
+                src = wd_raw[g][:, :, HALF * half : HALF * (half + 1)].rearrange("p j (c i) -> p c j i", i=RUN)
+                cast(WD_CAST_BY[half][g], dst, src)
 
-        def quant_wd(g):
+        def quantise_wd(half):
             nc.vector.quantize_mx(
-                out=wd_q[g][:].rearrange("p a n -> p (a n)").bitcast(FP8X4),
-                scales=wd_s[g][:].rearrange("p a n -> p (a n)"),
-                in_=wd_bf[g][:].rearrange("p a n -> p (a n)"),
+                out=wd_q[half][:].rearrange("p g n -> p (g n)").bitcast(FP8X4),
+                scales=wd_s[half][:].rearrange("p g n -> p (g n)"),
+                in_=wd_bf[half][:].rearrange("p g n -> p (g n)"),
             )
 
-        def entries(tile, c):
-            return tile[:, starts[c] // 16 : (starts[c] + CHUNKS[c]) // 16]
+        def table_operand(g, cols):
+            return v_w[g][:, cols].bitcast(FP8X4), v_s[4 * g : P, cols]
 
-        def gather_words(c, a):
-            nc.vector.tensor_copy(v_w[c][a], tab_w[a][:].bitcast(U32).indirect(entries(idx, c)))
+        pieces_done = []
 
-        def gather_scales(c):
-            nc.vector.tensor_copy(v_s[c], tab_s[:].bitcast(U8).indirect(entries(idx, c)))
-
-        def gather_all_words(a):
-            nc.vector.tensor_copy(v_all[a][:], tab_w[a][:].bitcast(U32).indirect(idx[:]))
-
-        def gather_all_scales(unused):
-            nc.vector.tensor_copy(vs_all[:], tab_s[:].bitcast(U8).indirect(idx[:]))
-
-        def unit(b, c):
-            w = CHUNKS[c]
-            per_bank = BANK // w
-            mine = turn("unit") % len(sq_ring)
-            if "u%d%d" % (b, c) in [GATE[k] for k in GATE]:
-                sq = room("u%d%d" % (b, c), 4 * w, F32).rearrange("p (t c) -> p t c", t=4)
-            else:
-                sq = sq_ring[mine][:, 0 : 4 * w].rearrange("p (t c) -> p t c", t=4)
-            inv = inv_ring[mine][:, 0 : 4 * w].rearrange("p (t c) -> p t c", t=4)
-            h_bf = h_ring[mine][:, 0 : 4 * w]
-            for t0 in range(0, 4, per_bank):
-                acc = a_banks[turn("a") % len(a_banks)][:].rearrange("p (t c) -> p t c", c=w)
+        def hill(b, c):
+            turn = len(pieces_done)
+            pieces_done.append((b, c))
+            square, factor, h_bf = squares[turn % HILL_SLOTS], factors[turn % HILL_SLOTS], h_bfs[turn % HILL_SLOTS]
+            per_bank = BANK // CHUNK
+            for t0 in range(0, PACK, per_bank):
+                bank = a_banks[(PACK * turn + t0) // per_bank % A_BANKS]
                 for t in range(t0, t0 + per_bank):
-                    for a in range(2):
+                    for g in both:
+                        words, scales = table_operand(g, slice(CHUNK * c, CHUNK * (c + 1)))
                         nc.tensor.matmul_mx(
-                            out=acc[:, t - t0, :],
-                            lhsT=wr_q[b][a][:, P * t : P * (t + 1)].bitcast(FP8X4),
-                            lhsT_scale=wr_s[b][a][:, P * t : P * (t + 1)],
-                            rhs=v_w[c][a].bitcast(FP8X4),
-                            rhs_scale=vs_all[4 * a : P, starts[c] : starts[c] + w],
-                            start=(a == 0),
-                            stop=(a == 1),
+                            out=bank[:, t - t0, :],
+                            lhsT=wr_q[b][g][:, P * t : P * (t + 1)].bitcast(FP8X4),
+                            lhsT_scale=wr_s[b][g][:, P * t : P * (t + 1)],
+                            rhs=words,
+                            rhs_scale=scales,
+                            start=(g == 0),
+                            stop=(g == PASSES - 1),
                         )
-                nc.scalar.activation(out=sq[:, t0 : t0 + per_bank, :], in_=acc[:], func=ACT.Square)
-            mode = RATE_ON[b][c]
-            sq_r = sq
-            halves = [(0, 2), (2, 4)] if mode == "B" else [(0, 4)]
-            for lo, hi in halves:
-                nc.scalar.activation(out=inv[:, lo:hi, :], in_=sq[:, lo:hi, :], func=ACT.Abs_reciprocal_sqrt, bias=1.0)
-            if mode != "B":
-                nc.scalar.activation(out=inv[:], in_=inv[:], func=ACT.Square)
-            for t in range(4):
-                r_col = rate_t[:, b, t : t + 1]
-                if mode == "B":
-                    nc.vector.scalar_tensor_tensor(inv[:, t, :], inv[:, t, :], r_col, inv[:, t, :], MULT, MULT)
-                elif mode == "S":
-                    nc.scalar.activation(out=inv[:, t, :], in_=inv[:, t, :], func=ACT.Copy, scale=r_col)
-                elif mode == "V":
-                    nc.vector.tensor_scalar(sq_r[:, t, :], sq[:, t, :], r_col, None, MULT)
-                else:
-                    nc.gpsimd.tensor_scalar(sq_r[:, t, :], sq[:, t, :], r_col, 0.0, MULT, ADD)
-            fin = nc.gpsimd if FIN[b][c] == "G" else nc.vector
-            walk = "p c i t" if FIN[b][c] == "G" else "p c t i"
-            parts = GSPLIT if FIN[b][c] == "G" else 1
-            for i in range(parts):
-                part = slice(i * w // 4 // parts, (i + 1) * w // 4 // parts)
-                fin.tensor_tensor(
-                    h_bf[:].rearrange("p (c i t) -> " + walk, i=4, t=4)[:, part],
-                    sq_r[:].rearrange("p t (c i) -> " + walk, i=4)[:, part],
-                    inv[:].rearrange("p t (c i) -> " + walk, i=4)[:, part],
-                    MULT,
+                nc.scalar.activation(out=square[:, t0 : t0 + per_bank, :], in_=bank[:], func=ACT.Square)
+            how = RATE_BY[b][c]
+            step = per_bank if how == "vector_both" else PACK
+            for t0 in range(0, PACK, step):
+                nc.scalar.activation(
+                    out=factor[:, t0 : t0 + step, :],
+                    in_=square[:, t0 : t0 + step, :],
+                    func=ACT.Abs_reciprocal_sqrt,
+                    bias=one[:],
                 )
-            nc.vector.quantize_mx(out=h_q[c][b][:].bitcast(FP8X4), scales=h_s[c][b][:], in_=h_bf[:])
+            if how != "vector_both":
+                nc.scalar.activation(out=factor[:], in_=factor[:], func=ACT.Square)
+            for t in range(PACK):
+                rate_col = rate_t[:, b, t : t + 1]
+                if how == "vector_both":
+                    nc.vector.scalar_tensor_tensor(factor[:, t, :], factor[:, t, :], rate_col, factor[:, t, :], MULT, MULT)
+                elif how == "vector_rate":
+                    nc.vector.tensor_scalar(square[:, t, :], square[:, t, :], rate_col, None, MULT)
+                else:
+                    nc.scalar.activation(out=factor[:, t, :], in_=factor[:, t, :], func=ACT.Copy, scale=rate_col)
+            nc.vector.tensor_tensor(
+                h_bf[:].rearrange("p (c i t) -> p c t i", i=RUN, t=PACK),
+                square[:].rearrange("p t (c i) -> p c t i", i=RUN),
+                factor[:].rearrange("p t (c i) -> p c t i", i=RUN),
+                MULT,
+            )
+            nc.vector.quantize_mx(out=h_q[b][c][:].bitcast(FP8X4), scales=h_s[b][c][:], in_=h_bf[:])
 
-        y_sb = {}
-        done = []
+        products_done = []
 
-        def product(n, c):
-            w = CHUNKS[c]
-            width = 512 if w == 512 else 128
-            g, n0 = n // 2, P * (n % 2)
-            mine = turn("y")
-            acc = y_banks[mine % len(y_banks)][:, 0:w]
-            for j0 in range(0, w, width):
-                cols = slice(j0, j0 + width)
-                for b in range(2):
+        def product_and_scatter(n, c):
+            bank = y_banks[len(products_done) % Y_BANKS]
+            products_done.append(n)
+            half, n0 = divmod(P * n, HALF)
+            for j0 in range(0, CHUNK, Y_WIDTH):
+                cols = slice(j0, j0 + Y_WIDTH)
+                for b in both:
                     nc.tensor.matmul_mx(
-                        out=acc[:, cols],
+                        out=bank[:, cols],
                         lhsT=wt_w[:, b, 2 * P * n : 2 * P * (n + 1)].bitcast(FP4X4),
                         lhsT_scale=wt_s[:, b, P * n : P * (n + 1)],
-                        rhs=h_q[c][b][:, cols].bitcast(FP8X4),
-                        rhs_scale=h_s[c][b][:, cols],
+                        rhs=h_q[b][c][:, cols].bitcast(FP8X4),
+                        rhs_scale=h_s[b][c][:, cols],
                         start=(b == 0),
                         stop=False,
                     )
-                for a in range(2):
+                for g in both:
+                    words, scales = table_operand(g, slice(CHUNK * c + j0, CHUNK * c + j0 + Y_WIDTH))
                     nc.tensor.matmul_mx(
-                        out=acc[:, cols],
-                        lhsT=wd_q[g][:, a, n0 : n0 + P].bitcast(FP8X4),
-                        lhsT_scale=wd_s[g][:, a, n0 : n0 + P],
-                        rhs=v_all[a][:, starts[c] + j0 : starts[c] + j0 + width].bitcast(FP8X4),
-                        rhs_scale=vs_all[4 * a : P, starts[c] + j0 : starts[c] + j0 + width],
+                        out=bank[:, cols],
+                        lhsT=wd_q[half][:, g, n0 : n0 + P].bitcast(FP8X4),
+                        lhsT_scale=wd_s[half][:, g, n0 : n0 + P],
+                        rhs=words,
+                        rhs_scale=scales,
                         start=False,
-                        stop=(a == 1),
+                        stop=(g == PASSES - 1),
                     )
-            y = y_ring[mine % len(y_ring)][:, 0:w]
-            source = GATE.get("y%d%d" % (n, c))
-            if source is not None:
-                place = turns.get(source, 0)
-                turns[source] = place + 1
-                y = rooms["slot_" + source][:, place * w : (place + 1) * w]
-            if YMUL[c] == "V":
-                nc.vector.tensor_tensor(y[:], acc[:], wgo_cols(c), MULT)
-            else:
-                nc.scalar.activation(out=y[:], in_=acc[:], func=ACT.Copy)
-            if YMUL[c] == "G":
-                nc.gpsimd.tensor_tensor(y[:], y[:], wgo_cols(c), MULT)
-            y_sb[(n, c)] = y
-
-        def scatter(n, c):
-            window = cache[n][:].indirect(entries(idx2, c))
-            if YMUL[c] == "F":
-                nc.vector.tensor_tensor(window, y_sb[(n, c)][:], wgo_cols(c), MULT)
-            else:
-                nc.vector.tensor_copy(window, y_sb[(n, c)][:])
-            done.append(n)
-            if len([m for m in done if m == n]) == len(CHUNKS):
+            nc.scalar.copy(out=y_sb[n][c][:], in_=bank[:])
+            nc.vector.tensor_tensor(
+                cache[n][:].indirect(idx2[:, LIST_COLS * c : LIST_COLS * (c + 1)]),
+                y_sb[n][c][:],
+                wgo_t[:, CHUNK * c : CHUNK * (c + 1)],
+                MULT,
+            )
+            if len([m for m in products_done if m == n]) == CHUNKS:
                 nc.sync.dma_start(out=out[P * n : P * (n + 1), :], in_=cache[n][:])
 
-        steps = {
-            "ga": gather_all_words, "gb": gather_all_scales, "gw": gather_words, "gs": gather_scales, "cr": cast_wr, "qr": quant_wr, "cd": cast_wd, "qd": quant_wd,
-            "u": unit, "y": product, "s": scatter,
-        }
-        for step in ORDER:
-            steps[step[0]](*step[1:])
-            key = step[0] + "".join([str(i) for i in step[1:]])
-            for name, pieces in LOADS:
-                if GATE.get(group_of(name)) == key:
-                    load(name, pieces)
+        for g in both:
+            nc.vector.tensor_copy(v_w[g][:], tab_w[g][:].bitcast(U32).indirect(idx[:]))
+        nc.vector.tensor_copy(v_s[:], tab_s[:].bitcast(U8).indirect(idx[:]))
+        for b in both:
+            for g in both:
+                cast_wr(b, g)
+            for g in both:
+                quantise_wr(b, g)
+
+        hill(0, 0)
+        hill(0, 1)
+        cast_wd(0)
+        hill(1, 0)
+        hill(1, 1)
+        quantise_wd(0)
+        hill(0, 2)
+        cast_wd(1)
+        quantise_wd(1)
+
+        order = [(n, c) for c in range(CHUNKS) for n in range(ROW_TILES)]
+        held_back = (ROW_TILES - 1, CHUNKS - 2)
+        order.remove(held_back)
+        order.append(held_back)
+        remaining = [(0, 3), (1, 2), (1, 3)]
+        for place, (n, c) in enumerate(order):
+            product_and_scatter(n, c)
+            if place % 2 == 1 and place // 2 < len(remaining):
+                hill(*remaining[place // 2])

@@ -30,17 +30,15 @@ HALF = N // 2
 RUN = 4
 A_BANKS = 4
 Y_BANKS = 4
-HILL_SLOTS = 3
+HILL_SLOTS = 4
 
-RATE_BY = [
-    ["vector_both", "vector_rate", "scalar", "scalar"],
-    ["vector_both", "vector_both", "scalar", "scalar"],
-]
-WR_CAST_BY = [
-    [["scalar"], ["scalar", "vector"]],
-    [["scalar", "vector"], ["vector", "vector"]],
-]
-WD_CAST_BY = [["vector", "vector"], ["scalar", "vector"]]
+RATE_BY = {(0, 0): 'both', (0, 1): 'both', (1, 0): 'vrate', (1, 1): 'vrate', (0, 2): 'scalar', (1, 2): 'scalar', (0, 3): 'scalar', (1, 3): 'scalar'}
+WR_CAST_BY = [[['vector', 'scalar'], ['scalar', 'vector']], [['vector', 'vector'], ['vector', 'vector']]]
+WD_CAST_BY = [['vector', 'vector'], ['scalar', 'scalar']]
+LOADS = ['idx', 'tw0', 'ts', 'tw1', 'wr00', 'wr01', 'wr10', 'wr11', 'rate', 'wd', 'wt', 'idx2', 'wgo']
+SPLIT = []
+STEPS = ['g0:0:1024', 'gs:0:1024', 'g1:0:1024', 'c00', 'c01', 'q00', 'q01', 'c10', 'c11', 'q10', 'q11', 'a00', 'r00', 'f00', 'm00', 'z00', 'd0', 'e0', 'a01', 'r01', 'f01', 'm01', 'z01', 'a10', 'r10', 'f10', 'm10', 'z10', 'p00', 's00', 'p10', 's10', 'a11', 'r11', 'f11', 'm11', 'z11', 'd1', 'e1', 'a02', 'r02', 'f02', 'm02', 'z02', 'p20', 's20', 'a12', 'r12', 'f12', 'm12', 'z12', 'p30', 's30', 'p01', 's01', 'p11', 's11', 'a03', 'r03', 'f03', 'm03', 'z03', 'p21', 's21', 'p31', 's31', 'p02', 's02', 'a13', 'r13', 'f13', 'm13', 'z13', 'p12', 's12', 'p22', 's22', 'p03', 's03', 'p13', 's13', 'p23', 's23', 'p33', 's33', 'p32', 's32']
+LATE = [(1, 2)]
 
 
 def tile_list_gene_regulation_derivatives_kernel(
@@ -98,30 +96,42 @@ def tile_list_gene_regulation_derivatives_kernel(
         def rows_of_pass(weight, g):
             return weight[PASS * g : PASS * (g + 1), :].rearrange("(p j) c -> p j c", j=PACK)
 
-        nc.scalar.dma_start(out=rate_t[:], in_=rate.rearrange("(b p t) -> p b t", b=PASSES, t=PACK))
-        nc.sync.dma_start(idx[:], offs)
-        for g in both:
-            nc.sync.dma_start(out=tab_w[g][:], in_=tab_words[g].rearrange("p t i -> p (t i)").bitcast(I32))
-        for q in range(4):
-            nc.sync.dma_start(out=tab_s[32 * q : 32 * q + 8, :], in_=tab_scales[:, 4 * q : 4 * q + 4, :].bitcast(I32))
-        for b in both:
-            for g in both:
-                width = PASS // 2 if (b, g) == (PASSES - 1, PASSES - 1) else PASS
+        def load(what):
+            if what == "idx":
+                nc.sync.dma_start(idx[:], offs)
+            elif what == "idx2":
+                nc.sync.dma_start(idx2[:], offs2)
+            elif what == "rate":
+                nc.sync.dma_start(out=rate_t[:], in_=rate.rearrange("(b p t) -> p b t", b=PASSES, t=PACK))
+            elif what == "wgo":
+                nc.sync.dma_start(out=wgo_t[:], in_=wgo)
+            elif what == "ts":
+                for q in range(4):
+                    nc.sync.dma_start(out=tab_s[32 * q : 32 * q + 8, :], in_=tab_scales[:, 4 * q : 4 * q + 4, :].bitcast(I32))
+            elif what.startswith("tw"):
+                g = int(what[2])
+                nc.sync.dma_start(out=tab_w[g][:], in_=tab_words[g].rearrange("p t i -> p (t i)").bitcast(I32))
+            elif what.startswith("wr"):
+                b, g = int(what[2]), int(what[3])
+                width = PASS // 2 if what in SPLIT else PASS
                 for c0 in range(0, PASS, width):
                     nc.sync.dma_start(
                         out=wr_raw[b][g][:, :, c0 : c0 + width],
                         in_=rows_of_pass(wr, g)[:, :, PASS * b + c0 : PASS * b + c0 + width],
                     )
-        for g in both:
-            nc.sync.dma_start(out=wd_raw[g][:], in_=rows_of_pass(wd, g))
-        for q in range(4):
-            nc.sync.dma_start(
-                out=wt_s[32 * q : 32 * q + 4, :, :].bitcast(I32),
-                in_=wt4_scales[:, 4 * q : 4 * q + 4, :].rearrange("g r n -> r g n").bitcast(I32),
-            )
-        nc.sync.dma_start(out=wt_w[:].bitcast(I32), in_=wt4_words.rearrange("g p c -> p g c").bitcast(I32))
-        nc.sync.dma_start(idx2[:], offs2)
-        nc.sync.dma_start(out=wgo_t[:], in_=wgo)
+            elif what == "wd":
+                for g in both:
+                    nc.sync.dma_start(out=wd_raw[g][:], in_=rows_of_pass(wd, g))
+            else:
+                for q in range(4):
+                    nc.sync.dma_start(
+                        out=wt_s[32 * q : 32 * q + 4, :, :].bitcast(I32),
+                        in_=wt4_scales[:, 4 * q : 4 * q + 4, :].rearrange("g r n -> r g n").bitcast(I32),
+                    )
+                nc.sync.dma_start(out=wt_w[:].bitcast(I32), in_=wt4_words.rearrange("g p c -> p g c").bitcast(I32))
+
+        for what in LOADS:
+            load(what)
 
         def cast(engine, dst, src):
             if engine == "vector":
@@ -155,13 +165,16 @@ def tile_list_gene_regulation_derivatives_kernel(
         def table_operand(g, cols):
             return v_w[g][:, cols].bitcast(FP8X4), v_s[4 * g : P, cols]
 
-        pieces_done = []
+        turns = {}
 
-        def hill(b, c):
-            turn = len(pieces_done)
-            pieces_done.append((b, c))
-            square, factor, h_bf = squares[turn % HILL_SLOTS], factors[turn % HILL_SLOTS], h_bfs[turn % HILL_SLOTS]
-            per_bank = BANK // CHUNK
+        def slot(b, c):
+            turn = turns.setdefault((b, c), len(turns))
+            return turn, squares[turn % HILL_SLOTS], factors[turn % HILL_SLOTS], h_bfs[turn % HILL_SLOTS]
+
+        per_bank = BANK // CHUNK
+
+        def first_product(b, c):
+            turn, square, factor, h_bf = slot(b, c)
             for t0 in range(0, PACK, per_bank):
                 bank = a_banks[(PACK * turn + t0) // per_bank % A_BANKS]
                 for t in range(t0, t0 + per_bank):
@@ -177,8 +190,10 @@ def tile_list_gene_regulation_derivatives_kernel(
                             stop=(g == PASSES - 1),
                         )
                 nc.scalar.activation(out=square[:, t0 : t0 + per_bank, :], in_=bank[:], func=ACT.Square)
-            how = RATE_BY[b][c]
-            step = per_bank if how == "vector_both" else PACK
+
+        def root(b, c):
+            turn, square, factor, h_bf = slot(b, c)
+            step = per_bank if RATE_BY[(b, c)] == "both" else PACK
             for t0 in range(0, PACK, step):
                 nc.scalar.activation(
                     out=factor[:, t0 : t0 + step, :],
@@ -186,42 +201,43 @@ def tile_list_gene_regulation_derivatives_kernel(
                     func=ACT.Abs_reciprocal_sqrt,
                     bias=one[:],
                 )
-            if how != "vector_both":
-                nc.scalar.activation(out=factor[:], in_=factor[:], func=ACT.Square)
+
+        def apply_rate(b, c):
+            turn, square, factor, h_bf = slot(b, c)
+            how = RATE_BY[(b, c)]
             for t in range(PACK):
                 rate_col = rate_t[:, b, t : t + 1]
-                if how == "vector_both":
+                if how == "both":
                     nc.vector.scalar_tensor_tensor(factor[:, t, :], factor[:, t, :], rate_col, factor[:, t, :], MULT, MULT)
-                elif how == "vector_rate":
+                elif how == "vrate":
                     nc.vector.tensor_scalar(square[:, t, :], square[:, t, :], rate_col, None, MULT)
                 else:
-                    nc.scalar.activation(out=factor[:, t, :], in_=factor[:, t, :], func=ACT.Copy, scale=rate_col)
+                    nc.scalar.activation(out=square[:, t, :], in_=square[:, t, :], func=ACT.Copy, scale=rate_col)
+            if how != "both":
+                nc.scalar.activation(out=factor[:], in_=factor[:], func=ACT.Square)
+
+        def multiply(b, c):
+            turn, square, factor, h_bf = slot(b, c)
             nc.vector.tensor_tensor(
                 h_bf[:].rearrange("p (c i t) -> p c t i", i=RUN, t=PACK),
                 square[:].rearrange("p t (c i) -> p c t i", i=RUN),
                 factor[:].rearrange("p t (c i) -> p c t i", i=RUN),
                 MULT,
             )
+
+        def quantise_h(b, c):
+            turn, square, factor, h_bf = slot(b, c)
             nc.vector.quantize_mx(out=h_q[b][c][:].bitcast(FP8X4), scales=h_s[b][c][:], in_=h_bf[:])
 
         products_done = []
+        scatters_done = []
 
-        def product_and_scatter(n, c):
+        def product(n, c):
             bank = y_banks[len(products_done) % Y_BANKS]
             products_done.append(n)
             half, n0 = divmod(P * n, HALF)
             for j0 in range(0, CHUNK, Y_WIDTH):
                 cols = slice(j0, j0 + Y_WIDTH)
-                for b in both:
-                    nc.tensor.matmul_mx(
-                        out=bank[:, cols],
-                        lhsT=wt_w[:, b, 2 * P * n : 2 * P * (n + 1)].bitcast(FP4X4),
-                        lhsT_scale=wt_s[:, b, P * n : P * (n + 1)],
-                        rhs=h_q[b][c][:, cols].bitcast(FP8X4),
-                        rhs_scale=h_s[b][c][:, cols],
-                        start=(b == 0),
-                        stop=False,
-                    )
                 for g in both:
                     words, scales = table_operand(g, slice(CHUNK * c + j0, CHUNK * c + j0 + Y_WIDTH))
                     nc.tensor.matmul_mx(
@@ -230,44 +246,53 @@ def tile_list_gene_regulation_derivatives_kernel(
                         lhsT_scale=wd_s[half][:, g, n0 : n0 + P],
                         rhs=words,
                         rhs_scale=scales,
-                        start=False,
-                        stop=(g == PASSES - 1),
+                        start=(g == 0),
+                        stop=False,
                     )
+                for b in both:
+                    nc.tensor.matmul_mx(
+                        out=bank[:, cols],
+                        lhsT=wt_w[:, b, 2 * P * n : 2 * P * (n + 1)].bitcast(FP4X4),
+                        lhsT_scale=wt_s[:, b, P * n : P * (n + 1)],
+                        rhs=h_q[b][c][:, cols].bitcast(FP8X4),
+                        rhs_scale=h_s[b][c][:, cols],
+                        start=False,
+                        stop=(b == PASSES - 1),
+                    )
+            if (n, c) in LATE:
+                y_sb[n][c] = squares[(len(RATE_BY) - 1) % HILL_SLOTS][:, LATE.index((n, c)), :]
             nc.scalar.copy(out=y_sb[n][c][:], in_=bank[:])
+
+        def scatter(n, c):
+            scatters_done.append(n)
             nc.vector.tensor_tensor(
                 cache[n][:].indirect(idx2[:, LIST_COLS * c : LIST_COLS * (c + 1)]),
                 y_sb[n][c][:],
                 wgo_t[:, CHUNK * c : CHUNK * (c + 1)],
                 MULT,
             )
-            if len([m for m in products_done if m == n]) == CHUNKS:
+            if len([m for m in scatters_done if m == n]) == CHUNKS:
                 nc.sync.dma_start(out=out[P * n : P * (n + 1), :], in_=cache[n][:])
 
-        for g in both:
-            nc.vector.tensor_copy(v_w[g][:], tab_w[g][:].bitcast(U32).indirect(idx[:]))
-        nc.vector.tensor_copy(v_s[:], tab_s[:].bitcast(U8).indirect(idx[:]))
-        for b in both:
-            for g in both:
-                cast_wr(b, g)
-            for g in both:
-                quantise_wr(b, g)
+        def gather(dst, window, cuts):
+            for j0, j1 in zip(cuts[:-1], cuts[1:]):
+                nc.vector.tensor_copy(dst[:, j0:j1], window.indirect(idx[:, j0 // 16 : j1 // 16]))
 
-        hill(0, 0)
-        hill(0, 1)
-        cast_wd(0)
-        hill(1, 0)
-        hill(1, 1)
-        quantise_wd(0)
-        hill(0, 2)
-        cast_wd(1)
-        quantise_wd(1)
-
-        order = [(n, c) for c in range(CHUNKS) for n in range(ROW_TILES)]
-        held_back = (ROW_TILES - 1, CHUNKS - 2)
-        order.remove(held_back)
-        order.append(held_back)
-        remaining = [(0, 3), (1, 2), (1, 3)]
-        for place, (n, c) in enumerate(order):
-            product_and_scatter(n, c)
-            if place % 2 == 1 and place // 2 < len(remaining):
-                hill(*remaining[place // 2])
+        for step in STEPS:
+            kind = step[0]
+            if kind == "g":
+                which, j0, j1 = step.split(":")
+                if which == "gs":
+                    gather(v_s, tab_s[:].bitcast(U8), [int(j0), int(j1)])
+                else:
+                    gather(v_w[int(which[1])], tab_w[int(which[1])][:].bitcast(U32), [int(j0), int(j1)])
+            elif kind == "c":
+                cast_wr(int(step[1]), int(step[2]))
+            elif kind == "q":
+                quantise_wr(int(step[1]), int(step[2]))
+            elif kind == "d":
+                cast_wd(int(step[1]))
+            elif kind == "e":
+                quantise_wd(int(step[1]))
+            else:
+                {"a": first_product, "r": root, "f": apply_rate, "m": multiply, "z": quantise_h, "p": product, "s": scatter}[kind](int(step[1]), int(step[2]))

@@ -28,17 +28,20 @@ BANK = 512
 Y_WIDTH = 128
 HALF = N // 2
 RUN = 4
-A_BANKS = 4
-Y_BANKS = 4
-HILL_SLOTS = 4
+A_BANKS = 6
+Y_BANKS = 2
+HILL_SLOTS = 3
 
-RATE_BY = {(0, 0): 'both', (0, 1): 'both', (1, 0): 'vrate', (1, 1): 'vrate', (0, 2): 'scalar', (1, 2): 'scalar', (0, 3): 'scalar', (1, 3): 'scalar'}
-WR_CAST_BY = [[['vector', 'scalar'], ['scalar', 'vector']], [['vector', 'vector'], ['vector', 'vector']]]
-WD_CAST_BY = [['vector', 'vector'], ['scalar', 'scalar']]
-LOADS = ['idx', 'tw0', 'ts', 'tw1', 'wr00', 'wr01', 'wr10', 'wr11', 'rate', 'wd', 'wt', 'idx2', 'wgo']
+RATE_BY = {(0, 0): 'both', (1, 0): 'vrate', (0, 1): 'both', (1, 1): 'both', (0, 2): 'scalar', (1, 2): 'scalar', (0, 3): 'scalar', (1, 3): 'scalar'}
+WR_CAST_BY = [[['scalar', 'scalar'], ['vector', 'scalar']], [['vector'], ['vector', 'vector']]]
+WD_CAST_BY = [['scalar', 'vector'], ['vector', 'scalar']]
+LOADS = ['idx', 'tw0', 'ts', 'tw1', 'wr00', 'wr01', 'wr10', 'wr11', 'rate', 'wd', 'wts', 'wt', 'idx2', 'wgo']
 SPLIT = []
-STEPS = ['g0:0:1024', 'gs:0:1024', 'g1:0:1024', 'c00', 'c01', 'q00', 'q01', 'c10', 'c11', 'q10', 'q11', 'a00', 'r00', 'f00', 'm00', 'z00', 'd0', 'e0', 'a01', 'r01', 'f01', 'm01', 'z01', 'a10', 'r10', 'f10', 'm10', 'z10', 'p00', 's00', 'p10', 's10', 'a11', 'r11', 'f11', 'm11', 'z11', 'd1', 'e1', 'a02', 'r02', 'f02', 'm02', 'z02', 'p20', 's20', 'a12', 'r12', 'f12', 'm12', 'z12', 'p30', 's30', 'p01', 's01', 'p11', 's11', 'a03', 'r03', 'f03', 'm03', 'z03', 'p21', 's21', 'p31', 's31', 'p02', 's02', 'a13', 'r13', 'f13', 'm13', 'z13', 'p12', 's12', 'p22', 's22', 'p03', 's03', 'p13', 's13', 'p23', 's23', 'p33', 's33', 'p32', 's32']
-LATE = [(1, 2)]
+STEPS = ['g0:0:1024', 'gs:0:1024', 'g1:0:1024', 'c00', 'c01', 'q00', 'q01', 'c10', 'c11', 'q10', 'q11', 'a00', 'r00', 'f00', 'm00', 'z00', 'd0', 'e0', 'a10', 'r10', 'f10', 'm10', 'z10', 'a01', 'r01', 'f01', 'm01', 'z01', 'a11', 'r11', 'f11', 'm11', 'z11', 'p00', 's00', 'a02', 'r02', 'f02', 'm02', 'z02', 'd1', 'e1', 'p10', 's10', 'p20', 's20', 'p30', 's30', 'a12', 'r12', 'f12', 'm12', 'z12', 'p01', 's01', 'p11', 's11', 'a03', 'r03', 'f03', 'm03', 'z03', 'p21', 's21', 'a13', 'r13', 'f13', 'm13', 'z13', 'p31', 's31', 'p02', 's02', 'p12', 's12', 'p22', 's22', 'p03', 's03', 'p13', 's13', 'p23', 's23', 'p32', 's32', 'p33', 's33']
+LATE = []
+ON_SCALAR = []
+BY_PLANES = [(0, 0), (0, 1)]
+GATHER_CUTS = [[0, 1024], [0, 1024], [0, 1024]]
 
 
 def tile_list_gene_regulation_derivatives_kernel(
@@ -97,17 +100,18 @@ def tile_list_gene_regulation_derivatives_kernel(
             return weight[PASS * g : PASS * (g + 1), :].rearrange("(p j) c -> p j c", j=PACK)
 
         def load(what):
+            queue = nc.scalar if what in ON_SCALAR else nc.sync
             if what == "idx":
                 nc.sync.dma_start(idx[:], offs)
             elif what == "idx2":
                 nc.sync.dma_start(idx2[:], offs2)
             elif what == "rate":
-                nc.sync.dma_start(out=rate_t[:], in_=rate.rearrange("(b p t) -> p b t", b=PASSES, t=PACK))
+                queue.dma_start(out=rate_t[:], in_=rate.rearrange("(b p t) -> p b t", b=PASSES, t=PACK))
             elif what == "wgo":
                 nc.sync.dma_start(out=wgo_t[:], in_=wgo)
             elif what == "ts":
                 for q in range(4):
-                    nc.sync.dma_start(out=tab_s[32 * q : 32 * q + 8, :], in_=tab_scales[:, 4 * q : 4 * q + 4, :].bitcast(I32))
+                    queue.dma_start(out=tab_s[32 * q : 32 * q + 8, :], in_=tab_scales[:, 4 * q : 4 * q + 4, :].bitcast(I32))
             elif what.startswith("tw"):
                 g = int(what[2])
                 nc.sync.dma_start(out=tab_w[g][:], in_=tab_words[g].rearrange("p t i -> p (t i)").bitcast(I32))
@@ -122,13 +126,14 @@ def tile_list_gene_regulation_derivatives_kernel(
             elif what == "wd":
                 for g in both:
                     nc.sync.dma_start(out=wd_raw[g][:], in_=rows_of_pass(wd, g))
-            else:
+            elif what == "wts":
                 for q in range(4):
-                    nc.sync.dma_start(
+                    queue.dma_start(
                         out=wt_s[32 * q : 32 * q + 4, :, :].bitcast(I32),
                         in_=wt4_scales[:, 4 * q : 4 * q + 4, :].rearrange("g r n -> r g n").bitcast(I32),
                     )
-                nc.sync.dma_start(out=wt_w[:].bitcast(I32), in_=wt4_words.rearrange("g p c -> p g c").bitcast(I32))
+            else:
+                queue.dma_start(out=wt_w[:].bitcast(I32), in_=wt4_words.rearrange("g p c -> p g c").bitcast(I32))
 
         for what in LOADS:
             load(what)
@@ -142,12 +147,23 @@ def tile_list_gene_regulation_derivatives_kernel(
         def cast_wr(b, g):
             dst = wr_bf[b][g][:].rearrange("p (t m j) -> p m j t", t=PACK, j=PACK)
             src = wr_raw[b][g][:].rearrange("p j (m t) -> p m j t", t=PACK)
+            if (b, g) in BY_PLANES:
+                for i, engine in enumerate(WR_CAST_BY[b][g]):
+                    share = PACK // len(WR_CAST_BY[b][g])
+                    cast(engine, dst[:, :, :, i * share : (i + 1) * share], src[:, :, :, i * share : (i + 1) * share])
+                return
             share = P // len(WR_CAST_BY[b][g])
             for i, engine in enumerate(WR_CAST_BY[b][g]):
                 cast(engine, dst[:, i * share : (i + 1) * share], src[:, i * share : (i + 1) * share])
 
         def quantise_wr(b, g):
-            nc.vector.quantize_mx(out=wr_q[b][g][:].bitcast(FP8X4), scales=wr_s[b][g][:], in_=wr_bf[b][g][:])
+            width = PASS // 2 if (b, g) in BY_PLANES else PASS
+            for c0 in range(0, PASS, width):
+                nc.vector.quantize_mx(
+                    out=wr_q[b][g][:, c0 : c0 + width].bitcast(FP8X4),
+                    scales=wr_s[b][g][:, c0 : c0 + width],
+                    in_=wr_bf[b][g][:, PACK * c0 : PACK * (c0 + width)],
+                )
 
         def cast_wd(half):
             for g in both:
@@ -236,20 +252,20 @@ def tile_list_gene_regulation_derivatives_kernel(
             bank = y_banks[len(products_done) % Y_BANKS]
             products_done.append(n)
             half, n0 = divmod(P * n, HALF)
-            for j0 in range(0, CHUNK, Y_WIDTH):
-                cols = slice(j0, j0 + Y_WIDTH)
-                for g in both:
-                    words, scales = table_operand(g, slice(CHUNK * c + j0, CHUNK * c + j0 + Y_WIDTH))
-                    nc.tensor.matmul_mx(
-                        out=bank[:, cols],
-                        lhsT=wd_q[half][:, g, n0 : n0 + P].bitcast(FP8X4),
-                        lhsT_scale=wd_s[half][:, g, n0 : n0 + P],
-                        rhs=words,
-                        rhs_scale=scales,
-                        start=(g == 0),
-                        stop=False,
-                    )
-                for b in both:
+            for g in both:
+                words, scales = table_operand(g, slice(CHUNK * c, CHUNK * (c + 1)))
+                nc.tensor.matmul_mx(
+                    out=bank[:],
+                    lhsT=wd_q[half][:, g, n0 : n0 + P].bitcast(FP8X4),
+                    lhsT_scale=wd_s[half][:, g, n0 : n0 + P],
+                    rhs=words,
+                    rhs_scale=scales,
+                    start=(g == 0),
+                    stop=False,
+                )
+            for b in both:
+                for j0 in range(0, CHUNK, Y_WIDTH):
+                    cols = slice(j0, j0 + Y_WIDTH)
                     nc.tensor.matmul_mx(
                         out=bank[:, cols],
                         lhsT=wt_w[:, b, 2 * P * n : 2 * P * (n + 1)].bitcast(FP4X4),
@@ -257,7 +273,7 @@ def tile_list_gene_regulation_derivatives_kernel(
                         rhs=h_q[b][c][:, cols].bitcast(FP8X4),
                         rhs_scale=h_s[b][c][:, cols],
                         start=False,
-                        stop=(b == PASSES - 1),
+                        stop=(b == PASSES - 1 and j0 + Y_WIDTH == CHUNK),
                     )
             if (n, c) in LATE:
                 y_sb[n][c] = squares[(len(RATE_BY) - 1) % HILL_SLOTS][:, LATE.index((n, c)), :]

@@ -32,16 +32,9 @@ A_BANKS = 6
 Y_BANKS = 2
 HILL_SLOTS = 3
 
-RATE_BY = {(0, 0): 'both', (1, 0): 'vrate', (0, 1): 'both', (1, 1): 'both', (0, 2): 'scalar', (1, 2): 'scalar', (0, 3): 'scalar', (1, 3): 'scalar'}
-WR_CAST_BY = [[['scalar', 'scalar'], ['vector', 'scalar']], [['vector'], ['vector', 'vector']]]
-WD_CAST_BY = [['scalar', 'vector'], ['vector', 'scalar']]
-LOADS = ['idx', 'tw0', 'ts', 'tw1', 'wr00', 'wr01', 'wr10', 'wr11', 'rate', 'wd', 'wts', 'wt', 'idx2', 'wgo']
-SPLIT = []
-STEPS = ['g0:0:1024', 'gs:0:1024', 'g1:0:1024', 'c00', 'c01', 'q00', 'q01', 'c10', 'c11', 'q10', 'q11', 'a00', 'r00', 'f00', 'm00', 'z00', 'd0', 'e0', 'a10', 'r10', 'f10', 'm10', 'z10', 'a01', 'r01', 'f01', 'm01', 'z01', 'a11', 'r11', 'f11', 'm11', 'z11', 'p00', 's00', 'a02', 'r02', 'f02', 'm02', 'z02', 'd1', 'e1', 'p10', 's10', 'p20', 's20', 'p30', 's30', 'a12', 'r12', 'f12', 'm12', 'z12', 'p01', 's01', 'p11', 's11', 'a03', 'r03', 'f03', 'm03', 'z03', 'p21', 's21', 'a13', 'r13', 'f13', 'm13', 'z13', 'p31', 's31', 'p02', 's02', 'p12', 's12', 'p22', 's22', 'p03', 's03', 'p13', 's13', 'p23', 's23', 'p32', 's32', 'p33', 's33']
-LATE = []
-ON_SCALAR = []
-BY_PLANES = [(0, 0), (0, 1)]
-GATHER_CUTS = [[0, 1024], [0, 1024], [0, 1024]]
+VECTOR_RATE_CHUNKS = 2
+SHARED_PIECE = (1, 0)
+PRODUCTS_PER_PIECE = 2
 
 
 def tile_list_gene_regulation_derivatives_kernel(
@@ -99,44 +92,31 @@ def tile_list_gene_regulation_derivatives_kernel(
         def rows_of_pass(weight, g):
             return weight[PASS * g : PASS * (g + 1), :].rearrange("(p j) c -> p j c", j=PACK)
 
-        def load(what):
-            queue = nc.scalar if what in ON_SCALAR else nc.sync
-            if what == "idx":
-                nc.sync.dma_start(idx[:], offs)
-            elif what == "idx2":
-                nc.sync.dma_start(idx2[:], offs2)
-            elif what == "rate":
-                queue.dma_start(out=rate_t[:], in_=rate.rearrange("(b p t) -> p b t", b=PASSES, t=PACK))
-            elif what == "wgo":
-                nc.sync.dma_start(out=wgo_t[:], in_=wgo)
-            elif what == "ts":
-                for q in range(4):
-                    queue.dma_start(out=tab_s[32 * q : 32 * q + 8, :], in_=tab_scales[:, 4 * q : 4 * q + 4, :].bitcast(I32))
-            elif what.startswith("tw"):
-                g = int(what[2])
-                nc.sync.dma_start(out=tab_w[g][:], in_=tab_words[g].rearrange("p t i -> p (t i)").bitcast(I32))
-            elif what.startswith("wr"):
-                b, g = int(what[2]), int(what[3])
-                width = PASS // 2 if what in SPLIT else PASS
-                for c0 in range(0, PASS, width):
-                    nc.sync.dma_start(
-                        out=wr_raw[b][g][:, :, c0 : c0 + width],
-                        in_=rows_of_pass(wr, g)[:, :, PASS * b + c0 : PASS * b + c0 + width],
-                    )
-            elif what == "wd":
-                for g in both:
-                    nc.sync.dma_start(out=wd_raw[g][:], in_=rows_of_pass(wd, g))
-            elif what == "wts":
-                for q in range(4):
-                    queue.dma_start(
-                        out=wt_s[32 * q : 32 * q + 4, :, :].bitcast(I32),
-                        in_=wt4_scales[:, 4 * q : 4 * q + 4, :].rearrange("g r n -> r g n").bitcast(I32),
-                    )
-            else:
-                queue.dma_start(out=wt_w[:].bitcast(I32), in_=wt4_words.rearrange("g p c -> p g c").bitcast(I32))
+        def load_wr(b, g):
+            nc.sync.dma_start(out=wr_raw[b][g][:], in_=rows_of_pass(wr, g)[:, :, PASS * b : PASS * (b + 1)])
 
-        for what in LOADS:
-            load(what)
+        def load_words(g):
+            nc.sync.dma_start(out=tab_w[g][:], in_=tab_words[g].rearrange("p t i -> p (t i)").bitcast(I32))
+
+        nc.sync.dma_start(idx[:], offs)
+        load_words(0)
+        for q in range(4):
+            nc.sync.dma_start(out=tab_s[32 * q : 32 * q + 8, :], in_=tab_scales[:, 4 * q : 4 * q + 4, :].bitcast(I32))
+        load_words(1)
+        for b in both:
+            for g in both:
+                load_wr(b, g)
+        nc.sync.dma_start(out=rate_t[:], in_=rate.rearrange("(b p t) -> p b t", b=PASSES, t=PACK))
+        for g in both:
+            nc.sync.dma_start(out=wd_raw[g][:], in_=rows_of_pass(wd, g))
+        for q in range(4):
+            nc.sync.dma_start(
+                out=wt_s[32 * q : 32 * q + 4, :, :].bitcast(I32),
+                in_=wt4_scales[:, 4 * q : 4 * q + 4, :].rearrange("g r n -> r g n").bitcast(I32),
+            )
+        nc.sync.dma_start(out=wt_w[:].bitcast(I32), in_=wt4_words.rearrange("g p c -> p g c").bitcast(I32))
+        nc.sync.dma_start(idx2[:], offs2)
+        nc.sync.dma_start(out=wgo_t[:], in_=wgo)
 
         def cast(engine, dst, src):
             if engine == "vector":
@@ -144,20 +124,19 @@ def tile_list_gene_regulation_derivatives_kernel(
             else:
                 nc.scalar.copy(out=dst, in_=src)
 
-        def cast_wr(b, g):
+        def cast_wr(b, g, engines, by_planes):
             dst = wr_bf[b][g][:].rearrange("p (t m j) -> p m j t", t=PACK, j=PACK)
             src = wr_raw[b][g][:].rearrange("p j (m t) -> p m j t", t=PACK)
-            if (b, g) in BY_PLANES:
-                for i, engine in enumerate(WR_CAST_BY[b][g]):
-                    share = PACK // len(WR_CAST_BY[b][g])
-                    cast(engine, dst[:, :, :, i * share : (i + 1) * share], src[:, :, :, i * share : (i + 1) * share])
-                return
-            share = P // len(WR_CAST_BY[b][g])
-            for i, engine in enumerate(WR_CAST_BY[b][g]):
-                cast(engine, dst[:, i * share : (i + 1) * share], src[:, i * share : (i + 1) * share])
+            share = (PACK if by_planes else P) // len(engines)
+            for i, engine in enumerate(engines):
+                part = slice(i * share, (i + 1) * share)
+                if by_planes:
+                    cast(engine, dst[:, :, :, part], src[:, :, :, part])
+                else:
+                    pairs = "p m j (u t) -> p u m j t"
+                    cast(engine, dst[:, part].rearrange(pairs, u=2), src[:, part].rearrange(pairs, u=2))
 
-        def quantise_wr(b, g):
-            width = PASS // 2 if (b, g) in BY_PLANES else PASS
+        def quantise_wr(b, g, width):
             for c0 in range(0, PASS, width):
                 nc.vector.quantize_mx(
                     out=wr_q[b][g][:, c0 : c0 + width].bitcast(FP8X4),
@@ -169,7 +148,7 @@ def tile_list_gene_regulation_derivatives_kernel(
             for g in both:
                 dst = wd_bf[half][:, g, :].rearrange("p (c i j) -> p c j i", i=RUN, j=PACK)
                 src = wd_raw[g][:, :, HALF * half : HALF * (half + 1)].rearrange("p j (c i) -> p c j i", i=RUN)
-                cast(WD_CAST_BY[half][g], dst, src)
+                cast("scalar" if g == half else "vector", dst, src)
 
         def quantise_wd(half):
             nc.vector.quantize_mx(
@@ -181,16 +160,13 @@ def tile_list_gene_regulation_derivatives_kernel(
         def table_operand(g, cols):
             return v_w[g][:, cols].bitcast(FP8X4), v_s[4 * g : P, cols]
 
-        turns = {}
+        pieces_done = []
 
-        def slot(b, c):
-            turn = turns.setdefault((b, c), len(turns))
-            return turn, squares[turn % HILL_SLOTS], factors[turn % HILL_SLOTS], h_bfs[turn % HILL_SLOTS]
-
-        per_bank = BANK // CHUNK
-
-        def first_product(b, c):
-            turn, square, factor, h_bf = slot(b, c)
+        def hill(b, c):
+            turn = len(pieces_done)
+            pieces_done.append((b, c))
+            square, factor, h_bf = squares[turn % HILL_SLOTS], factors[turn % HILL_SLOTS], h_bfs[turn % HILL_SLOTS]
+            per_bank = BANK // CHUNK
             for t0 in range(0, PACK, per_bank):
                 bank = a_banks[(PACK * turn + t0) // per_bank % A_BANKS]
                 for t in range(t0, t0 + per_bank):
@@ -206,10 +182,9 @@ def tile_list_gene_regulation_derivatives_kernel(
                             stop=(g == PASSES - 1),
                         )
                 nc.scalar.activation(out=square[:, t0 : t0 + per_bank, :], in_=bank[:], func=ACT.Square)
-
-        def root(b, c):
-            turn, square, factor, h_bf = slot(b, c)
-            step = per_bank if RATE_BY[(b, c)] == "both" else PACK
+            shared = (b, c) == SHARED_PIECE
+            on_vector = c < VECTOR_RATE_CHUNKS and not shared
+            step = per_bank if on_vector else PACK
             for t0 in range(0, PACK, step):
                 nc.scalar.activation(
                     out=factor[:, t0 : t0 + step, :],
@@ -217,38 +192,27 @@ def tile_list_gene_regulation_derivatives_kernel(
                     func=ACT.Abs_reciprocal_sqrt,
                     bias=one[:],
                 )
-
-        def apply_rate(b, c):
-            turn, square, factor, h_bf = slot(b, c)
-            how = RATE_BY[(b, c)]
             for t in range(PACK):
                 rate_col = rate_t[:, b, t : t + 1]
-                if how == "both":
+                if on_vector:
                     nc.vector.scalar_tensor_tensor(factor[:, t, :], factor[:, t, :], rate_col, factor[:, t, :], MULT, MULT)
-                elif how == "vrate":
+                elif shared:
                     nc.vector.tensor_scalar(square[:, t, :], square[:, t, :], rate_col, None, MULT)
                 else:
                     nc.scalar.activation(out=square[:, t, :], in_=square[:, t, :], func=ACT.Copy, scale=rate_col)
-            if how != "both":
+            if not on_vector:
                 nc.scalar.activation(out=factor[:], in_=factor[:], func=ACT.Square)
-
-        def multiply(b, c):
-            turn, square, factor, h_bf = slot(b, c)
             nc.vector.tensor_tensor(
                 h_bf[:].rearrange("p (c i t) -> p c t i", i=RUN, t=PACK),
                 square[:].rearrange("p t (c i) -> p c t i", i=RUN),
                 factor[:].rearrange("p t (c i) -> p c t i", i=RUN),
                 MULT,
             )
-
-        def quantise_h(b, c):
-            turn, square, factor, h_bf = slot(b, c)
             nc.vector.quantize_mx(out=h_q[b][c][:].bitcast(FP8X4), scales=h_s[b][c][:], in_=h_bf[:])
 
         products_done = []
-        scatters_done = []
 
-        def product(n, c):
+        def product_and_scatter(n, c):
             bank = y_banks[len(products_done) % Y_BANKS]
             products_done.append(n)
             half, n0 = divmod(P * n, HALF)
@@ -275,40 +239,43 @@ def tile_list_gene_regulation_derivatives_kernel(
                         start=False,
                         stop=(b == PASSES - 1 and j0 + Y_WIDTH == CHUNK),
                     )
-            if (n, c) in LATE:
-                y_sb[n][c] = squares[(len(RATE_BY) - 1) % HILL_SLOTS][:, LATE.index((n, c)), :]
             nc.scalar.copy(out=y_sb[n][c][:], in_=bank[:])
-
-        def scatter(n, c):
-            scatters_done.append(n)
             nc.vector.tensor_tensor(
                 cache[n][:].indirect(idx2[:, LIST_COLS * c : LIST_COLS * (c + 1)]),
                 y_sb[n][c][:],
                 wgo_t[:, CHUNK * c : CHUNK * (c + 1)],
                 MULT,
             )
-            if len([m for m in scatters_done if m == n]) == CHUNKS:
+            if len([m for m in products_done if m == n]) == CHUNKS:
                 nc.sync.dma_start(out=out[P * n : P * (n + 1), :], in_=cache[n][:])
 
-        def gather(dst, window, cuts):
-            for j0, j1 in zip(cuts[:-1], cuts[1:]):
-                nc.vector.tensor_copy(dst[:, j0:j1], window.indirect(idx[:, j0 // 16 : j1 // 16]))
+        nc.vector.tensor_copy(v_w[0][:], tab_w[0][:].bitcast(U32).indirect(idx[:]))
+        nc.vector.tensor_copy(v_s[:], tab_s[:].bitcast(U8).indirect(idx[:]))
+        nc.vector.tensor_copy(v_w[1][:], tab_w[1][:].bitcast(U32).indirect(idx[:]))
+        cast_wr(0, 0, ["scalar", "scalar"], True)
+        cast_wr(0, 1, ["vector", "scalar"], True)
+        for g in both:
+            quantise_wr(0, g, PASS // 2)
+        cast_wr(1, 0, ["vector"], False)
+        cast_wr(1, 1, ["vector", "vector"], False)
+        for g in both:
+            quantise_wr(1, g, PASS)
 
-        for step in STEPS:
-            kind = step[0]
-            if kind == "g":
-                which, j0, j1 = step.split(":")
-                if which == "gs":
-                    gather(v_s, tab_s[:].bitcast(U8), [int(j0), int(j1)])
-                else:
-                    gather(v_w[int(which[1])], tab_w[int(which[1])][:].bitcast(U32), [int(j0), int(j1)])
-            elif kind == "c":
-                cast_wr(int(step[1]), int(step[2]))
-            elif kind == "q":
-                quantise_wr(int(step[1]), int(step[2]))
-            elif kind == "d":
-                cast_wd(int(step[1]))
-            elif kind == "e":
-                quantise_wd(int(step[1]))
-            else:
-                {"a": first_product, "r": root, "f": apply_rate, "m": multiply, "z": quantise_h, "p": product, "s": scatter}[kind](int(step[1]), int(step[2]))
+        waiting = [(n, c) for c in range(CHUNKS) for n in range(ROW_TILES)]
+        held_back = (ROW_TILES - 1, CHUNKS - 2)
+        waiting.remove(held_back)
+        waiting.insert(len(waiting) - 1, held_back)
+        pieces = [(b, c) for c in range(CHUNKS) for b in both]
+        first_with_products = PASSES * VECTOR_RATE_CHUNKS - 1
+        for turn, (b, c) in enumerate(pieces):
+            hill(b, c)
+            if turn in (0, first_with_products):
+                half = 0 if turn == 0 else 1
+                cast_wd(half)
+                quantise_wd(half)
+            if turn >= first_with_products:
+                count = PRODUCTS_PER_PIECE - (1 if turn == len(pieces) - 2 else 0)
+                for place in range(count):
+                    product_and_scatter(*waiting.pop(0))
+        for n, c in waiting:
+            product_and_scatter(n, c)

@@ -35,6 +35,7 @@ HILL_SLOTS = 3
 VECTOR_RATE_CHUNKS = 2
 SHARED_PIECE = (1, 0)
 PRODUCTS_PER_PIECE = 2
+LATE_PRODUCTS = 1
 
 
 def tile_list_gene_regulation_derivatives_kernel(
@@ -277,5 +278,8 @@ def tile_list_gene_regulation_derivatives_kernel(
                 count = PRODUCTS_PER_PIECE - (1 if turn == len(pieces) - 2 else 0)
                 for place in range(count):
                     product_and_scatter(*waiting.pop(0))
+        last_square = squares[(len(pieces) - 1) % HILL_SLOTS]
+        for place in range(LATE_PRODUCTS):
+            y_sb[ROW_TILES - 2 - place][CHUNKS - 2] = last_square[:, place, :]
         for n, c in waiting:
             product_and_scatter(n, c)

@@ -80,6 +80,10 @@ def tile_list_gene_regulation_derivatives_kernel(
         h_q = [[held("h_q%d%d" % (b, c), [P, CHUNK], U32) for c in range(CHUNKS)] for b in both]
         h_s = [[held("h_s%d%d" % (b, c), [P, CHUNK], U8) for c in range(CHUNKS)] for b in both]
         y_sb = [[held("y%d%d" % (n, c), [P, CHUNK], F32) for c in range(CHUNKS)] for n in range(ROW_TILES)]
+        held_back = (ROW_TILES - 1, CHUNKS - 2)
+        y_pair = held("y_pair", [P, 2 * CHUNK], F32)
+        for i in range(2):
+            y_sb[ROW_TILES - 1][CHUNKS - 2 + i] = y_pair[:, CHUNK * i : CHUNK * (i + 1)]
         cache = [held("cache%d" % n, [P, T2], F32) for n in range(ROW_TILES)]
 
         nc.vector.memset(one[:], 1.0)
@@ -241,10 +245,14 @@ def tile_list_gene_regulation_derivatives_kernel(
                         stop=(b == PASSES - 1 and j0 + Y_WIDTH == CHUNK),
                     )
             nc.scalar.copy(out=y_sb[n][c][:], in_=bank[:])
+            if (n, c) == held_back:
+                return
+            joined = (n, c - 1) == held_back
+            c0 = c - 1 if joined else c
             nc.vector.tensor_tensor(
-                cache[n][:].indirect(idx2[:, LIST_COLS * c : LIST_COLS * (c + 1)]),
-                y_sb[n][c][:],
-                wgo_t[:, CHUNK * c : CHUNK * (c + 1)],
+                cache[n][:].indirect(idx2[:, LIST_COLS * c0 : LIST_COLS * (c + 1)]),
+                y_pair[:] if joined else y_sb[n][c][:],
+                wgo_t[:, CHUNK * c0 : CHUNK * (c + 1)],
                 MULT,
             )
             if len([m for m in products_done if m == n]) == CHUNKS:
@@ -263,7 +271,6 @@ def tile_list_gene_regulation_derivatives_kernel(
             quantise_wr(1, g, PASS)
 
         waiting = [(n, c) for c in range(CHUNKS) for n in range(ROW_TILES)]
-        held_back = (ROW_TILES - 1, CHUNKS - 2)
         waiting.remove(held_back)
         waiting.insert(len(waiting) - 1, held_back)
         pieces = [(b, c) for c in range(CHUNKS) for b in both]

@@ -35,7 +35,6 @@ HILL_SLOTS = 3
 VECTOR_RATE_CHUNKS = 2
 SHARED_PIECE = (1, 0)
 PRODUCTS_PER_PIECE = 2
-LATE_PRODUCTS = 1
 
 
 def tile_list_gene_regulation_derivatives_kernel(
@@ -79,11 +78,18 @@ def tile_list_gene_regulation_derivatives_kernel(
         h_bfs = [held("h_bf%d" % i, [P, PACK * CHUNK], BF16) for i in range(HILL_SLOTS)]
         h_q = [[held("h_q%d%d" % (b, c), [P, CHUNK], U32) for c in range(CHUNKS)] for b in both]
         h_s = [[held("h_s%d%d" % (b, c), [P, CHUNK], U8) for c in range(CHUNKS)] for b in both]
-        y_sb = [[held("y%d%d" % (n, c), [P, CHUNK], F32) for c in range(CHUNKS)] for n in range(ROW_TILES)]
         held_back = (ROW_TILES - 1, CHUNKS - 2)
+        filler = (ROW_TILES - 2, CHUNKS - 2)
         y_pair = held("y_pair", [P, 2 * CHUNK], F32)
-        for i in range(2):
-            y_sb[ROW_TILES - 1][CHUNKS - 2 + i] = y_pair[:, CHUNK * i : CHUNK * (i + 1)]
+        y_sb = {
+            held_back: y_pair[:, :CHUNK],
+            (ROW_TILES - 1, CHUNKS - 1): y_pair[:, CHUNK:],
+            filler: squares[(PASSES * CHUNKS - 1) % HILL_SLOTS][:, 0, :],
+        }
+        for n in range(ROW_TILES):
+            for c in range(CHUNKS):
+                if (n, c) not in y_sb:
+                    y_sb[(n, c)] = held("y%d%d" % (n, c), [P, CHUNK], F32)[:]
         cache = [held("cache%d" % n, [P, T2], F32) for n in range(ROW_TILES)]
 
         nc.vector.memset(one[:], 1.0)
@@ -107,10 +113,11 @@ def tile_list_gene_regulation_derivatives_kernel(
         load_words(0)
         for q in range(4):
             nc.sync.dma_start(out=tab_s[32 * q : 32 * q + 8, :], in_=tab_scales[:, 4 * q : 4 * q + 4, :].bitcast(I32))
+        for g in both:
+            load_wr(0, g)
         load_words(1)
-        for b in both:
-            for g in both:
-                load_wr(b, g)
+        for g in both:
+            load_wr(1, g)
         nc.sync.dma_start(out=rate_t[:], in_=rate.rearrange("(b p t) -> p b t", b=PASSES, t=PACK))
         for g in both:
             nc.sync.dma_start(out=wd_raw[g][:], in_=rows_of_pass(wd, g))
@@ -219,7 +226,7 @@ def tile_list_gene_regulation_derivatives_kernel(
 
         def product_and_scatter(n, c):
             bank = y_banks[len(products_done) % Y_BANKS]
-            products_done.append(n)
+            products_done.append((n, c))
             half, n0 = divmod(P * n, HALF)
             for g in both:
                 words, scales = table_operand(g, slice(CHUNK * c, CHUNK * (c + 1)))
@@ -244,27 +251,28 @@ def tile_list_gene_regulation_derivatives_kernel(
                         start=False,
                         stop=(b == PASSES - 1 and j0 + Y_WIDTH == CHUNK),
                     )
-            nc.scalar.copy(out=y_sb[n][c][:], in_=bank[:])
+            nc.scalar.copy(out=y_sb[(n, c)], in_=bank[:])
             if (n, c) == held_back:
                 return
             joined = (n, c - 1) == held_back
             c0 = c - 1 if joined else c
             nc.vector.tensor_tensor(
                 cache[n][:].indirect(idx2[:, LIST_COLS * c0 : LIST_COLS * (c + 1)]),
-                y_pair[:] if joined else y_sb[n][c][:],
+                y_pair[:] if joined else y_sb[(n, c)],
                 wgo_t[:, CHUNK * c0 : CHUNK * (c + 1)],
                 MULT,
             )
-            if len([m for m in products_done if m == n]) == CHUNKS:
+            if c == CHUNKS - 1:
                 nc.sync.dma_start(out=out[P * n : P * (n + 1), :], in_=cache[n][:])
 
         nc.vector.tensor_copy(v_w[0][:], tab_w[0][:].bitcast(U32).indirect(idx[:]))
         nc.vector.tensor_copy(v_s[:], tab_s[:].bitcast(U8).indirect(idx[:]))
-        nc.vector.tensor_copy(v_w[1][:], tab_w[1][:].bitcast(U32).indirect(idx[:]))
         cast_wr(0, 0, ["scalar", "scalar"], True)
         cast_wr(0, 1, ["vector", "scalar"], True)
         for g in both:
             quantise_wr(0, g, PASS // 2)
+        for j0, j1 in ((0, CHUNK), (CHUNK, S)):
+            nc.vector.tensor_copy(v_w[1][:, j0:j1], tab_w[1][:].bitcast(U32).indirect(idx[:, j0 // 16 : j1 // 16]))
         cast_wr(1, 0, ["vector"], False)
         cast_wr(1, 1, ["vector", "vector"], False)
         for g in both:
@@ -285,8 +293,5 @@ def tile_list_gene_regulation_derivatives_kernel(
                 count = PRODUCTS_PER_PIECE - (1 if turn == len(pieces) - 2 else 0)
                 for place in range(count):
                     product_and_scatter(*waiting.pop(0))
-        last_square = squares[(len(pieces) - 1) % HILL_SLOTS]
-        for place in range(LATE_PRODUCTS):
-            y_sb[ROW_TILES - 2 - place][CHUNKS - 2] = last_square[:, place, :]
         for n, c in waiting:
             product_and_scatter(n, c)

@@ -95,10 +95,12 @@ def tile_list_gene_regulation_derivatives_kernel(
         nc.vector.memset(one[:], 1.0)
         nc.scalar.activation(out=one[:], in_=one[:], func=ACT.Abs_reciprocal_sqrt)
         nc.scalar.activation(out=one[:], in_=one[:], func=ACT.Sign)
-        nc.vector.memset(tab_s[:], 0)
-        nc.vector.memset(wt_s[:].rearrange("p g n -> p (g n)").bitcast(I32), 0)
-        for n in range(ROW_TILES):
-            nc.vector.memset(cache[n][:], 0.0)
+        nc.gpsimd.memset(tab_s[:], 0)
+        for n in range(ROW_TILES // 2):
+            nc.vector.memset(cache[n][:, : T2 // 2 + 1], 0.0)
+            nc.vector.memset(cache[n][:, T2 // 2 + 1 :], 0.0)
+            nc.gpsimd.memset(cache[ROW_TILES // 2 + n][:], 0.0)
+        nc.gpsimd.memset(wt_s[:].rearrange("p g n -> p (g n)").bitcast(I32), 0)
 
         def rows_of_pass(weight, g):
             return weight[PASS * g : PASS * (g + 1), :].rearrange("(p j) c -> p j c", j=PACK)

@@ -35,6 +35,7 @@ HILL_SLOTS = 3
 VECTOR_RATE_CHUNKS = 2
 SHARED_PIECE = (1, 0)
 PRODUCTS_PER_PIECE = 2
+JOINED_TILES = 2
 
 
 def tile_list_gene_regulation_derivatives_kernel(
@@ -78,14 +79,13 @@ def tile_list_gene_regulation_derivatives_kernel(
         h_bfs = [held("h_bf%d" % i, [P, PACK * CHUNK], BF16) for i in range(HILL_SLOTS)]
         h_q = [[held("h_q%d%d" % (b, c), [P, CHUNK], U32) for c in range(CHUNKS)] for b in both]
         h_s = [[held("h_s%d%d" % (b, c), [P, CHUNK], U8) for c in range(CHUNKS)] for b in both]
-        held_back = (ROW_TILES - 1, CHUNKS - 2)
-        filler = (ROW_TILES - 2, CHUNKS - 2)
-        y_pair = held("y_pair", [P, 2 * CHUNK], F32)
-        y_sb = {
-            held_back: y_pair[:, :CHUNK],
-            (ROW_TILES - 1, CHUNKS - 1): y_pair[:, CHUNK:],
-            filler: squares[(PASSES * CHUNKS - 1) % HILL_SLOTS][:, 0, :],
-        }
+        joined_tiles = range(ROW_TILES - JOINED_TILES, ROW_TILES)
+        filler = (ROW_TILES - JOINED_TILES - 1, CHUNKS - 2)
+        y_pair = {n: held("y_pair%d" % n, [P, 2 * CHUNK], F32) for n in joined_tiles}
+        y_sb = {filler: squares[(PASSES * CHUNKS - 1) % HILL_SLOTS][:, 0, :]}
+        for n in joined_tiles:
+            y_sb[(n, CHUNKS - 2)] = y_pair[n][:, :CHUNK]
+            y_sb[(n, CHUNKS - 1)] = y_pair[n][:, CHUNK:]
         for n in range(ROW_TILES):
             for c in range(CHUNKS):
                 if (n, c) not in y_sb:
@@ -254,13 +254,13 @@ def tile_list_gene_regulation_derivatives_kernel(
                         stop=(b == PASSES - 1 and j0 + Y_WIDTH == CHUNK),
                     )
             nc.scalar.copy(out=y_sb[(n, c)], in_=bank[:])
-            if (n, c) == held_back:
+            if n in joined_tiles and c == CHUNKS - 2:
                 return
-            joined = (n, c - 1) == held_back
+            joined = n in joined_tiles and c == CHUNKS - 1
             c0 = c - 1 if joined else c
             nc.vector.tensor_tensor(
                 cache[n][:].indirect(idx2[:, LIST_COLS * c0 : LIST_COLS * (c + 1)]),
-                y_pair[:] if joined else y_sb[(n, c)],
+                y_pair[n][:] if joined else y_sb[(n, c)],
                 wgo_t[:, CHUNK * c0 : CHUNK * (c + 1)],
                 MULT,
             )
@@ -281,8 +281,9 @@ def tile_list_gene_regulation_derivatives_kernel(
             quantise_wr(1, g, PASS)
 
         waiting = [(n, c) for c in range(CHUNKS) for n in range(ROW_TILES)]
-        waiting.remove(held_back)
-        waiting.insert(len(waiting) - 1, held_back)
+        for n in joined_tiles:
+            waiting.remove((n, CHUNKS - 2))
+            waiting.insert(waiting.index((n, CHUNKS - 1)), (n, CHUNKS - 2))
         pieces = [(b, c) for c in range(CHUNKS) for b in both]
         first_with_products = PASSES * VECTOR_RATE_CHUNKS - 1
         for turn, (b, c) in enumerate(pieces):

@@ -96,10 +96,10 @@ def tile_list_gene_regulation_derivatives_kernel(
         nc.scalar.activation(out=one[:], in_=one[:], func=ACT.Abs_reciprocal_sqrt)
         nc.scalar.activation(out=one[:], in_=one[:], func=ACT.Sign)
         nc.gpsimd.memset(tab_s[:], 0)
-        for n in range(ROW_TILES // 2):
-            nc.vector.memset(cache[n][:, : T2 // 2 + 1], 0.0)
-            nc.vector.memset(cache[n][:, T2 // 2 + 1 :], 0.0)
-            nc.gpsimd.memset(cache[ROW_TILES // 2 + n][:], 0.0)
+        nc.vector.memset(cache[0][:, : T2 // 2 + 1], 0.0)
+        nc.vector.memset(cache[0][:, T2 // 2 + 1 :], 0.0)
+        for n in range(1, ROW_TILES):
+            nc.gpsimd.memset(cache[n][:], 0.0)
         nc.gpsimd.memset(wt_s[:].rearrange("p g n -> p (g n)").bitcast(I32), 0)
 
         def rows_of_pass(weight, g):
@@ -265,7 +265,11 @@ def tile_list_gene_regulation_derivatives_kernel(
                 MULT,
             )
             if c == CHUNKS - 1:
-                nc.sync.dma_start(out=out[P * n : P * (n + 1), :], in_=cache[n][:])
+                if n < ROW_TILES - 1:
+                    nc.sync.dma_start(out=out[P * n : P * (n + 1), :], in_=cache[n][:])
+                else:
+                    for queue, cols in ((nc.sync, slice(0, T2 // 2)), (nc.scalar, slice(T2 // 2, T2))):
+                        queue.dma_start(out=out[P * n : P * (n + 1), cols], in_=cache[n][:, cols])
 
         nc.vector.tensor_copy(v_w[0][:], tab_w[0][:].bitcast(U32).indirect(idx[:]))
         nc.vector.tensor_copy(v_s[:], tab_s[:].bitcast(U8).indirect(idx[:]))

@@ -33,9 +33,9 @@ Y_BANKS = 2
 HILL_SLOTS = 3
 
 VECTOR_RATE_CHUNKS = 2
-SHARED_PIECE = (1, 0)
+SHARED_PIECES = ((1, 0), (1, 1))
 PRODUCTS_PER_PIECE = 2
-JOINED_TILES = 2
+JOINED_TILES = 1
 
 
 def tile_list_gene_regulation_derivatives_kernel(
@@ -196,7 +196,7 @@ def tile_list_gene_regulation_derivatives_kernel(
                             stop=(g == PASSES - 1),
                         )
                 nc.scalar.activation(out=square[:, t0 : t0 + per_bank, :], in_=bank[:], func=ACT.Square)
-            shared = (b, c) == SHARED_PIECE
+            shared = (b, c) in SHARED_PIECES
             on_vector = c < VECTOR_RATE_CHUNKS and not shared
             step = per_bank if on_vector else PACK
             for t0 in range(0, PACK, step):
@@ -216,13 +216,20 @@ def tile_list_gene_regulation_derivatives_kernel(
                     nc.scalar.activation(out=square[:, t, :], in_=square[:, t, :], func=ACT.Copy, scale=rate_col)
             if not on_vector:
                 nc.scalar.activation(out=factor[:], in_=factor[:], func=ACT.Square)
-            nc.vector.tensor_tensor(
-                h_bf[:].rearrange("p (c i t) -> p c t i", i=RUN, t=PACK),
-                square[:].rearrange("p t (c i) -> p c t i", i=RUN),
-                factor[:].rearrange("p t (c i) -> p c t i", i=RUN),
-                MULT,
-            )
-            nc.vector.quantize_mx(out=h_q[b][c][:].bitcast(FP8X4), scales=h_s[b][c][:], in_=h_bf[:])
+            halves = [slice(j0, j0 + CHUNK // 2) for j0 in (0, CHUNK // 2)]
+            for cols in halves:
+                nc.vector.tensor_tensor(
+                    h_bf[:, PACK * cols.start : PACK * cols.stop].rearrange("p (c i t) -> p c t i", i=RUN, t=PACK),
+                    square[:, :, cols].rearrange("p t (c i) -> p c t i", i=RUN),
+                    factor[:, :, cols].rearrange("p t (c i) -> p c t i", i=RUN),
+                    MULT,
+                )
+            for cols in halves:
+                nc.vector.quantize_mx(
+                    out=h_q[b][c][:, cols].bitcast(FP8X4),
+                    scales=h_s[b][c][:, cols],
+                    in_=h_bf[:, PACK * cols.start : PACK * cols.stop],
+                )
 
         products_done = []
 
@@ -279,10 +286,9 @@ def tile_list_gene_regulation_derivatives_kernel(
             quantise_wr(0, g, PASS // 2)
         for j0, j1 in ((0, CHUNK), (CHUNK, S)):
             nc.vector.tensor_copy(v_w[1][:, j0:j1], tab_w[1][:].bitcast(U32).indirect(idx[:, j0 // 16 : j1 // 16]))
-        cast_wr(1, 0, ["vector"], False)
-        cast_wr(1, 1, ["vector", "vector"], False)
         for g in both:
-            quantise_wr(1, g, PASS)
+            cast_wr(1, g, ["vector", "vector"], True)
+            quantise_wr(1, g, PASS // 2)
 
         waiting = [(n, c) for c in range(CHUNKS) for n in range(ROW_TILES)]
         for n in joined_tiles:

@@ -82,7 +82,7 @@ def tile_list_gene_regulation_derivatives_kernel(
         joined_tiles = range(ROW_TILES - JOINED_TILES, ROW_TILES)
         filler = (ROW_TILES - JOINED_TILES - 1, CHUNKS - 2)
         y_pair = {n: held("y_pair%d" % n, [P, 2 * CHUNK], F32) for n in joined_tiles}
-        y_sb = {filler: squares[(PASSES * CHUNKS - 1) % HILL_SLOTS][:, 0, :]}
+        y_sb = {filler: factors[(PASSES * CHUNKS - 1) % HILL_SLOTS][:, 0, :]}
         for n in joined_tiles:
             y_sb[(n, CHUNKS - 2)] = y_pair[n][:, :CHUNK]
             y_sb[(n, CHUNKS - 1)] = y_pair[n][:, CHUNK:]
@@ -183,8 +183,8 @@ def tile_list_gene_regulation_derivatives_kernel(
             per_bank = BANK // CHUNK
             for t0 in range(0, PACK, per_bank):
                 bank = a_banks[(PACK * turn + t0) // per_bank % A_BANKS]
-                for t in range(t0, t0 + per_bank):
-                    for g in both:
+                for g in both:
+                    for t in range(t0, t0 + per_bank):
                         words, scales = table_operand(g, slice(CHUNK * c, CHUNK * (c + 1)))
                         nc.tensor.matmul_mx(
                             out=bank[:, t - t0, :],
@@ -192,8 +192,8 @@ def tile_list_gene_regulation_derivatives_kernel(
                             lhsT_scale=wr_s[b][g][:, P * t : P * (t + 1)],
                             rhs=words,
                             rhs_scale=scales,
-                            start=(g == 0),
-                            stop=(g == PASSES - 1),
+                            start=(g == 0 and t == t0),
+                            stop=(g == PASSES - 1 and t == t0 + per_bank - 1),
                         )
                 nc.scalar.activation(out=square[:, t0 : t0 + per_bank, :], in_=bank[:], func=ACT.Square)
             shared = (b, c) in SHARED_PIECES
@@ -206,22 +206,24 @@ def tile_list_gene_regulation_derivatives_kernel(
                     func=ACT.Abs_reciprocal_sqrt,
                     bias=one[:],
                 )
+            rated = square if c < VECTOR_RATE_CHUNKS else wr_raw[0][b][:, :, CHUNK * (c % 2) : CHUNK * (c % 2 + 1)]
+            second = wr_raw[1][1][:, :, CHUNK * c : CHUNK * (c + 1)] if on_vector else factor
             for t in range(PACK):
                 rate_col = rate_t[:, b, t : t + 1]
                 if on_vector:
-                    nc.vector.scalar_tensor_tensor(factor[:, t, :], factor[:, t, :], rate_col, factor[:, t, :], MULT, MULT)
+                    nc.vector.scalar_tensor_tensor(second[:, t, :], factor[:, t, :], rate_col, factor[:, t, :], MULT, MULT)
                 elif shared:
                     nc.vector.tensor_scalar(square[:, t, :], square[:, t, :], rate_col, None, MULT)
                 else:
-                    nc.scalar.activation(out=square[:, t, :], in_=square[:, t, :], func=ACT.Copy, scale=rate_col)
+                    nc.scalar.activation(out=rated[:, t, :], in_=square[:, t, :], func=ACT.Copy, scale=rate_col)
             if not on_vector:
                 nc.scalar.activation(out=factor[:], in_=factor[:], func=ACT.Square)
             halves = [slice(j0, j0 + CHUNK // 2) for j0 in (0, CHUNK // 2)]
             for cols in halves:
                 nc.vector.tensor_tensor(
                     h_bf[:, PACK * cols.start : PACK * cols.stop].rearrange("p (c i t) -> p c t i", i=RUN, t=PACK),
-                    square[:, :, cols].rearrange("p t (c i) -> p c t i", i=RUN),
-                    factor[:, :, cols].rearrange("p t (c i) -> p c t i", i=RUN),
+                    rated[:, :, cols].rearrange("p t (c i) -> p c t i", i=RUN),
+                    second[:, :, cols].rearrange("p t (c i) -> p c t i", i=RUN),
                     MULT,
                 )
             for cols in halves:
@@ -303,7 +305,7 @@ def tile_list_gene_regulation_derivatives_kernel(
                 cast_wd(half)
                 quantise_wd(half)
             if turn >= first_with_products:
-                count = PRODUCTS_PER_PIECE - (1 if turn == len(pieces) - 2 else 0)
+                count = PRODUCTS_PER_PIECE + (1 if turn in (5, 6) else 0)
                 for place in range(count):
                     product_and_scatter(*waiting.pop(0))
         for n, c in waiting:

@@ -25,7 +25,6 @@ CHUNK = 256
 CHUNKS = S // CHUNK
 LIST_COLS = CHUNK // 16
 BANK = 512
-Y_WIDTH = 128
 HALF = N // 2
 RUN = 4
 A_BANKS = 6
@@ -33,9 +32,7 @@ Y_BANKS = 2
 HILL_SLOTS = 3
 
 VECTOR_RATE_CHUNKS = 2
-SHARED_PIECES = ((1, 0), (1, 1))
-PRODUCTS_PER_PIECE = 2
-JOINED_TILES = 1
+PRODUCTS_BEHIND_PIECES = (2, 2, 3, 3)
 
 
 def tile_list_gene_regulation_derivatives_kernel(
@@ -79,13 +76,13 @@ def tile_list_gene_regulation_derivatives_kernel(
         h_bfs = [held("h_bf%d" % i, [P, PACK * CHUNK], BF16) for i in range(HILL_SLOTS)]
         h_q = [[held("h_q%d%d" % (b, c), [P, CHUNK], U32) for c in range(CHUNKS)] for b in both]
         h_s = [[held("h_s%d%d" % (b, c), [P, CHUNK], U8) for c in range(CHUNKS)] for b in both]
-        joined_tiles = range(ROW_TILES - JOINED_TILES, ROW_TILES)
-        filler = (ROW_TILES - JOINED_TILES - 1, CHUNKS - 2)
-        y_pair = {n: held("y_pair%d" % n, [P, 2 * CHUNK], F32) for n in joined_tiles}
-        y_sb = {filler: factors[(PASSES * CHUNKS - 1) % HILL_SLOTS][:, 0, :]}
-        for n in joined_tiles:
-            y_sb[(n, CHUNKS - 2)] = y_pair[n][:, :CHUNK]
-            y_sb[(n, CHUNKS - 1)] = y_pair[n][:, CHUNK:]
+        last_tile, last_chunk, last_turn = ROW_TILES - 1, CHUNKS - 1, PASSES * CHUNKS - 1
+        y_pair = held("y_pair", [P, 2 * CHUNK], F32)
+        y_sb = {
+            (last_tile - 1, last_chunk - 1): factors[last_turn % HILL_SLOTS][:, 0, :],
+            (last_tile, last_chunk - 1): y_pair[:, :CHUNK],
+            (last_tile, last_chunk): y_pair[:, CHUNK:],
+        }
         for n in range(ROW_TILES):
             for c in range(CHUNKS):
                 if (n, c) not in y_sb:
@@ -138,19 +135,15 @@ def tile_list_gene_regulation_derivatives_kernel(
             else:
                 nc.scalar.copy(out=dst, in_=src)
 
-        def cast_wr(b, g, engines, by_planes):
+        def cast_wr(b, g, engines):
             dst = wr_bf[b][g][:].rearrange("p (t m j) -> p m j t", t=PACK, j=PACK)
             src = wr_raw[b][g][:].rearrange("p j (m t) -> p m j t", t=PACK)
-            share = (PACK if by_planes else P) // len(engines)
-            for i, engine in enumerate(engines):
-                part = slice(i * share, (i + 1) * share)
-                if by_planes:
-                    cast(engine, dst[:, :, :, part], src[:, :, :, part])
-                else:
-                    pairs = "p m j (u t) -> p u m j t"
-                    cast(engine, dst[:, part].rearrange(pairs, u=2), src[:, part].rearrange(pairs, u=2))
+            for pair, engine in enumerate(engines):
+                planes = slice(2 * pair, 2 * pair + 2)
+                cast(engine, dst[:, :, :, planes], src[:, :, :, planes])
 
-        def quantise_wr(b, g, width):
+        def quantise_wr(b, g):
+            width = PASS // 2
             for c0 in range(0, PASS, width):
                 nc.vector.quantize_mx(
                     out=wr_q[b][g][:, c0 : c0 + width].bitcast(FP8X4),
@@ -165,11 +158,10 @@ def tile_list_gene_regulation_derivatives_kernel(
                 cast("scalar" if g == half else "vector", dst, src)
 
         def quantise_wd(half):
-            nc.vector.quantize_mx(
-                out=wd_q[half][:].rearrange("p g n -> p (g n)").bitcast(FP8X4),
-                scales=wd_s[half][:].rearrange("p g n -> p (g n)"),
-                in_=wd_bf[half][:].rearrange("p g n -> p (g n)"),
-            )
+            for g in (half, 1 - half):
+                nc.vector.quantize_mx(
+                    out=wd_q[half][:, g, :].bitcast(FP8X4), scales=wd_s[half][:, g, :], in_=wd_bf[half][:, g, :]
+                )
 
         def table_operand(g, cols):
             return v_w[g][:, cols].bitcast(FP8X4), v_s[4 * g : P, cols]
@@ -181,6 +173,7 @@ def tile_list_gene_regulation_derivatives_kernel(
             pieces_done.append((b, c))
             square, factor, h_bf = squares[turn % HILL_SLOTS], factors[turn % HILL_SLOTS], h_bfs[turn % HILL_SLOTS]
             per_bank = BANK // CHUNK
+            halves = [slice(j0, j0 + CHUNK // 2) for j0 in (0, CHUNK // 2)]
             for t0 in range(0, PACK, per_bank):
                 bank = a_banks[(PACK * turn + t0) // per_bank % A_BANKS]
                 for g in both:
@@ -196,9 +189,9 @@ def tile_list_gene_regulation_derivatives_kernel(
                             stop=(g == PASSES - 1 and t == t0 + per_bank - 1),
                         )
                 nc.scalar.activation(out=square[:, t0 : t0 + per_bank, :], in_=bank[:], func=ACT.Square)
-            shared = (b, c) in SHARED_PIECES
-            on_vector = c < VECTOR_RATE_CHUNKS and not shared
-            step = per_bank if on_vector else PACK
+            vector_rates = c < VECTOR_RATE_CHUNKS
+            vector_squares = vector_rates and b == 0
+            step = per_bank if vector_squares else PACK
             for t0 in range(0, PACK, step):
                 nc.scalar.activation(
                     out=factor[:, t0 : t0 + step, :],
@@ -206,24 +199,26 @@ def tile_list_gene_regulation_derivatives_kernel(
                     func=ACT.Abs_reciprocal_sqrt,
                     bias=one[:],
                 )
-            rated = square if c < VECTOR_RATE_CHUNKS else wr_raw[0][b][:, :, CHUNK * (c % 2) : CHUNK * (c % 2 + 1)]
-            second = wr_raw[1][1][:, :, CHUNK * c : CHUNK * (c + 1)] if on_vector else factor
+            c_late = c - VECTOR_RATE_CHUNKS
+            rated = square if vector_rates else wr_raw[0][b][:, :, CHUNK * c_late : CHUNK * (c_late + 1)]
             for t in range(PACK):
                 rate_col = rate_t[:, b, t : t + 1]
-                if on_vector:
-                    nc.vector.scalar_tensor_tensor(second[:, t, :], factor[:, t, :], rate_col, factor[:, t, :], MULT, MULT)
-                elif shared:
+                if vector_squares:
+                    for cols in halves if t == PACK - 1 else [slice(0, CHUNK)]:
+                        plane = factor[:, t, cols]
+                        nc.vector.scalar_tensor_tensor(plane, plane, rate_col, plane, MULT, MULT)
+                elif vector_rates:
                     nc.vector.tensor_scalar(square[:, t, :], square[:, t, :], rate_col, None, MULT)
                 else:
                     nc.scalar.activation(out=rated[:, t, :], in_=square[:, t, :], func=ACT.Copy, scale=rate_col)
-            if not on_vector:
-                nc.scalar.activation(out=factor[:], in_=factor[:], func=ACT.Square)
-            halves = [slice(j0, j0 + CHUNK // 2) for j0 in (0, CHUNK // 2)]
+            if not vector_squares:
+                for cols in halves if turn == last_turn else [slice(0, CHUNK)]:
+                    nc.scalar.activation(out=factor[:, :, cols], in_=factor[:, :, cols], func=ACT.Square)
             for cols in halves:
                 nc.vector.tensor_tensor(
                     h_bf[:, PACK * cols.start : PACK * cols.stop].rearrange("p (c i t) -> p c t i", i=RUN, t=PACK),
                     rated[:, :, cols].rearrange("p t (c i) -> p c t i", i=RUN),
-                    second[:, :, cols].rearrange("p t (c i) -> p c t i", i=RUN),
+                    factor[:, :, cols].rearrange("p t (c i) -> p c t i", i=RUN),
                     MULT,
                 )
             for cols in halves:
@@ -251,30 +246,28 @@ def tile_list_gene_regulation_derivatives_kernel(
                     stop=False,
                 )
             for b in both:
-                for j0 in range(0, CHUNK, Y_WIDTH):
-                    cols = slice(j0, j0 + Y_WIDTH)
-                    nc.tensor.matmul_mx(
-                        out=bank[:, cols],
-                        lhsT=wt_w[:, b, 2 * P * n : 2 * P * (n + 1)].bitcast(FP4X4),
-                        lhsT_scale=wt_s[:, b, P * n : P * (n + 1)],
-                        rhs=h_q[b][c][:, cols].bitcast(FP8X4),
-                        rhs_scale=h_s[b][c][:, cols],
-                        start=False,
-                        stop=(b == PASSES - 1 and j0 + Y_WIDTH == CHUNK),
-                    )
+                nc.tensor.matmul_mx(
+                    out=bank[:],
+                    lhsT=wt_w[:, b, 2 * P * n : 2 * P * (n + 1)].bitcast(FP4X4),
+                    lhsT_scale=wt_s[:, b, P * n : P * (n + 1)],
+                    rhs=h_q[b][c][:].bitcast(FP8X4),
+                    rhs_scale=h_s[b][c][:],
+                    start=False,
+                    stop=(b == PASSES - 1),
+                )
             nc.scalar.copy(out=y_sb[(n, c)], in_=bank[:])
-            if n in joined_tiles and c == CHUNKS - 2:
+            if (n, c) == (last_tile, last_chunk - 1):
                 return
-            joined = n in joined_tiles and c == CHUNKS - 1
+            joined = (n, c) == (last_tile, last_chunk)
             c0 = c - 1 if joined else c
             nc.vector.tensor_tensor(
                 cache[n][:].indirect(idx2[:, LIST_COLS * c0 : LIST_COLS * (c + 1)]),
-                y_pair[n][:] if joined else y_sb[(n, c)],
+                y_pair[:] if joined else y_sb[(n, c)],
                 wgo_t[:, CHUNK * c0 : CHUNK * (c + 1)],
                 MULT,
             )
-            if c == CHUNKS - 1:
-                if n < ROW_TILES - 1:
+            if c == last_chunk:
+                if n < last_tile:
                     nc.sync.dma_start(out=out[P * n : P * (n + 1), :], in_=cache[n][:])
                 else:
                     for queue, cols in ((nc.sync, slice(0, T2 // 2)), (nc.scalar, slice(T2 // 2, T2))):
@@ -282,31 +275,28 @@ def tile_list_gene_regulation_derivatives_kernel(
 
         nc.vector.tensor_copy(v_w[0][:], tab_w[0][:].bitcast(U32).indirect(idx[:]))
         nc.vector.tensor_copy(v_s[:], tab_s[:].bitcast(U8).indirect(idx[:]))
-        cast_wr(0, 0, ["scalar", "scalar"], True)
-        cast_wr(0, 1, ["vector", "scalar"], True)
+        cast_wr(0, 0, ["scalar", "scalar"])
+        cast_wr(0, 1, ["vector", "scalar"])
         for g in both:
-            quantise_wr(0, g, PASS // 2)
+            quantise_wr(0, g)
         for j0, j1 in ((0, CHUNK), (CHUNK, S)):
             nc.vector.tensor_copy(v_w[1][:, j0:j1], tab_w[1][:].bitcast(U32).indirect(idx[:, j0 // 16 : j1 // 16]))
         for g in both:
-            cast_wr(1, g, ["vector", "vector"], True)
-            quantise_wr(1, g, PASS // 2)
+            cast_wr(1, g, ["vector", "vector"])
+            quantise_wr(1, g)
 
         waiting = [(n, c) for c in range(CHUNKS) for n in range(ROW_TILES)]
-        for n in joined_tiles:
-            waiting.remove((n, CHUNKS - 2))
-            waiting.insert(waiting.index((n, CHUNKS - 1)), (n, CHUNKS - 2))
-        pieces = [(b, c) for c in range(CHUNKS) for b in both]
+        waiting.remove((last_tile, last_chunk - 1))
+        waiting.insert(len(waiting) - 1, (last_tile, last_chunk - 1))
         first_with_products = PASSES * VECTOR_RATE_CHUNKS - 1
-        for turn, (b, c) in enumerate(pieces):
+        for turn, (b, c) in enumerate([(b, c) for c in range(CHUNKS) for b in both]):
             hill(b, c)
             if turn in (0, first_with_products):
                 half = 0 if turn == 0 else 1
                 cast_wd(half)
                 quantise_wd(half)
-            if turn >= first_with_products:
-                count = PRODUCTS_PER_PIECE + (1 if turn in (5, 6) else 0)
-                for place in range(count):
+            if first_with_products <= turn < last_turn:
+                for place in range(PRODUCTS_BEHIND_PIECES[turn - first_with_products]):
                     product_and_scatter(*waiting.pop(0))
         for n, c in waiting:
             product_and_scatter(n, c)

@@ -29,10 +29,11 @@ HALF = N // 2
 RUN = 4
 A_BANKS = 6
 Y_BANKS = 2
-HILL_SLOTS = 3
-
-VECTOR_RATE_CHUNKS = 2
-PRODUCTS_BEHIND_PIECES = (2, 2, 3, 3)
+SQUARE_SLOTS = 3
+FACTOR_SLOTS = 4
+PIECES = [(b, c) for c in range(CHUNKS) for b in range(PASSES)]
+VECTOR_RATE_PIECES = 2
+VECTOR_PRODUCT_PIECES = 3
 
 
 def tile_list_gene_regulation_derivatives_kernel(
@@ -52,7 +53,7 @@ def tile_list_gene_regulation_derivatives_kernel(
         idx = lists.tile([P, S // 16], U16, name="idx")
         idx2 = lists.tile([P, S // 16], U16, name="idx2")
         a_banks = [psum.tile([P, BANK // CHUNK, CHUNK], F32, name="a_bank%d" % i) for i in range(A_BANKS)]
-        y_banks = [psum.tile([P, CHUNK], F32, name="y_bank%d" % i) for i in range(Y_BANKS)]
+        y_banks = [psum.tile([P, BANK // CHUNK, CHUNK], F32, name="y_bank%d" % i) for i in range(Y_BANKS)]
 
         tab_w = [held("tab_w%d" % g, [P, T], I32) for g in both]
         tab_s = held("tab_s", [P, T // 4], I32)
@@ -71,22 +72,15 @@ def tile_list_gene_regulation_derivatives_kernel(
         rate_t = held("rate_t", [P, PASSES, PACK], F32)
         wgo_t = held("wgo_t", [P, S], F32)
         one = held("one", [P, 1], F32)
-        squares = [held("square%d" % i, [P, PACK, CHUNK], F32) for i in range(HILL_SLOTS)]
-        factors = [held("factor%d" % i, [P, PACK, CHUNK], F32) for i in range(HILL_SLOTS)]
-        h_bfs = [held("h_bf%d" % i, [P, PACK * CHUNK], BF16) for i in range(HILL_SLOTS)]
+        squares = [held("square%d" % i, [P, PACK, CHUNK], F32) for i in range(SQUARE_SLOTS)]
+        rateds = [held("rated%d" % i, [P, PACK, CHUNK], F32) for i in range(SQUARE_SLOTS)]
+        factors = [held("factor%d" % i, [P, PACK, CHUNK], F32) for i in range(FACTOR_SLOTS)]
+        h_early = [held("h_early%d" % i, [P, PACK * CHUNK], BF16) for i in range(VECTOR_PRODUCT_PIECES - 1)]
+        h_late = wd_bf[1][:, 0, :]
         h_q = [[held("h_q%d%d" % (b, c), [P, CHUNK], U32) for c in range(CHUNKS)] for b in both]
         h_s = [[held("h_s%d%d" % (b, c), [P, CHUNK], U8) for c in range(CHUNKS)] for b in both]
-        last_tile, last_chunk, last_turn = ROW_TILES - 1, CHUNKS - 1, PASSES * CHUNKS - 1
+        y_last = held("y_last", [P, ROW_TILES - 1, CHUNK], F32)
         y_pair = held("y_pair", [P, 2 * CHUNK], F32)
-        y_sb = {
-            (last_tile - 1, last_chunk - 1): factors[last_turn % HILL_SLOTS][:, 0, :],
-            (last_tile, last_chunk - 1): y_pair[:, :CHUNK],
-            (last_tile, last_chunk): y_pair[:, CHUNK:],
-        }
-        for n in range(ROW_TILES):
-            for c in range(CHUNKS):
-                if (n, c) not in y_sb:
-                    y_sb[(n, c)] = held("y%d%d" % (n, c), [P, CHUNK], F32)[:]
         cache = [held("cache%d" % n, [P, T2], F32) for n in range(ROW_TILES)]
 
         nc.vector.memset(one[:], 1.0)
@@ -158,22 +152,31 @@ def tile_list_gene_regulation_derivatives_kernel(
                 cast("scalar" if g == half else "vector", dst, src)
 
         def quantise_wd(half):
-            for g in (half, 1 - half):
+            if half == 0:
+                for g in (half, 1 - half):
+                    nc.vector.quantize_mx(
+                        out=wd_q[half][:, g, :].bitcast(FP8X4), scales=wd_s[half][:, g, :], in_=wd_bf[half][:, g, :]
+                    )
+            else:
                 nc.vector.quantize_mx(
-                    out=wd_q[half][:, g, :].bitcast(FP8X4), scales=wd_s[half][:, g, :], in_=wd_bf[half][:, g, :]
+                    out=wd_q[half][:].rearrange("p g c -> p (g c)").bitcast(FP8X4),
+                    scales=wd_s[half][:].rearrange("p g c -> p (g c)"),
+                    in_=wd_bf[half][:].rearrange("p g c -> p (g c)"),
                 )
 
         def table_operand(g, cols):
             return v_w[g][:, cols].bitcast(FP8X4), v_s[4 * g : P, cols]
 
-        pieces_done = []
+        halves = [slice(j0, j0 + CHUNK // 2) for j0 in (0, CHUNK // 2)]
+        whole = [slice(0, CHUNK)]
 
-        def hill(b, c):
-            turn = len(pieces_done)
-            pieces_done.append((b, c))
-            square, factor, h_bf = squares[turn % HILL_SLOTS], factors[turn % HILL_SLOTS], h_bfs[turn % HILL_SLOTS]
+        def h_buffer(turn):
+            return h_early[turn][:] if turn < len(h_early) else h_late
+
+        def two_factors(turn):
+            b, c = PIECES[turn]
+            square, factor = squares[turn % SQUARE_SLOTS], factors[turn % FACTOR_SLOTS]
             per_bank = BANK // CHUNK
-            halves = [slice(j0, j0 + CHUNK // 2) for j0 in (0, CHUNK // 2)]
             for t0 in range(0, PACK, per_bank):
                 bank = a_banks[(PACK * turn + t0) // per_bank % A_BANKS]
                 for g in both:
@@ -189,9 +192,8 @@ def tile_list_gene_regulation_derivatives_kernel(
                             stop=(g == PASSES - 1 and t == t0 + per_bank - 1),
                         )
                 nc.scalar.activation(out=square[:, t0 : t0 + per_bank, :], in_=bank[:], func=ACT.Square)
-            vector_rates = c < VECTOR_RATE_CHUNKS
-            vector_squares = vector_rates and b == 0
-            step = per_bank if vector_squares else PACK
+            vector_rates = turn < VECTOR_RATE_PIECES
+            step = per_bank if vector_rates else PACK
             for t0 in range(0, PACK, step):
                 nc.scalar.activation(
                     out=factor[:, t0 : t0 + step, :],
@@ -199,79 +201,75 @@ def tile_list_gene_regulation_derivatives_kernel(
                     func=ACT.Abs_reciprocal_sqrt,
                     bias=one[:],
                 )
-            c_late = c - VECTOR_RATE_CHUNKS
-            rated = square if vector_rates else wr_raw[0][b][:, :, CHUNK * c_late : CHUNK * (c_late + 1)]
+            rated = square if vector_rates else rateds[turn % SQUARE_SLOTS]
             for t in range(PACK):
                 rate_col = rate_t[:, b, t : t + 1]
-                if vector_squares:
-                    for cols in halves if t == PACK - 1 else [slice(0, CHUNK)]:
+                if vector_rates:
+                    for cols in halves if t == PACK - 1 else whole:
                         plane = factor[:, t, cols]
                         nc.vector.scalar_tensor_tensor(plane, plane, rate_col, plane, MULT, MULT)
-                elif vector_rates:
-                    nc.vector.tensor_scalar(square[:, t, :], square[:, t, :], rate_col, None, MULT)
                 else:
                     nc.scalar.activation(out=rated[:, t, :], in_=square[:, t, :], func=ACT.Copy, scale=rate_col)
-            if not vector_squares:
-                for cols in halves if turn == last_turn else [slice(0, CHUNK)]:
-                    nc.scalar.activation(out=factor[:, :, cols], in_=factor[:, :, cols], func=ACT.Square)
-            for cols in halves:
-                nc.vector.tensor_tensor(
+            if not vector_rates:
+                nc.scalar.activation(out=factor[:], in_=factor[:], func=ACT.Square)
+            return rated, factor
+
+        def multiply_out(turn, rated, factor, engine, parts):
+            h_bf = h_buffer(turn)
+            for cols in parts:
+                engine.tensor_tensor(
                     h_bf[:, PACK * cols.start : PACK * cols.stop].rearrange("p (c i t) -> p c t i", i=RUN, t=PACK),
                     rated[:, :, cols].rearrange("p t (c i) -> p c t i", i=RUN),
                     factor[:, :, cols].rearrange("p t (c i) -> p c t i", i=RUN),
                     MULT,
                 )
-            for cols in halves:
+
+        def quantise_h(turn, parts):
+            b, c = PIECES[turn]
+            h_bf = h_buffer(turn)
+            for cols in parts:
                 nc.vector.quantize_mx(
                     out=h_q[b][c][:, cols].bitcast(FP8X4),
                     scales=h_s[b][c][:, cols],
                     in_=h_bf[:, PACK * cols.start : PACK * cols.stop],
                 )
 
-        products_done = []
+        groups_done = []
 
-        def product_and_scatter(n, c):
-            bank = y_banks[len(products_done) % Y_BANKS]
-            products_done.append((n, c))
-            half, n0 = divmod(P * n, HALF)
-            for g in both:
-                words, scales = table_operand(g, slice(CHUNK * c, CHUNK * (c + 1)))
-                nc.tensor.matmul_mx(
-                    out=bank[:],
-                    lhsT=wd_q[half][:, g, n0 : n0 + P].bitcast(FP8X4),
-                    lhsT_scale=wd_s[half][:, g, n0 : n0 + P],
-                    rhs=words,
-                    rhs_scale=scales,
-                    start=(g == 0),
-                    stop=False,
-                )
+        def products(places):
+            bank = y_banks[len(groups_done) % Y_BANKS]
+            groups_done.append(places)
+            for i, (n, c) in enumerate(places):
+                half, n0 = divmod(P * n, HALF)
+                for g in both:
+                    words, scales = table_operand(g, slice(CHUNK * c, CHUNK * (c + 1)))
+                    nc.tensor.matmul_mx(
+                        out=bank[:, i, :],
+                        lhsT=wd_q[half][:, g, n0 : n0 + P].bitcast(FP8X4),
+                        lhsT_scale=wd_s[half][:, g, n0 : n0 + P],
+                        rhs=words,
+                        rhs_scale=scales,
+                        start=(i == 0 and g == 0),
+                        stop=False,
+                    )
             for b in both:
-                nc.tensor.matmul_mx(
-                    out=bank[:],
-                    lhsT=wt_w[:, b, 2 * P * n : 2 * P * (n + 1)].bitcast(FP4X4),
-                    lhsT_scale=wt_s[:, b, P * n : P * (n + 1)],
-                    rhs=h_q[b][c][:].bitcast(FP8X4),
-                    rhs_scale=h_s[b][c][:],
-                    start=False,
-                    stop=(b == PASSES - 1),
-                )
-            nc.scalar.copy(out=y_sb[(n, c)], in_=bank[:])
-            if (n, c) == (last_tile, last_chunk - 1):
-                return
-            joined = (n, c) == (last_tile, last_chunk)
-            c0 = c - 1 if joined else c
-            nc.vector.tensor_tensor(
-                cache[n][:].indirect(idx2[:, LIST_COLS * c0 : LIST_COLS * (c + 1)]),
-                y_pair[:] if joined else y_sb[(n, c)],
-                wgo_t[:, CHUNK * c0 : CHUNK * (c + 1)],
-                MULT,
-            )
-            if c == last_chunk:
-                if n < last_tile:
-                    nc.sync.dma_start(out=out[P * n : P * (n + 1), :], in_=cache[n][:])
-                else:
-                    for queue, cols in ((nc.sync, slice(0, T2 // 2)), (nc.scalar, slice(T2 // 2, T2))):
-                        queue.dma_start(out=out[P * n : P * (n + 1), cols], in_=cache[n][:, cols])
+                for i, (n, c) in enumerate(places):
+                    nc.tensor.matmul_mx(
+                        out=bank[:, i, :],
+                        lhsT=wt_w[:, b, 2 * P * n : 2 * P * (n + 1)].bitcast(FP4X4),
+                        lhsT_scale=wt_s[:, b, P * n : P * (n + 1)],
+                        rhs=h_q[b][c][:].bitcast(FP8X4),
+                        rhs_scale=h_s[b][c][:],
+                        start=False,
+                        stop=(b == PASSES - 1 and i == len(places) - 1),
+                    )
+            return bank
+
+        def list2(c0, c1):
+            return idx2[:, LIST_COLS * c0 : LIST_COLS * c1]
+
+        def fused_scatter(n, c0, c1, y_sb):
+            nc.vector.tensor_tensor(cache[n][:].indirect(list2(c0, c1)), y_sb, wgo_t[:, CHUNK * c0 : CHUNK * c1], MULT)
 
         nc.vector.tensor_copy(v_w[0][:], tab_w[0][:].bitcast(U32).indirect(idx[:]))
         nc.vector.tensor_copy(v_s[:], tab_s[:].bitcast(U8).indirect(idx[:]))
@@ -285,18 +283,40 @@ def tile_list_gene_regulation_derivatives_kernel(
             cast_wr(1, g, ["vector", "vector"])
             quantise_wr(1, g)
 
-        waiting = [(n, c) for c in range(CHUNKS) for n in range(ROW_TILES)]
-        waiting.remove((last_tile, last_chunk - 1))
-        waiting.insert(len(waiting) - 1, (last_tile, last_chunk - 1))
-        first_with_products = PASSES * VECTOR_RATE_CHUNKS - 1
-        for turn, (b, c) in enumerate([(b, c) for c in range(CHUNKS) for b in both]):
-            hill(b, c)
-            if turn in (0, first_with_products):
-                half = 0 if turn == 0 else 1
-                cast_wd(half)
-                quantise_wd(half)
-            if first_with_products <= turn < last_turn:
-                for place in range(PRODUCTS_BEHIND_PIECES[turn - first_with_products]):
-                    product_and_scatter(*waiting.pop(0))
-        for n, c in waiting:
-            product_and_scatter(n, c)
+        for turn in range(VECTOR_PRODUCT_PIECES - 1):
+            rated, factor = two_factors(turn)
+            multiply_out(turn, rated, factor, nc.vector, halves)
+            quantise_h(turn, halves)
+            cast_wd(turn)
+            quantise_wd(turn)
+        last_turn = len(PIECES) - 1
+        for turn in range(VECTOR_PRODUCT_PIECES - 1, last_turn):
+            rated, factor = two_factors(turn)
+            multiply_out(turn, rated, factor, nc.vector if turn < VECTOR_PRODUCT_PIECES else nc.gpsimd, whole)
+            c, pair = divmod(turn - (VECTOR_PRODUCT_PIECES - 1), 2)
+            places = [(2 * pair, c), (2 * pair + 1, c)]
+            bank = products(places)
+            for i in range(2):
+                nc.vector.tensor_tensor(factor[:, i, :], bank[:, i, :], wgo_t[:, CHUNK * c : CHUNK * (c + 1)], MULT)
+            quantise_h(turn, whole)
+            for i, (n, c) in enumerate(places):
+                nc.vector.tensor_copy(cache[n][:].indirect(list2(c, c + 1)), factor[:, i, :])
+        rated, factor = two_factors(last_turn)
+        multiply_out(last_turn, rated, factor, nc.gpsimd, whole)
+        last_tile, last_chunk = ROW_TILES - 1, CHUNKS - 1
+        bank = products([(last_tile - 1, last_chunk - 1), (last_tile, last_chunk - 1)])
+        nc.scalar.copy(out=factor[:, 0, :], in_=bank[:, 0, :])
+        nc.scalar.copy(out=y_pair[:, :CHUNK], in_=bank[:, 1, :])
+        quantise_h(last_turn, whole)
+        fused_scatter(last_tile - 1, last_chunk - 1, last_chunk, factor[:, 0, :])
+        for n in range(ROW_TILES):
+            bank = products([(n, last_chunk)])
+            if n < last_tile:
+                nc.scalar.copy(out=y_last[:, n, :], in_=bank[:, 0, :])
+                fused_scatter(n, last_chunk, last_chunk + 1, y_last[:, n, :])
+                nc.sync.dma_start(out=out[P * n : P * (n + 1), :], in_=cache[n][:])
+            else:
+                nc.scalar.copy(out=y_pair[:, CHUNK:], in_=bank[:, 0, :])
+                fused_scatter(n, last_chunk - 1, last_chunk + 1, y_pair[:])
+                for queue, cols in ((nc.sync, slice(0, T2 // 2)), (nc.scalar, slice(T2 // 2, T2))):
+                    queue.dma_start(out=out[P * n : P * (n + 1), cols], in_=cache[n][:, cols])

@@ -11,6 +11,7 @@ U8 = mybir.dt.uint8
 FP8X4 = mybir.dt.float8_e4m3fn_x4
 FP4X4 = mybir.dt.float4_e2m1fn_x4
 MULT = mybir.AluOpType.mult
+ADD = mybir.AluOpType.add
 ACT = mybir.ActivationFunctionType
 
 K, H, N, T, S, T2 = 1024, 1024, 512, 2048, 1024, 2048
@@ -33,6 +34,7 @@ SQUARE_SLOTS = 3
 FACTOR_SLOTS = 4
 PIECES = [(b, c) for c in range(CHUNKS) for b in range(PASSES)]
 VECTOR_RATE_PIECES = 2
+GPSIMD_PLANES = 2
 VECTOR_PRODUCT_PIECES = 3
 
 
@@ -63,7 +65,7 @@ def tile_list_gene_regulation_derivatives_kernel(
         wr_bf = [[held("wr_bf%d%d" % (b, g), [P, PACK * PASS], BF16) for g in both] for b in both]
         wr_q = [[held("wr_q%d%d" % (b, g), [P, PASS], U32) for g in both] for b in both]
         wr_s = [[held("wr_s%d%d" % (b, g), [P, PASS], U8) for g in both] for b in both]
-        wd_raw = [held("wd_raw%d" % g, [P, PACK, N], F32) for g in both]
+        wd_raw = [[held("wd_raw%d%d" % (half, g), [P, PACK, HALF], F32) for g in both] for half in range(2)]
         wd_bf = [held("wd_bf%d" % half, [P, PASSES, PACK * HALF], BF16) for half in range(2)]
         wd_q = [held("wd_q%d" % half, [P, PASSES, HALF], U32) for half in range(2)]
         wd_s = [held("wd_s%d" % half, [P, PASSES, HALF], U8) for half in range(2)]
@@ -73,9 +75,10 @@ def tile_list_gene_regulation_derivatives_kernel(
         wgo_t = held("wgo_t", [P, S], F32)
         one = held("one", [P, 1], F32)
         squares = [held("square%d" % i, [P, PACK, CHUNK], F32) for i in range(SQUARE_SLOTS)]
-        rateds = [held("rated%d" % i, [P, PACK, CHUNK], F32) for i in range(SQUARE_SLOTS)]
+        rateds = [held("rated%d" % i, [P, PACK, CHUNK], F32) for i in range(2)]
+        rated_late = held("rated_late", [P, 2 * PACK - GPSIMD_PLANES, CHUNK], F32)
         factors = [held("factor%d" % i, [P, PACK, CHUNK], F32) for i in range(FACTOR_SLOTS)]
-        h_early = [held("h_early%d" % i, [P, PACK * CHUNK], BF16) for i in range(VECTOR_PRODUCT_PIECES - 1)]
+        h_early = [held("h_early%d" % i, [P, PACK * CHUNK], BF16) for i in range(VECTOR_PRODUCT_PIECES)]
         h_late = wd_bf[1][:, 0, :]
         h_q = [[held("h_q%d%d" % (b, c), [P, CHUNK], U32) for c in range(CHUNKS)] for b in both]
         h_s = [[held("h_s%d%d" % (b, c), [P, CHUNK], U8) for c in range(CHUNKS)] for b in both]
@@ -112,8 +115,9 @@ def tile_list_gene_regulation_derivatives_kernel(
         for g in both:
             load_wr(1, g)
         nc.sync.dma_start(out=rate_t[:], in_=rate.rearrange("(b p t) -> p b t", b=PASSES, t=PACK))
-        for g in both:
-            nc.sync.dma_start(out=wd_raw[g][:], in_=rows_of_pass(wd, g))
+        for half in range(2):
+            for g in both:
+                nc.sync.dma_start(out=wd_raw[half][g][:], in_=rows_of_pass(wd, g)[:, :, HALF * half : HALF * (half + 1)])
         for q in range(4):
             nc.sync.dma_start(
                 out=wt_s[32 * q : 32 * q + 4, :, :].bitcast(I32),
@@ -148,8 +152,8 @@ def tile_list_gene_regulation_derivatives_kernel(
         def cast_wd(half):
             for g in both:
                 dst = wd_bf[half][:, g, :].rearrange("p (c i j) -> p c j i", i=RUN, j=PACK)
-                src = wd_raw[g][:, :, HALF * half : HALF * (half + 1)].rearrange("p j (c i) -> p c j i", i=RUN)
-                cast("scalar" if g == half else "vector", dst, src)
+                src = wd_raw[half][g][:].rearrange("p j (c i) -> p c j i", i=RUN)
+                cast("scalar" if half == 1 else "vector", dst, src)
 
         def quantise_wd(half):
             if half == 0:
@@ -201,13 +205,17 @@ def tile_list_gene_regulation_derivatives_kernel(
                     func=ACT.Abs_reciprocal_sqrt,
                     bias=one[:],
                 )
-            rated = square if vector_rates else rateds[turn % SQUARE_SLOTS]
+            late = turn > VECTOR_PRODUCT_PIECES
+            first = (PACK - GPSIMD_PLANES) * (turn % 2)
+            rated = square if vector_rates else rated_late[:, first : first + PACK, :] if late else rateds[turn % 2]
             for t in range(PACK):
                 rate_col = rate_t[:, b, t : t + 1]
                 if vector_rates:
                     for cols in halves if t == PACK - 1 else whole:
                         plane = factor[:, t, cols]
                         nc.vector.scalar_tensor_tensor(plane, plane, rate_col, plane, MULT, MULT)
+                elif late and PACK - GPSIMD_PLANES <= first + t < PACK:
+                    nc.gpsimd.tensor_scalar(rated[:, t, :], square[:, t, :], rate_col, 0.0, MULT, ADD)
                 else:
                     nc.scalar.activation(out=rated[:, t, :], in_=square[:, t, :], func=ACT.Copy, scale=rate_col)
             if not vector_rates:
@@ -287,8 +295,9 @@ def tile_list_gene_regulation_derivatives_kernel(
             rated, factor = two_factors(turn)
             multiply_out(turn, rated, factor, nc.vector, halves)
             quantise_h(turn, halves)
-            cast_wd(turn)
-            quantise_wd(turn)
+        for half in range(2):
+            cast_wd(half)
+            quantise_wd(half)
         last_turn = len(PIECES) - 1
         for turn in range(VECTOR_PRODUCT_PIECES - 1, last_turn):
             rated, factor = two_factors(turn)

@@ -28,13 +28,13 @@ LIST_COLS = CHUNK // 16
 BANK = 512
 HALF = N // 2
 RUN = 4
-A_BANKS = 6
-Y_BANKS = 2
+BANKS = 8
 SQUARE_SLOTS = 3
 FACTOR_SLOTS = 4
-PIECES = [(b, c) for c in range(CHUNKS) for b in range(PASSES)]
-VECTOR_RATE_PIECES = 2
-GPSIMD_PLANES = 2
+PIECES = [(0, 0), (0, 1), (1, 0), (1, 1)] + [(b, c) for c in range(2, CHUNKS) for b in range(PASSES)]
+PIECE_BANKS = [0, 2, 4, 0, 2, 4, 6, 2]
+GROUP_BANKS = [6, 6, 0, 1, 4, 5, 6, 7, 0, 1]
+GPSIMD_PLANES = 1
 VECTOR_PRODUCT_PIECES = 3
 
 
@@ -54,8 +54,7 @@ def tile_list_gene_regulation_derivatives_kernel(
 
         idx = lists.tile([P, S // 16], U16, name="idx")
         idx2 = lists.tile([P, S // 16], U16, name="idx2")
-        a_banks = [psum.tile([P, BANK // CHUNK, CHUNK], F32, name="a_bank%d" % i) for i in range(A_BANKS)]
-        y_banks = [psum.tile([P, BANK // CHUNK, CHUNK], F32, name="y_bank%d" % i) for i in range(Y_BANKS)]
+        banks = [psum.tile([P, BANK // CHUNK, CHUNK], F32, name="bank%d" % i) for i in range(BANKS)]
 
         tab_w = [held("tab_w%d" % g, [P, T], I32) for g in both]
         tab_s = held("tab_s", [P, T // 4], I32)
@@ -75,7 +74,7 @@ def tile_list_gene_regulation_derivatives_kernel(
         wgo_t = held("wgo_t", [P, S], F32)
         one = held("one", [P, 1], F32)
         squares = [held("square%d" % i, [P, PACK, CHUNK], F32) for i in range(SQUARE_SLOTS)]
-        rateds = [held("rated%d" % i, [P, PACK, CHUNK], F32) for i in range(2)]
+        rated_early = held("rated_early", [P, PACK, CHUNK], F32)
         rated_late = held("rated_late", [P, 2 * PACK - GPSIMD_PLANES, CHUNK], F32)
         factors = [held("factor%d" % i, [P, PACK, CHUNK], F32) for i in range(FACTOR_SLOTS)]
         h_early = [held("h_early%d" % i, [P, PACK * CHUNK], BF16) for i in range(VECTOR_PRODUCT_PIECES)]
@@ -102,6 +101,10 @@ def tile_list_gene_regulation_derivatives_kernel(
         def load_wr(b, g):
             nc.sync.dma_start(out=wr_raw[b][g][:], in_=rows_of_pass(wr, g)[:, :, PASS * b : PASS * (b + 1)])
 
+        def load_wd(half):
+            for g in both:
+                nc.sync.dma_start(out=wd_raw[half][g][:], in_=rows_of_pass(wd, g)[:, :, HALF * half : HALF * (half + 1)])
+
         def load_words(g):
             nc.sync.dma_start(out=tab_w[g][:], in_=tab_words[g].rearrange("p t i -> p (t i)").bitcast(I32))
 
@@ -115,9 +118,7 @@ def tile_list_gene_regulation_derivatives_kernel(
         for g in both:
             load_wr(1, g)
         nc.sync.dma_start(out=rate_t[:], in_=rate.rearrange("(b p t) -> p b t", b=PASSES, t=PACK))
-        for half in range(2):
-            for g in both:
-                nc.sync.dma_start(out=wd_raw[half][g][:], in_=rows_of_pass(wd, g)[:, :, HALF * half : HALF * (half + 1)])
+        load_wd(0)
         for q in range(4):
             nc.sync.dma_start(
                 out=wt_s[32 * q : 32 * q + 4, :, :].bitcast(I32),
@@ -126,6 +127,7 @@ def tile_list_gene_regulation_derivatives_kernel(
         nc.sync.dma_start(out=wt_w[:].bitcast(I32), in_=wt4_words.rearrange("g p c -> p g c").bitcast(I32))
         nc.sync.dma_start(idx2[:], offs2)
         nc.sync.dma_start(out=wgo_t[:], in_=wgo)
+        load_wd(1)
 
         def cast(engine, dst, src):
             if engine == "vector":
@@ -153,7 +155,7 @@ def tile_list_gene_regulation_derivatives_kernel(
             for g in both:
                 dst = wd_bf[half][:, g, :].rearrange("p (c i j) -> p c j i", i=RUN, j=PACK)
                 src = wd_raw[half][g][:].rearrange("p j (c i) -> p c j i", i=RUN)
-                cast("scalar" if half == 1 else "vector", dst, src)
+                cast("scalar" if (half, g) == (0, 1) else "vector", dst, src)
 
         def quantise_wd(half):
             if half == 0:
@@ -182,7 +184,7 @@ def tile_list_gene_regulation_derivatives_kernel(
             square, factor = squares[turn % SQUARE_SLOTS], factors[turn % FACTOR_SLOTS]
             per_bank = BANK // CHUNK
             for t0 in range(0, PACK, per_bank):
-                bank = a_banks[(PACK * turn + t0) // per_bank % A_BANKS]
+                bank = banks[PIECE_BANKS[turn] + t0 // per_bank]
                 for g in both:
                     for t in range(t0, t0 + per_bank):
                         words, scales = table_operand(g, slice(CHUNK * c, CHUNK * (c + 1)))
@@ -196,30 +198,35 @@ def tile_list_gene_regulation_derivatives_kernel(
                             stop=(g == PASSES - 1 and t == t0 + per_bank - 1),
                         )
                 nc.scalar.activation(out=square[:, t0 : t0 + per_bank, :], in_=bank[:], func=ACT.Square)
-            vector_rates = turn < VECTOR_RATE_PIECES
-            step = per_bank if vector_rates else PACK
-            for t0 in range(0, PACK, step):
-                nc.scalar.activation(
-                    out=factor[:, t0 : t0 + step, :],
-                    in_=square[:, t0 : t0 + step, :],
-                    func=ACT.Abs_reciprocal_sqrt,
-                    bias=one[:],
-                )
+            vector_rates = c == 0
             late = turn > VECTOR_PRODUCT_PIECES
             first = (PACK - GPSIMD_PLANES) * (turn % 2)
-            rated = square if vector_rates else rated_late[:, first : first + PACK, :] if late else rateds[turn % 2]
-            for t in range(PACK):
-                rate_col = rate_t[:, b, t : t + 1]
-                if vector_rates:
+            on_gpsimd = turn >= VECTOR_PRODUCT_PIECES
+            rated = square if vector_rates else rated_late[:, first : first + PACK, :] if on_gpsimd else rated_early
+
+            def inverse_root(planes):
+                nc.scalar.activation(
+                    out=factor[:, planes, :], in_=square[:, planes, :], func=ACT.Abs_reciprocal_sqrt, bias=one[:]
+                )
+
+            if vector_rates:
+                for t0 in range(0, PACK, per_bank):
+                    inverse_root(slice(t0, t0 + per_bank))
+                for t in range(PACK):
                     for cols in halves if t == PACK - 1 else whole:
                         plane = factor[:, t, cols]
-                        nc.vector.scalar_tensor_tensor(plane, plane, rate_col, plane, MULT, MULT)
-                elif late and PACK - GPSIMD_PLANES <= first + t < PACK:
+                        nc.vector.scalar_tensor_tensor(plane, plane, rate_t[:, b, t : t + 1], plane, MULT, MULT)
+                return rated, factor
+            for t in range(PACK):
+                rate_col = rate_t[:, b, t : t + 1]
+                if t == per_bank:
+                    inverse_root(slice(0, PACK))
+                if late and PACK - GPSIMD_PLANES <= first + t < PACK:
                     nc.gpsimd.tensor_scalar(rated[:, t, :], square[:, t, :], rate_col, 0.0, MULT, ADD)
                 else:
                     nc.scalar.activation(out=rated[:, t, :], in_=square[:, t, :], func=ACT.Copy, scale=rate_col)
-            if not vector_rates:
-                nc.scalar.activation(out=factor[:], in_=factor[:], func=ACT.Square)
+            for cols in halves if turn == len(PIECES) - 1 else whole:
+                nc.scalar.activation(out=factor[:, :, cols], in_=factor[:, :, cols], func=ACT.Square)
             return rated, factor
 
         def multiply_out(turn, rated, factor, engine, parts):
@@ -245,7 +252,7 @@ def tile_list_gene_regulation_derivatives_kernel(
         groups_done = []
 
         def products(places):
-            bank = y_banks[len(groups_done) % Y_BANKS]
+            bank = banks[GROUP_BANKS[len(groups_done)]]
             groups_done.append(places)
             for i, (n, c) in enumerate(places):
                 half, n0 = divmod(P * n, HALF)
@@ -291,27 +298,35 @@ def tile_list_gene_regulation_derivatives_kernel(
             cast_wr(1, g, ["vector", "vector"])
             quantise_wr(1, g)
 
-        for turn in range(VECTOR_PRODUCT_PIECES - 1):
-            rated, factor = two_factors(turn)
-            multiply_out(turn, rated, factor, nc.vector, halves)
-            quantise_h(turn, halves)
-        for half in range(2):
-            cast_wd(half)
-            quantise_wd(half)
-        last_turn = len(PIECES) - 1
-        for turn in range(VECTOR_PRODUCT_PIECES - 1, last_turn):
-            rated, factor = two_factors(turn)
-            multiply_out(turn, rated, factor, nc.vector if turn < VECTOR_PRODUCT_PIECES else nc.gpsimd, whole)
-            c, pair = divmod(turn - (VECTOR_PRODUCT_PIECES - 1), 2)
+        def step(pair_number, staged, turn):
+            c, pair = divmod(pair_number, 2)
             places = [(2 * pair, c), (2 * pair + 1, c)]
             bank = products(places)
             for i in range(2):
-                nc.vector.tensor_tensor(factor[:, i, :], bank[:, i, :], wgo_t[:, CHUNK * c : CHUNK * (c + 1)], MULT)
-            quantise_h(turn, whole)
+                nc.vector.tensor_tensor(staged[:, i, :], bank[:, i, :], wgo_t[:, CHUNK * c : CHUNK * (c + 1)], MULT)
+            if turn is not None:
+                quantise_h(turn, whole)
             for i, (n, c) in enumerate(places):
-                nc.vector.tensor_copy(cache[n][:].indirect(list2(c, c + 1)), factor[:, i, :])
+                nc.vector.tensor_copy(cache[n][:].indirect(list2(c, c + 1)), staged[:, i, :])
+
+        for turn in range(VECTOR_PRODUCT_PIECES):
+            rated, factor = two_factors(turn)
+            multiply_out(turn, rated, factor, nc.vector, halves)
+            quantise_h(turn, halves)
+            if turn == 0:
+                cast_wd(0)
+            if turn == 1:
+                quantise_wd(0)
+        cast_wd(1)
+        quantise_wd(1)
+        step(0, wd_raw[1][1], None)
+        last_turn = len(PIECES) - 1
+        for turn in range(VECTOR_PRODUCT_PIECES, last_turn):
+            rated, factor = two_factors(turn)
+            multiply_out(turn, rated, factor, nc.gpsimd, whole)
+            step(turn - VECTOR_PRODUCT_PIECES + 1, factor, turn)
         rated, factor = two_factors(last_turn)
-        multiply_out(last_turn, rated, factor, nc.gpsimd, whole)
+        multiply_out(last_turn, rated, factor, nc.gpsimd, halves)
         last_tile, last_chunk = ROW_TILES - 1, CHUNKS - 1
         bank = products([(last_tile - 1, last_chunk - 1), (last_tile, last_chunk - 1)])
         nc.scalar.copy(out=factor[:, 0, :], in_=bank[:, 0, :])

@@ -302,10 +302,10 @@ def tile_list_gene_regulation_derivatives_kernel(
             c, pair = divmod(pair_number, 2)
             places = [(2 * pair, c), (2 * pair + 1, c)]
             bank = products(places)
-            for i in range(2):
-                nc.vector.tensor_tensor(staged[:, i, :], bank[:, i, :], wgo_t[:, CHUNK * c : CHUNK * (c + 1)], MULT)
             if turn is not None:
                 quantise_h(turn, whole)
+            for i in range(2):
+                nc.vector.tensor_tensor(staged[:, i, :], bank[:, i, :], wgo_t[:, CHUNK * c : CHUNK * (c + 1)], MULT)
             for i, (n, c) in enumerate(places):
                 nc.vector.tensor_copy(cache[n][:].indirect(list2(c, c + 1)), staged[:, i, :])
 

@@ -65,7 +65,10 @@ def tile_list_gene_regulation_derivatives_kernel(
         wr_q = [[held("wr_q%d%d" % (b, g), [P, PASS], U32) for g in both] for b in both]
         wr_s = [[held("wr_s%d%d" % (b, g), [P, PASS], U8) for g in both] for b in both]
         wd_raw = [[held("wd_raw%d%d" % (half, g), [P, PACK, HALF], F32) for g in both] for half in range(2)]
-        wd_bf = [held("wd_bf%d" % half, [P, PASSES, PACK * HALF], BF16) for half in range(2)]
+        third = PACK * HALF
+        wd_long = held("wd_long", [P, 3 * third], BF16)
+        wd_bf = [held("wd_bf0", [P, PASSES * third], BF16)[:], wd_long[:, : PASSES * third]]
+        rated_first = wd_long[:, third:].bitcast(F32).rearrange("p (t c) -> p t c", t=PACK)
         wd_q = [held("wd_q%d" % half, [P, PASSES, HALF], U32) for half in range(2)]
         wd_s = [held("wd_s%d" % half, [P, PASSES, HALF], U8) for half in range(2)]
         wt_w = held("wt_w", [P, PASSES, 2 * N], U8)
@@ -78,7 +81,7 @@ def tile_list_gene_regulation_derivatives_kernel(
         rated_late = held("rated_late", [P, 2 * PACK - GPSIMD_PLANES, CHUNK], F32)
         factors = [held("factor%d" % i, [P, PACK, CHUNK], F32) for i in range(FACTOR_SLOTS)]
         h_early = [held("h_early%d" % i, [P, PACK * CHUNK], BF16) for i in range(VECTOR_PRODUCT_PIECES)]
-        h_late = wd_bf[1][:, 0, :]
+        h_late = wd_long[:, :third]
         h_q = [[held("h_q%d%d" % (b, c), [P, CHUNK], U32) for c in range(CHUNKS)] for b in both]
         h_s = [[held("h_s%d%d" % (b, c), [P, CHUNK], U8) for c in range(CHUNKS)] for b in both]
         y_last = held("y_last", [P, ROW_TILES - 1, CHUNK], F32)
@@ -101,9 +104,8 @@ def tile_list_gene_regulation_derivatives_kernel(
         def load_wr(b, g):
             nc.sync.dma_start(out=wr_raw[b][g][:], in_=rows_of_pass(wr, g)[:, :, PASS * b : PASS * (b + 1)])
 
-        def load_wd(half):
-            for g in both:
-                nc.sync.dma_start(out=wd_raw[half][g][:], in_=rows_of_pass(wd, g)[:, :, HALF * half : HALF * (half + 1)])
+        def load_wd(half, g):
+            nc.sync.dma_start(out=wd_raw[half][g][:], in_=rows_of_pass(wd, g)[:, :, HALF * half : HALF * (half + 1)])
 
         def load_words(g):
             nc.sync.dma_start(out=tab_w[g][:], in_=tab_words[g].rearrange("p t i -> p (t i)").bitcast(I32))
@@ -118,16 +120,18 @@ def tile_list_gene_regulation_derivatives_kernel(
         for g in both:
             load_wr(1, g)
         nc.sync.dma_start(out=rate_t[:], in_=rate.rearrange("(b p t) -> p b t", b=PASSES, t=PACK))
-        load_wd(0)
+        for g in both:
+            load_wd(0, g)
         for q in range(4):
             nc.sync.dma_start(
                 out=wt_s[32 * q : 32 * q + 4, :, :].bitcast(I32),
                 in_=wt4_scales[:, 4 * q : 4 * q + 4, :].rearrange("g r n -> r g n").bitcast(I32),
             )
+        load_wd(1, 0)
         nc.sync.dma_start(out=wt_w[:].bitcast(I32), in_=wt4_words.rearrange("g p c -> p g c").bitcast(I32))
         nc.sync.dma_start(idx2[:], offs2)
         nc.sync.dma_start(out=wgo_t[:], in_=wgo)
-        load_wd(1)
+        load_wd(1, 1)
 
         def cast(engine, dst, src):
             if engine == "vector":
@@ -153,21 +157,23 @@ def tile_list_gene_regulation_derivatives_kernel(
 
         def cast_wd(half):
             for g in both:
-                dst = wd_bf[half][:, g, :].rearrange("p (c i j) -> p c j i", i=RUN, j=PACK)
+                dst = wd_bf[half][:, third * g : third * (g + 1)].rearrange("p (c i j) -> p c j i", i=RUN, j=PACK)
                 src = wd_raw[half][g][:].rearrange("p j (c i) -> p c j i", i=RUN)
-                cast("scalar" if (half, g) == (0, 1) else "vector", dst, src)
+                cast("scalar" if g != half else "vector", dst, src)
 
         def quantise_wd(half):
             if half == 0:
                 for g in (half, 1 - half):
                     nc.vector.quantize_mx(
-                        out=wd_q[half][:, g, :].bitcast(FP8X4), scales=wd_s[half][:, g, :], in_=wd_bf[half][:, g, :]
+                        out=wd_q[half][:, g, :].bitcast(FP8X4),
+                        scales=wd_s[half][:, g, :],
+                        in_=wd_bf[half][:, third * g : third * (g + 1)],
                     )
             else:
                 nc.vector.quantize_mx(
                     out=wd_q[half][:].rearrange("p g c -> p (g c)").bitcast(FP8X4),
                     scales=wd_s[half][:].rearrange("p g c -> p (g c)"),
-                    in_=wd_bf[half][:].rearrange("p g c -> p (g c)"),
+                    in_=wd_bf[half],
                 )
 
         def table_operand(g, cols):
@@ -183,7 +189,7 @@ def tile_list_gene_regulation_derivatives_kernel(
             b, c = PIECES[turn]
             square, factor = squares[turn % SQUARE_SLOTS], factors[turn % FACTOR_SLOTS]
             per_bank = BANK // CHUNK
-            for t0 in range(0, PACK, per_bank):
+            for t0 in range(0, PACK, per_bank) if turn != VECTOR_PRODUCT_PIECES else (per_bank, 0):
                 bank = banks[PIECE_BANKS[turn] + t0 // per_bank]
                 for g in both:
                     for t in range(t0, t0 + per_bank):
@@ -199,10 +205,18 @@ def tile_list_gene_regulation_derivatives_kernel(
                         )
                 nc.scalar.activation(out=square[:, t0 : t0 + per_bank, :], in_=bank[:], func=ACT.Square)
             vector_rates = c == 0
-            late = turn > VECTOR_PRODUCT_PIECES
             first = (PACK - GPSIMD_PLANES) * (turn % 2)
-            on_gpsimd = turn >= VECTOR_PRODUCT_PIECES
-            rated = square if vector_rates else rated_late[:, first : first + PACK, :] if on_gpsimd else rated_early
+            shared = [t for t in range(PACK) if PACK - GPSIMD_PLANES <= first + t < PACK]
+            if vector_rates:
+                rated = square
+            elif turn < VECTOR_PRODUCT_PIECES:
+                rated, shared = rated_early, []
+            elif turn == VECTOR_PRODUCT_PIECES:
+                rated, shared = rated_first, [0, 1]
+            else:
+                rated = rated_late[:, first : first + PACK, :]
+                if turn == VECTOR_PRODUCT_PIECES + 1:
+                    shared = []
 
             def inverse_root(planes):
                 nc.scalar.activation(
@@ -217,11 +231,12 @@ def tile_list_gene_regulation_derivatives_kernel(
                         plane = factor[:, t, cols]
                         nc.vector.scalar_tensor_tensor(plane, plane, rate_t[:, b, t : t + 1], plane, MULT, MULT)
                 return rated, factor
-            for t in range(PACK):
+            own = [t for t in range(PACK) if t not in shared]
+            for t in shared + own:
                 rate_col = rate_t[:, b, t : t + 1]
-                if t == per_bank:
+                if t == own[len(own) // 2]:
                     inverse_root(slice(0, PACK))
-                if late and PACK - GPSIMD_PLANES <= first + t < PACK:
+                if t in shared:
                     nc.gpsimd.tensor_scalar(rated[:, t, :], square[:, t, :], rate_col, 0.0, MULT, ADD)
                 else:
                     nc.scalar.activation(out=rated[:, t, :], in_=square[:, t, :], func=ACT.Copy, scale=rate_col)

@@ -113,7 +113,16 @@ def tile_list_gene_regulation_derivatives_kernel(
         nc.sync.dma_start(idx[:], offs)
         load_words(0)
         for q in range(4):
-            nc.sync.dma_start(out=tab_s[32 * q : 32 * q + 8, :], in_=tab_scales[:, 4 * q : 4 * q + 4, :].bitcast(I32))
+            if q < 2:
+                nc.sync.dma_start(
+                    out=tab_s[32 * q : 32 * q + 8, :], in_=tab_scales[:, 4 * q : 4 * q + 4, :].bitcast(I32)
+                )
+            else:
+                for g in both:
+                    nc.sync.dma_start(
+                        out=tab_s[32 * q + 4 * g : 32 * q + 4 * g + 4, :],
+                        in_=tab_scales[g, 4 * q : 4 * q + 4, :].bitcast(I32),
+                    )
         for g in both:
             load_wr(0, g)
         load_words(1)

@@ -56,15 +56,25 @@ def tile_list_gene_regulation_derivatives_kernel(
         idx2 = lists.tile([P, S // 16], U16, name="idx2")
         banks = [psum.tile([P, BANK // CHUNK, CHUNK], F32, name="bank%d" % i) for i in range(BANKS)]
 
-        tab_w = [held("tab_w%d" % g, [P, T], I32) for g in both]
+        tab_w = held("tab_w", [P, T], I32)
         tab_s = held("tab_s", [P, T // 4], I32)
         v_w = [held("v_w%d" % g, [P, S], U32) for g in both]
         v_s = held("v_s", [P, S], U8)
-        wr_raw = [[held("wr_raw%d%d" % (b, g), [P, PACK, PASS], F32) for g in both] for b in both]
-        wr_bf = [[held("wr_bf%d%d" % (b, g), [P, PACK * PASS], BF16) for g in both] for b in both]
+        block = PACK * PASS
+        stage = [held("stage%d" % g, [P, block], F32) for g in both]
+        wr_bf_first = held("wr_bf_first", [P, PASSES * block], BF16)
+        wr_flat = [[stage[0][:], stage[1][:]], [stage[0][:], wr_bf_first[:].bitcast(F32)]]
+        wr_raw = [[wr_flat[b][g].rearrange("p (j c) -> p j c", j=PACK) for g in both] for b in both]
+        wr_bf = [
+            [wr_bf_first[:, block * g : block * (g + 1)] for g in both],
+            [held("wr_bf1%d" % g, [P, block], BF16)[:] for g in both],
+        ]
         wr_q = [[held("wr_q%d%d" % (b, g), [P, PASS], U32) for g in both] for b in both]
         wr_s = [[held("wr_s%d%d" % (b, g), [P, PASS], U8) for g in both] for b in both]
-        wd_raw = [[held("wd_raw%d%d" % (half, g), [P, PACK, HALF], F32) for g in both] for half in range(2)]
+        wd_raw = [
+            [stage[0][:, PACK * HALF * g : PACK * HALF * (g + 1)].rearrange("p (j c) -> p j c", j=PACK) for g in both],
+            [held("wd_raw1%d" % g, [P, PACK, HALF], F32)[:] for g in both],
+        ]
         third = PACK * HALF
         wd_long = held("wd_long", [P, 3 * third], BF16)
         wd_bf = [held("wd_bf0", [P, PASSES * third], BF16)[:], wd_long[:, : PASSES * third]]
@@ -102,13 +112,13 @@ def tile_list_gene_regulation_derivatives_kernel(
             return weight[PASS * g : PASS * (g + 1), :].rearrange("(p j) c -> p j c", j=PACK)
 
         def load_wr(b, g):
-            nc.sync.dma_start(out=wr_raw[b][g][:], in_=rows_of_pass(wr, g)[:, :, PASS * b : PASS * (b + 1)])
+            nc.sync.dma_start(out=wr_raw[b][g], in_=rows_of_pass(wr, g)[:, :, PASS * b : PASS * (b + 1)])
 
         def load_wd(half, g):
-            nc.sync.dma_start(out=wd_raw[half][g][:], in_=rows_of_pass(wd, g)[:, :, HALF * half : HALF * (half + 1)])
+            nc.sync.dma_start(out=wd_raw[half][g], in_=rows_of_pass(wd, g)[:, :, HALF * half : HALF * (half + 1)])
 
         def load_words(g):
-            nc.sync.dma_start(out=tab_w[g][:], in_=tab_words[g].rearrange("p t i -> p (t i)").bitcast(I32))
+            nc.sync.dma_start(out=tab_w[:], in_=tab_words[g].rearrange("p t i -> p (t i)").bitcast(I32))
 
         nc.sync.dma_start(idx[:], offs)
         load_words(0)
@@ -125,22 +135,6 @@ def tile_list_gene_regulation_derivatives_kernel(
                     )
         for g in both:
             load_wr(0, g)
-        load_words(1)
-        for g in both:
-            load_wr(1, g)
-        nc.sync.dma_start(out=rate_t[:], in_=rate.rearrange("(b p t) -> p b t", b=PASSES, t=PACK))
-        for g in both:
-            load_wd(0, g)
-        for q in range(4):
-            nc.sync.dma_start(
-                out=wt_s[32 * q : 32 * q + 4, :, :].bitcast(I32),
-                in_=wt4_scales[:, 4 * q : 4 * q + 4, :].rearrange("g r n -> r g n").bitcast(I32),
-            )
-        load_wd(1, 0)
-        nc.sync.dma_start(out=wt_w[:].bitcast(I32), in_=wt4_words.rearrange("g p c -> p g c").bitcast(I32))
-        nc.sync.dma_start(idx2[:], offs2)
-        nc.sync.dma_start(out=wgo_t[:], in_=wgo)
-        load_wd(1, 1)
 
         def cast(engine, dst, src):
             if engine == "vector":
@@ -149,8 +143,8 @@ def tile_list_gene_regulation_derivatives_kernel(
                 nc.scalar.copy(out=dst, in_=src)
 
         def cast_wr(b, g, engines):
-            dst = wr_bf[b][g][:].rearrange("p (t m j) -> p m j t", t=PACK, j=PACK)
-            src = wr_raw[b][g][:].rearrange("p j (m t) -> p m j t", t=PACK)
+            dst = wr_bf[b][g].rearrange("p (t m j) -> p m j t", t=PACK, j=PACK)
+            src = wr_raw[b][g].rearrange("p j (m t) -> p m j t", t=PACK)
             for pair, engine in enumerate(engines):
                 planes = slice(2 * pair, 2 * pair + 2)
                 cast(engine, dst[:, :, :, planes], src[:, :, :, planes])
@@ -167,7 +161,7 @@ def tile_list_gene_regulation_derivatives_kernel(
         def cast_wd(half):
             for g in both:
                 dst = wd_bf[half][:, third * g : third * (g + 1)].rearrange("p (c i j) -> p c j i", i=RUN, j=PACK)
-                src = wd_raw[half][g][:].rearrange("p j (c i) -> p c j i", i=RUN)
+                src = wd_raw[half][g].rearrange("p j (c i) -> p c j i", i=RUN)
                 cast("scalar" if g != half else "vector", dst, src)
 
         def quantise_wd(half):
@@ -310,17 +304,34 @@ def tile_list_gene_regulation_derivatives_kernel(
         def fused_scatter(n, c0, c1, y_sb):
             nc.vector.tensor_tensor(cache[n][:].indirect(list2(c0, c1)), y_sb, wgo_t[:, CHUNK * c0 : CHUNK * c1], MULT)
 
-        nc.vector.tensor_copy(v_w[0][:], tab_w[0][:].bitcast(U32).indirect(idx[:]))
+        nc.vector.tensor_copy(v_w[0][:], tab_w[:].bitcast(U32).indirect(idx[:]))
+        load_words(1)
         nc.vector.tensor_copy(v_s[:], tab_s[:].bitcast(U8).indirect(idx[:]))
         cast_wr(0, 0, ["scalar", "scalar"])
+        load_wr(1, 0)
         cast_wr(0, 1, ["vector", "scalar"])
         for g in both:
             quantise_wr(0, g)
+        load_wr(1, 1)
+        nc.sync.dma_start(out=rate_t[:], in_=rate.rearrange("(b p t) -> p b t", b=PASSES, t=PACK))
         for j0, j1 in ((0, CHUNK), (CHUNK, S)):
-            nc.vector.tensor_copy(v_w[1][:, j0:j1], tab_w[1][:].bitcast(U32).indirect(idx[:, j0 // 16 : j1 // 16]))
+            nc.vector.tensor_copy(v_w[1][:, j0:j1], tab_w[:].bitcast(U32).indirect(idx[:, j0 // 16 : j1 // 16]))
+        cast_wr(1, 0, ["vector", "vector"])
         for g in both:
-            cast_wr(1, g, ["vector", "vector"])
-            quantise_wr(1, g)
+            load_wd(0, g)
+        for q in range(4):
+            nc.sync.dma_start(
+                out=wt_s[32 * q : 32 * q + 4, :, :].bitcast(I32),
+                in_=wt4_scales[:, 4 * q : 4 * q + 4, :].rearrange("g r n -> r g n").bitcast(I32),
+            )
+        load_wd(1, 0)
+        nc.sync.dma_start(out=wt_w[:].bitcast(I32), in_=wt4_words.rearrange("g p c -> p g c").bitcast(I32))
+        nc.sync.dma_start(idx2[:], offs2)
+        nc.sync.dma_start(out=wgo_t[:], in_=wgo)
+        load_wd(1, 1)
+        quantise_wr(1, 0)
+        cast_wr(1, 1, ["vector", "vector"])
+        quantise_wr(1, 1)
 
         def step(pair_number, staged, turn):
             c, pair = divmod(pair_number, 2)

from contextlib import ExitStack

import concourse.mybir as mybir

F32 = mybir.dt.float32
BF16 = mybir.dt.bfloat16
I32 = mybir.dt.int32
U32 = mybir.dt.uint32
U16 = mybir.dt.uint16
U8 = mybir.dt.uint8
FP8X4 = mybir.dt.float8_e4m3fn_x4
FP4X4 = mybir.dt.float4_e2m1fn_x4
MULT = mybir.AluOpType.mult
ADD = mybir.AluOpType.add
ACT = mybir.ActivationFunctionType

K, H, N, T, S, T2 = 1024, 1024, 512, 2048, 1024, 2048
FLOPS = 2 * K * H * S + 2 * H * N * S + 2 * K * N * S

P = 128
PACK = 4
PASS = P * PACK
PASSES = K // PASS
ROW_TILES = N // P
CHUNK = 256
CHUNKS = S // CHUNK
LIST_COLS = CHUNK // 16
BANK = 512
HALF = N // 2
RUN = 4
BANKS = 8
SQUARE_SLOTS = 3
FACTOR_SLOTS = 4
PIECES = [(0, 0), (0, 1), (1, 0), (1, 1)] + [(b, c) for c in range(2, CHUNKS) for b in range(PASSES)]
PIECE_BANKS = [0, 2, 4, 0, 2, 4, 6, 2]
GROUP_BANKS = [6, 6, 0, 1, 4, 5, 6, 7, 0, 1]
GPSIMD_PLANES = 1
VECTOR_PRODUCT_PIECES = 3


def tile_list_gene_regulation_derivatives_kernel(
    tc, tab_words, tab_scales, offs, wr, rate, wt4_words, wt4_scales, wd, wgo, offs2, out
):
    nc = tc.nc
    both = range(PASSES)

    with ExitStack() as ctx:
        lists = ctx.enter_context(tc.tile_pool(name="lists", bufs=1))
        keep = ctx.enter_context(tc.tile_pool(name="keep", bufs=1))
        psum = ctx.enter_context(tc.psum_pool(name="psum", bufs=1))

        def held(name, shape, dtype):
            return keep.tile(shape, dtype, name=name, align_bytes=64)

        idx = lists.tile([P, S // 16], U16, name="idx")
        idx2 = lists.tile([P, S // 16], U16, name="idx2")
        banks = [psum.tile([P, BANK // CHUNK, CHUNK], F32, name="bank%d" % i) for i in range(BANKS)]

        tab_w = held("tab_w", [P, T], I32)
        tab_s = held("tab_s", [P, T // 4], I32)
        v_w = [held("v_w%d" % g, [P, S], U32) for g in both]
        v_s = held("v_s", [P, S], U8)
        block = PACK * PASS
        stage = [held("stage%d" % g, [P, block], F32) for g in both]
        wr_bf_first = held("wr_bf_first", [P, PASSES * block], BF16)
        wr_flat = [[stage[0][:], stage[1][:]], [stage[0][:], wr_bf_first[:].bitcast(F32)]]
        wr_raw = [[wr_flat[b][g].rearrange("p (j c) -> p j c", j=PACK) for g in both] for b in both]
        wr_bf = [
            [wr_bf_first[:, block * g : block * (g + 1)] for g in both],
            [held("wr_bf1%d" % g, [P, block], BF16)[:] for g in both],
        ]
        wr_q = [[held("wr_q%d%d" % (b, g), [P, PASS], U32) for g in both] for b in both]
        wr_s = [[held("wr_s%d%d" % (b, g), [P, PASS], U8) for g in both] for b in both]
        wd_raw = [
            [stage[0][:, PACK * HALF * g : PACK * HALF * (g + 1)].rearrange("p (j c) -> p j c", j=PACK) for g in both],
            [held("wd_raw1%d" % g, [P, PACK, HALF], F32)[:] for g in both],
        ]
        third = PACK * HALF
        wd_long = held("wd_long", [P, 3 * third], BF16)
        wd_bf = [held("wd_bf0", [P, PASSES * third], BF16)[:], wd_long[:, : PASSES * third]]
        rated_first = wd_long[:, third:].bitcast(F32).rearrange("p (t c) -> p t c", t=PACK)
        wd_q = [held("wd_q%d" % half, [P, PASSES, HALF], U32) for half in range(2)]
        wd_s = [held("wd_s%d" % half, [P, PASSES, HALF], U8) for half in range(2)]
        wt_w = held("wt_w", [P, PASSES, 2 * N], U8)
        wt_s = held("wt_s", [P, PASSES, N], U8)
        rate_t = held("rate_t", [P, PASSES, PACK], F32)
        wgo_t = held("wgo_t", [P, S], F32)
        one = held("one", [P, 1], F32)
        squares = [held("square%d" % i, [P, PACK, CHUNK], F32) for i in range(SQUARE_SLOTS)]
        rated_early = held("rated_early", [P, PACK, CHUNK], F32)
        rated_late = held("rated_late", [P, 2 * PACK - GPSIMD_PLANES, CHUNK], F32)
        factors = [held("factor%d" % i, [P, PACK, CHUNK], F32) for i in range(FACTOR_SLOTS)]
        h_early = [held("h_early%d" % i, [P, PACK * CHUNK], BF16) for i in range(VECTOR_PRODUCT_PIECES)]
        h_late = wd_long[:, :third]
        h_q = [[held("h_q%d%d" % (b, c), [P, CHUNK], U32) for c in range(CHUNKS)] for b in both]
        h_s = [[held("h_s%d%d" % (b, c), [P, CHUNK], U8) for c in range(CHUNKS)] for b in both]
        y_last = held("y_last", [P, ROW_TILES - 1, CHUNK], F32)
        y_pair = held("y_pair", [P, 2 * CHUNK], F32)
        cache = [held("cache%d" % n, [P, T2], F32) for n in range(ROW_TILES)]

        nc.vector.memset(one[:], 1.0)
        nc.scalar.activation(out=one[:], in_=one[:], func=ACT.Abs_reciprocal_sqrt)
        nc.scalar.activation(out=one[:], in_=one[:], func=ACT.Sign)
        nc.gpsimd.memset(tab_s[:], 0)
        nc.vector.memset(cache[0][:, : T2 // 2 + 1], 0.0)
        nc.vector.memset(cache[0][:, T2 // 2 + 1 :], 0.0)
        for n in range(1, ROW_TILES):
            nc.gpsimd.memset(cache[n][:], 0.0)
        nc.gpsimd.memset(wt_s[:].rearrange("p g n -> p (g n)").bitcast(I32), 0)

        def rows_of_pass(weight, g):
            return weight[PASS * g : PASS * (g + 1), :].rearrange("(p j) c -> p j c", j=PACK)

        def load_wr(b, g):
            nc.sync.dma_start(out=wr_raw[b][g], in_=rows_of_pass(wr, g)[:, :, PASS * b : PASS * (b + 1)])

        def load_wd(half, g):
            nc.sync.dma_start(out=wd_raw[half][g], in_=rows_of_pass(wd, g)[:, :, HALF * half : HALF * (half + 1)])

        def load_words(g):
            nc.sync.dma_start(out=tab_w[:], in_=tab_words[g].rearrange("p t i -> p (t i)").bitcast(I32))

        nc.sync.dma_start(idx[:], offs)
        load_words(0)
        for q in range(4):
            if q < 2:
                nc.sync.dma_start(
                    out=tab_s[32 * q : 32 * q + 8, :], in_=tab_scales[:, 4 * q : 4 * q + 4, :].bitcast(I32)
                )
            else:
                for g in both:
                    nc.sync.dma_start(
                        out=tab_s[32 * q + 4 * g : 32 * q + 4 * g + 4, :],
                        in_=tab_scales[g, 4 * q : 4 * q + 4, :].bitcast(I32),
                    )
        for g in both:
            load_wr(0, g)

        def cast(engine, dst, src):
            if engine == "vector":
                nc.vector.tensor_copy(out=dst, in_=src)
            else:
                nc.scalar.copy(out=dst, in_=src)

        def cast_wr(b, g, engines):
            dst = wr_bf[b][g].rearrange("p (t m j) -> p m j t", t=PACK, j=PACK)
            src = wr_raw[b][g].rearrange("p j (m t) -> p m j t", t=PACK)
            for pair, engine in enumerate(engines):
                planes = slice(2 * pair, 2 * pair + 2)
                cast(engine, dst[:, :, :, planes], src[:, :, :, planes])

        def quantise_wr(b, g):
            width = PASS // 2
            for c0 in range(0, PASS, width):
                nc.vector.quantize_mx(
                    out=wr_q[b][g][:, c0 : c0 + width].bitcast(FP8X4),
                    scales=wr_s[b][g][:, c0 : c0 + width],
                    in_=wr_bf[b][g][:, PACK * c0 : PACK * (c0 + width)],
                )

        def cast_wd(half):
            for g in both:
                dst = wd_bf[half][:, third * g : third * (g + 1)].rearrange("p (c i j) -> p c j i", i=RUN, j=PACK)
                src = wd_raw[half][g].rearrange("p j (c i) -> p c j i", i=RUN)
                cast("scalar" if g != half else "vector", dst, src)

        def quantise_wd(half):
            if half == 0:
                for g in (half, 1 - half):
                    nc.vector.quantize_mx(
                        out=wd_q[half][:, g, :].bitcast(FP8X4),
                        scales=wd_s[half][:, g, :],
                        in_=wd_bf[half][:, third * g : third * (g + 1)],
                    )
            else:
                nc.vector.quantize_mx(
                    out=wd_q[half][:].rearrange("p g c -> p (g c)").bitcast(FP8X4),
                    scales=wd_s[half][:].rearrange("p g c -> p (g c)"),
                    in_=wd_bf[half],
                )

        def table_operand(g, cols):
            return v_w[g][:, cols].bitcast(FP8X4), v_s[4 * g : P, cols]

        halves = [slice(j0, j0 + CHUNK // 2) for j0 in (0, CHUNK // 2)]
        whole = [slice(0, CHUNK)]

        def h_buffer(turn):
            return h_early[turn][:] if turn < len(h_early) else h_late

        def two_factors(turn):
            b, c = PIECES[turn]
            square, factor = squares[turn % SQUARE_SLOTS], factors[turn % FACTOR_SLOTS]
            per_bank = BANK // CHUNK
            for t0 in range(0, PACK, per_bank) if turn != VECTOR_PRODUCT_PIECES else (per_bank, 0):
                bank = banks[PIECE_BANKS[turn] + t0 // per_bank]
                for g in both:
                    for t in range(t0, t0 + per_bank):
                        words, scales = table_operand(g, slice(CHUNK * c, CHUNK * (c + 1)))
                        nc.tensor.matmul_mx(
                            out=bank[:, t - t0, :],
                            lhsT=wr_q[b][g][:, P * t : P * (t + 1)].bitcast(FP8X4),
                            lhsT_scale=wr_s[b][g][:, P * t : P * (t + 1)],
                            rhs=words,
                            rhs_scale=scales,
                            start=(g == 0 and t == t0),
                            stop=(g == PASSES - 1 and t == t0 + per_bank - 1),
                        )
                nc.scalar.activation(out=square[:, t0 : t0 + per_bank, :], in_=bank[:], func=ACT.Square)
            vector_rates = c == 0
            first = (PACK - GPSIMD_PLANES) * (turn % 2)
            shared = [t for t in range(PACK) if PACK - GPSIMD_PLANES <= first + t < PACK]
            if vector_rates:
                rated = square
            elif turn < VECTOR_PRODUCT_PIECES:
                rated, shared = rated_early, []
            elif turn == VECTOR_PRODUCT_PIECES:
                rated, shared = rated_first, [0, 1]
            else:
                rated = rated_late[:, first : first + PACK, :]
                if turn == VECTOR_PRODUCT_PIECES + 1:
                    shared = []

            def inverse_root(planes):
                nc.scalar.activation(
                    out=factor[:, planes, :], in_=square[:, planes, :], func=ACT.Abs_reciprocal_sqrt, bias=one[:]
                )

            if vector_rates:
                for t0 in range(0, PACK, per_bank):
                    inverse_root(slice(t0, t0 + per_bank))
                for t in range(PACK):
                    for cols in halves if t == PACK - 1 else whole:
                        plane = factor[:, t, cols]
                        nc.vector.scalar_tensor_tensor(plane, plane, rate_t[:, b, t : t + 1], plane, MULT, MULT)
                return rated, factor
            own = [t for t in range(PACK) if t not in shared]
            for t in shared + own:
                rate_col = rate_t[:, b, t : t + 1]
                if t == own[len(own) // 2]:
                    inverse_root(slice(0, PACK))
                if t in shared:
                    nc.gpsimd.tensor_scalar(rated[:, t, :], square[:, t, :], rate_col, 0.0, MULT, ADD)
                else:
                    nc.scalar.activation(out=rated[:, t, :], in_=square[:, t, :], func=ACT.Copy, scale=rate_col)
            for cols in halves if turn == len(PIECES) - 1 else whole:
                nc.scalar.activation(out=factor[:, :, cols], in_=factor[:, :, cols], func=ACT.Square)
            return rated, factor

        def multiply_out(turn, rated, factor, engine, parts):
            h_bf = h_buffer(turn)
            for cols in parts:
                engine.tensor_tensor(
                    h_bf[:, PACK * cols.start : PACK * cols.stop].rearrange("p (c i t) -> p c t i", i=RUN, t=PACK),
                    rated[:, :, cols].rearrange("p t (c i) -> p c t i", i=RUN),
                    factor[:, :, cols].rearrange("p t (c i) -> p c t i", i=RUN),
                    MULT,
                )

        def quantise_h(turn, parts):
            b, c = PIECES[turn]
            h_bf = h_buffer(turn)
            for cols in parts:
                nc.vector.quantize_mx(
                    out=h_q[b][c][:, cols].bitcast(FP8X4),
                    scales=h_s[b][c][:, cols],
                    in_=h_bf[:, PACK * cols.start : PACK * cols.stop],
                )

        groups_done = []

        def products(places):
            bank = banks[GROUP_BANKS[len(groups_done)]]
            groups_done.append(places)
            for i, (n, c) in enumerate(places):
                half, n0 = divmod(P * n, HALF)
                for g in both:
                    words, scales = table_operand(g, slice(CHUNK * c, CHUNK * (c + 1)))
                    nc.tensor.matmul_mx(
                        out=bank[:, i, :],
                        lhsT=wd_q[half][:, g, n0 : n0 + P].bitcast(FP8X4),
                        lhsT_scale=wd_s[half][:, g, n0 : n0 + P],
                        rhs=words,
                        rhs_scale=scales,
                        start=(i == 0 and g == 0),
                        stop=False,
                    )
            for b in both:
                for i, (n, c) in enumerate(places):
                    nc.tensor.matmul_mx(
                        out=bank[:, i, :],
                        lhsT=wt_w[:, b, 2 * P * n : 2 * P * (n + 1)].bitcast(FP4X4),
                        lhsT_scale=wt_s[:, b, P * n : P * (n + 1)],
                        rhs=h_q[b][c][:].bitcast(FP8X4),
                        rhs_scale=h_s[b][c][:],
                        start=False,
                        stop=(b == PASSES - 1 and i == len(places) - 1),
                    )
            return bank

        def list2(c0, c1):
            return idx2[:, LIST_COLS * c0 : LIST_COLS * c1]

        def fused_scatter(n, c0, c1, y_sb):
            nc.vector.tensor_tensor(cache[n][:].indirect(list2(c0, c1)), y_sb, wgo_t[:, CHUNK * c0 : CHUNK * c1], MULT)

        nc.vector.tensor_copy(v_w[0][:], tab_w[:].bitcast(U32).indirect(idx[:]))
        load_words(1)
        nc.vector.tensor_copy(v_s[:], tab_s[:].bitcast(U8).indirect(idx[:]))
        cast_wr(0, 0, ["scalar", "scalar"])
        load_wr(1, 0)
        cast_wr(0, 1, ["vector", "scalar"])
        for g in both:
            quantise_wr(0, g)
        load_wr(1, 1)
        nc.sync.dma_start(out=rate_t[:], in_=rate.rearrange("(b p t) -> p b t", b=PASSES, t=PACK))
        for j0, j1 in ((0, CHUNK), (CHUNK, S)):
            nc.vector.tensor_copy(v_w[1][:, j0:j1], tab_w[:].bitcast(U32).indirect(idx[:, j0 // 16 : j1 // 16]))
        cast_wr(1, 0, ["vector", "vector"])
        for g in both:
            load_wd(0, g)
        for q in range(4):
            nc.sync.dma_start(
                out=wt_s[32 * q : 32 * q + 4, :, :].bitcast(I32),
                in_=wt4_scales[:, 4 * q : 4 * q + 4, :].rearrange("g r n -> r g n").bitcast(I32),
            )
        load_wd(1, 0)
        nc.sync.dma_start(out=wt_w[:].bitcast(I32), in_=wt4_words.rearrange("g p c -> p g c").bitcast(I32))
        nc.sync.dma_start(idx2[:], offs2)
        nc.sync.dma_start(out=wgo_t[:], in_=wgo)
        load_wd(1, 1)
        quantise_wr(1, 0)
        cast_wr(1, 1, ["vector", "vector"])
        quantise_wr(1, 1)

        def step(pair_number, staged, turn):
            c, pair = divmod(pair_number, 2)
            places = [(2 * pair, c), (2 * pair + 1, c)]
            bank = products(places)
            if turn is not None:
                quantise_h(turn, whole)
            for i in range(2):
                nc.vector.tensor_tensor(staged[:, i, :], bank[:, i, :], wgo_t[:, CHUNK * c : CHUNK * (c + 1)], MULT)
            for i, (n, c) in enumerate(places):
                nc.vector.tensor_copy(cache[n][:].indirect(list2(c, c + 1)), staged[:, i, :])

        for turn in range(VECTOR_PRODUCT_PIECES):
            rated, factor = two_factors(turn)
            multiply_out(turn, rated, factor, nc.vector, halves)
            quantise_h(turn, halves)
            if turn == 0:
                cast_wd(0)
            if turn == 1:
                quantise_wd(0)
        cast_wd(1)
        quantise_wd(1)
        step(0, wd_raw[1][1], None)
        last_turn = len(PIECES) - 1
        for turn in range(VECTOR_PRODUCT_PIECES, last_turn):
            rated, factor = two_factors(turn)
            multiply_out(turn, rated, factor, nc.gpsimd, whole)
            step(turn - VECTOR_PRODUCT_PIECES + 1, factor, turn)
        rated, factor = two_factors(last_turn)
        multiply_out(last_turn, rated, factor, nc.gpsimd, halves)
        last_tile, last_chunk = ROW_TILES - 1, CHUNKS - 1
        bank = products([(last_tile - 1, last_chunk - 1), (last_tile, last_chunk - 1)])
        nc.scalar.copy(out=factor[:, 0, :], in_=bank[:, 0, :])
        nc.scalar.copy(out=y_pair[:, :CHUNK], in_=bank[:, 1, :])
        quantise_h(last_turn, whole)
        fused_scatter(last_tile - 1, last_chunk - 1, last_chunk, factor[:, 0, :])
        for n in range(ROW_TILES):
            bank = products([(n, last_chunk)])
            if n < last_tile:
                nc.scalar.copy(out=y_last[:, n, :], in_=bank[:, 0, :])
                fused_scatter(n, last_chunk, last_chunk + 1, y_last[:, n, :])
                nc.sync.dma_start(out=out[P * n : P * (n + 1), :], in_=cache[n][:])
            else:
                nc.scalar.copy(out=y_pair[:, CHUNK:], in_=bank[:, 0, :])
                fused_scatter(n, last_chunk - 1, last_chunk + 1, y_pair[:])
                for queue, cols in ((nc.sync, slice(0, T2 // 2)), (nc.scalar, slice(T2 // 2, T2))):
                    queue.dma_start(out=out[P * n : P * (n + 1), cols], in_=cache[n][:, cols])
